import numpy as np, ml_dtypes
CORES = [48,51,52,55]
N = 4
BF = ml_dtypes.bfloat16
def gentries(a):
    return np.ascontiguousarray(a.reshape(8, 16, -1).transpose(0, 2, 1)).reshape(8, -1)
def gtable(e):
    e = np.asarray(e); return np.ascontiguousarray(e.reshape(8, -1, 16).transpose(0, 2, 1)).reshape(128, -1).astype(np.int32)
F, STEP, CAPP, V, R, D = 4096, 256, 160, 8192, 3, 3
def aim(rng, s):
    p = rng.integers(1, 64, F); o = rng.permutation(F); k = s - int(np.sum(p)); room = (63 - p if k > 0 else p - 1)[o]
    p[o] += np.sign(k) * np.clip(abs(k) - (np.add.accumulate(room) - room), 0, room)
    return p
def rise(rng):
    top = N * CAPP * STEP + int(rng.integers(62, STEP + 1)); lo, hi, best = F, N * CAPP * STEP, -1
    for k in range(20):
        s = (lo + hi) // 2 if k else F; v = aim(rng, s); z = v.copy()
        for a in range(R - 1):
            z[np.flatnonzero(np.diff(np.add.accumulate(z) // STEP, prepend=0))] = 63
        u = int(np.sum(z))
        if u >= top: hi = s
        else:
            lo = s
            if u > best: best, p, last = u, v, z
    total = np.concatenate([np.zeros(1, np.int64), np.add.accumulate(last)]) + 63 * (F - np.arange(F + 1))
    p[np.flatnonzero(total < top)[0]:] = 63
    return p
def links(rng):
    lab = rng.integers(0, rng.integers(8, 257), F); o = np.argsort(lab, kind="stable"); b, c = o[:-1], o[1:]
    on = (lab[b] == lab[c]) & (rng.random(F - 1) > 0.05); v = np.stack([np.arange(F), np.arange(F)])
    v[0, c[on]] = b[on]; v[1, b[on]] = c[on]
    return v
def whole(rng, m, *shape):
    return rng.integers(-m, m + 1, shape).astype(np.float32).astype(BF)
def draw(rng, lo, hi):
    v = np.stack([np.stack([links(rng) for g in range(8)]) for r in range(N)]).astype(np.int32)
    return {"x": whole(rng, 8, N, 128, F), "prv": np.ascontiguousarray(v[:, :, 0]), "nxt": np.ascontiguousarray(v[:, :, 1]), "key": rng.integers(0, V, (N, 8, F)).astype(np.int32), "rw": rng.integers(-255, 256, (N, 8, F)).astype(np.int32),
            "pri": np.stack([gtable(np.stack([aim(rng, int(rng.integers(lo * F, hi * F))) for g in range(8)])) for r in range(N)]), "w": whole(rng, 4, N, 128, 2 * D + 1), "val": whole(rng, 8, N, 128, V)}
def put(d, r, g, p):
    e = gentries(d["pri"][r]); e[g] = p; d["pri"][r] = gtable(e)
def setup_inputs(rng):
    return draw(rng, 24, 34)
def setup_inputs_full(rng):
    d = draw(rng, 24, 34); o = rng.permutation(N); late = rng.random((N, 8)) < 0.2; late[o[1], rng.permutation(8)[:4]] = True; late[o[0]] = False
    m = rng.random((N, 8)) < 0.3; m[o[0]] = True; m = m & ~late
    for r, g in np.argwhere(m):
        put(d, r, g, aim(rng, N * CAPP * STEP + int(rng.integers(0, STEP))))
        d["x"][r, 16 * g:16 * g + 16] = whole(rng, 1, 16, F); d["rw"][r, g] = rng.integers(-60, 61, F)
    for r, g in np.argwhere(late):
        put(d, r, g, rise(rng))
        d["x"][r, 16 * g:16 * g + 16] = 0; d["rw"][r, g] = 340; d["rw"][r, g, 0] = 0
    return d
def setup_inputs_even(rng):
    d = draw(rng, 24, 34)
    for r in range(N):
        d["pri"][r] = gtable(np.repeat(rng.permutation(np.array([16, 16, 16, 32, 32, 32, 32, 32]))[:, None], F, 1))
    return d
def setup_inputs_few(rng):
    d = draw(rng, 24, 34)
    for r in range(N):
        o = rng.permutation(8)[:4]
        for g in o[1:]: d["x"][r, 16 * g:16 * g + 16] = 0
        for g in o[:2]: put(d, r, g, np.ones(F, np.int64))
        for g in o[2:]: put(d, r, g, aim(rng, int(rng.integers(12 * F, 17 * F))))
        d["rw"][r, o[1]] = 0; d["rw"][r, o[2]] = rng.choice(np.array([0, 8, -8, 16, -16, 5, -5]), F); d["rw"][r, o[3]] = rng.choice(np.array([-336, -342, 336, 341, 335, 330]), F)
    return d
def setup_inputs_loose(rng):
    d = draw(rng, 8, 17); d["prv"] = rng.integers(0, F, (N, 8, F)).astype(np.int32); d["nxt"] = rng.integers(0, F, (N, 8, F)).astype(np.int32)
    for n, m in (("x", 8), ("w", 4), ("val", 8)):
        d[n] = (m * (2 * rng.integers(0, 2, d[n].shape) - 1)).astype(np.float32).astype(BF)
    d["rw"] = (1023 * rng.integers(-1, 2, (N, 8, F))).astype(np.int32)
    for r in range(N):
        o = rng.permutation(8)
        d["prv"][r, o[0]] = 0; d["nxt"][r, o[0]] = F - 1; d["prv"][r, o[1]] = np.arange(F); d["nxt"][r, o[1]] = np.arange(F)
        d["prv"][r, o[2]] = (np.arange(F) - 1) % F; d["nxt"][r, o[2]] = (np.arange(F) + 1) % F
        d["key"][r, o[3]] = V - 1; d["key"][r, o[4]] = rng.choice(np.array([0, V - 1]), F)
        d["x"][r, 16 * o[5]:16 * o[5] + 16] = 8
    q = rng.integers(0, N); d["w"][q] = 4; d["val"][q] = 8
    return d
def setup_inputs_spread(rng):
    d = draw(rng, 8, 17)
    for n, m in (("x", F), ("val", V)):
        s = np.left_shift(1, rng.integers(0, 4, (N, 1, m))) * (rng.random((N, 1, m)) > 0.0625)
        d[n] = (rng.integers(-1, 2, (N, 128, m)) * s).astype(np.float32).astype(BF)
    d["w"] = (rng.integers(-4, 5, (N, 128, 2 * D + 1)) * (rng.random((N, 128, 1)) > 0.4)).astype(np.float32).astype(BF)
    d["key"] = np.minimum(rng.random((N, 8, F)) ** 3 * V, V - 1).astype(np.int32)
    d["rw"] = np.right_shift(rng.integers(-1023, 1024, (N, 8, F)), rng.integers(0, 11, (N, 8, F))).astype(np.int32)
    return d
def play(x, prv, nxt, key, rw, pri, w, val):
    X = x.astype(np.float32).reshape(N, 8, 16, F); W = w.astype(np.float32).reshape(N, 8, 16, 2 * D + 1); A = val.astype(np.float32).reshape(N, 8, 16, V)
    P = np.stack([gentries(pri[r]) for r in range(N)]).astype(np.int64); most = 0
    for a in range(R):
        for r in range(N):
            for g in range(8):
                t = np.flatnonzero(np.diff(np.add.accumulate(P[r, g]) // STEP, prepend=0)); most = max(most, len(t))
                q = np.arange(len(t)) % N
                pt = {0: t}
                for k in range(1, D + 1):
                    pt[k] = nxt[r, g][pt[k - 1]]; pt[-k] = prv[r, g][pt[1 - k]]
                h = np.zeros((len(t), 16), np.float32)
                for k in range(-D, D + 1):
                    h += W[q, g, :, D + k] * X[r, g][:, pt[k]].T
                e = np.sum(A[q, g, :, key[r, g][t]] * h, axis=1) + (rw[r, g][pt[0]] + rw[r, g][pt[1]] + rw[r, g][pt[2]])
                P[r, g, t] = np.minimum(np.maximum(np.abs(e).astype(np.int64) >> 4, 1), 63)
    return P, most
def check_inputs(d):
    bad = []
    for n, lo, hi in (("x", -8, 8), ("prv", 0, F - 1), ("nxt", 0, F - 1), ("key", 0, V - 1), ("rw", -1023, 1023), ("pri", 1, 63), ("w", -4, 4), ("val", -8, 8)):
        v = np.asarray(d[n]).astype(np.float32)
        if not (np.isfinite(v).all() and (v == np.floor(v)).all() and v.min() >= lo and v.max() <= hi): bad.append(n)
    if not bad and play(**d)[1] > N * CAPP: bad.append("CAPP")
    return bad
def reference(x, prv, nxt, key, rw, pri, w, val):
    P, most = play(x, prv, nxt, key, rw, pri, w, val)
    y = np.stack([gtable(P[r]) for r in range(N)])
    return {"y": y.astype(np.float32)}

@@ -1,0 +1,461 @@
+from concourse.bass import DstId, RemoteDMATransfer
+from concourse.mybir import AluOpType as A, ActivationFunctionType as AF
+
+F, V, R, N = 4096, 8192, 3, 4
+BIG = 65536.0
+LW = 9 * 128
+H = 2
+C = 256 // H
+S = N * C
+J = S // 16
+
+
+def _sb(cols, dtype):
+    return ("sbuf", [128] + (cols if isinstance(cols, list) else [cols]), dtype)
+
+
+SCRATCH = {"PS": ("psum", [128, 4096], "float32"), "VAL": _sb(V, "bfloat16"), "LALL": _sb(N * LW, "bfloat16")}
+SCRATCH.update({n: _sb(F, "bfloat16") for n in ("X", "BASE", "CT", "TB", "TA", "ADD", "PT")})
+SCRATCH.update({n: _sb(1024, "bfloat16") for n in ("HI", "LO", "O", "GC", "GB", "GA", "GP", "GR", "RC", "RB", "RA", "RP")})
+SCRATCH.update({n: _sb(128, "bfloat16") for n in ("TMP", "TMR", "SAME", "S256", "ID", "MA", "PK", "SEL", "RWS", "EQ", "LBX")})
+SCRATCH.update({
+    "NAT": _sb(1024, "int32"), "RY": _sb(256, "bfloat16"), "LTI": _sb([4, 8, 16], "int32"), "LTF": _sb([4, 8, 16], "float32"),
+    "WF": _sb(512, "float32"), "WL": _sb(512, "uint16"), "PRI": _sb(256, "int32"), "PB": _sb(272, "bfloat16"),
+    "Y": _sb(256, "float32"), "WR": _sb(16, "bfloat16"), "WC": _sb(16, "float32"), "WD": _sb(8, "float32"),
+    "PI": _sb(4, "int32"), "CI": _sb(4, "int32"), "CF": _sb(8, "float32"), "ONES": _sb(256, "bfloat16"),
+    "NEG": _sb(512, "bfloat16"), "INA": _sb(512, "bfloat16"), "IND": _sb(512, "bfloat16"),
+    "TMQ": _sb(64, "bfloat16"), "SAMH": _sb(128, "float16"), "TRI": _sb(512, "bfloat16"), "IDS": _sb(384, "bfloat16"),
+    "PM": _sb(64, "bfloat16"), "WID": _sb(4 * 144, "bfloat16"), "SQ": _sb(8, "bfloat16"), "TJ": _sb(J, "float32"),
+    "TBC": _sb(J, "bfloat16"), "CS": _sb(H * 512, "float16"), "SI": _sb(256, "int32"), "SA": _sb(256, "int32"),
+    "CB": _sb(256, "bfloat16"), "LT": _sb(64, "uint16"), "LN": _sb(64, "uint16"), "LP": _sb(64, "uint16"),
+    "KL": _sb(R * 64, "uint16"), "KIN": _sb(R * 48, "uint16"), "VO": _sb(R * 768, "bfloat16"), "VG": _sb(R * 1024, "bfloat16"),
+    "PR": _sb(1024, "float16"), "C5": _sb(256, "float32"), "M": _sb(1024, "float32"), "AB": _sb(256, "float32"),
+    "YB": _sb(256, "bfloat16"),
+})
+SEMAPHORES = (["v", "s", "p", "g", "ls", "la", "n0", "n1", "n2", "lt", "wl", "pri", "x", "z", "pt", "add", "ta"]
+              + [n % k for n in ("pp%d", "tb%d", "y%d", "val%d") for k in range(4)]
+              + [n % (k, h) for n in ("ka%d_%d", "va%d_%d") for k in range(R) for h in range(H)])
+
+CY, PE, GAT, FIX, WAKE, HOP, ROW, BW = 1.04e-3, 0.52e-3, 1.56, 0.06, 0.1, 2.4, 0.03, 20e3
+PLAN = {"gc": "vs", "gb": "s", "ga": "s", "gp": "s", "vo": "vs", "rc": "v", "rb": "v", "ra": "v", "rp": "s", "vown": "v", "evac": 6,
+        "early": 2, "lag": 2, "late": 3, "first": "pkxz", "then": "l", "llat": 11.0}
+
+
+def lanes(topo, src, dsts):
+    far = [c for c in dsts if topo.die(c) != topo.die(src)]
+    near = [c for c in dsts if c not in far]
+    out = {}
+    for part, start in ((far, 0), (near, 1)):
+        for k, c in enumerate(part):
+            e = topo.engines(src, c)[start::2]
+            n = 1
+            while 2 * n * len(part) <= len(e):
+                n *= 2
+            out[c] = e[k * n:(k + 1) * n]
+    return out
+
+
+def order(ops):
+    n = len(ops)
+    succ = [[] for _ in range(n)]
+    for i, o in enumerate(ops):
+        for d in o["deps"] | o["after"]:
+            succ[d].append(i)
+    tail = [0.0] * n
+    for i in range(n - 1, -1, -1):
+        tail[i] = ops[i]["cost"] + ops[i]["lat"] + max([tail[j] + WAKE for j in succ[i]] + [0.0])
+    left = [len(o["deps"] | o["after"]) for o in ops]
+    start, end, free, wire = [0.0] * n, [0.0] * n, {}, [0.0]
+    ready = [i for i in range(n) if not left[i]]
+    done = []
+
+    def est(i):
+        o = ops[i]
+        return max([free.get(o["q"], 0.0)] + [end[d] + WAKE for d in o["deps"]] + [start[d] for d in o["after"]])
+    while ready:
+        e = {i: est(i) for i in ready}
+        j = min(ready, key=lambda i: (e[i] + ops[i]["cost"], i))
+        near = [i for i in ready if ops[i]["q"] == ops[j]["q"] and e[i] < e[j] + ops[j]["cost"]]
+        k = max(near, key=lambda i: (ops[i]["kind"] == "dma", round(tail[i] - e[i], 3), -i))
+        o = ops[k]
+        start[k] = e[k]
+        free[o["q"]] = e[k] + o["cost"]
+        end[k] = free[o["q"]] + o["lat"]
+        if o["wire"]:
+            wire[0] = max(wire[0], end[k] - 0.7) + o["wire"]
+            end[k] = wire[0] + 0.7
+        ready.remove(k)
+        done.append(k)
+        for i in succ[k]:
+            left[i] -= 1
+            if not left[i]:
+                ready.append(i)
+    return done
+
+
+def rank_program(g, core, T, topo):
+    cores = list(T.cores)
+    rank = T.rank_of(core)
+    if rank is None:
+        return
+    peers = [c for c in cores if c != core]
+    Q = {"v": g.vector, "s": g.scalar, "p": g.tensor, "g": g, "y": g.sync}
+    ops, wrs, rds, last = [], {}, {}, {}
+
+    def add(q, kind, rd, wr, cost, lat=0.0, wire=0.0, fixed=False, **k):
+        deps = set()
+        for key in rd:
+            deps |= set(wrs.get(key, []))
+        for key in wr:
+            deps |= set(wrs.get(key, []) + rds.get(key, []))
+        i = len(ops)
+        after = set()
+        if fixed:
+            if q in last:
+                after.add(last[q])
+            last[q] = i
+        for key in wr:
+            wrs[key], rds[key] = [i], []
+        for key in rd:
+            rds.setdefault(key, []).append(i)
+        ops.append(dict(k, q=q, kind=kind, deps=deps, after=after, cost=cost, lat=lat, wire=wire))
+
+    def op(q, fn, rd, wr, cost):
+        add(q, "op", rd, wr, cost, fn=fn)
+
+    def mm(items, rd, wr, n):
+        def fn():
+            for it in items:
+                end = g.tensor.matmul(*it)
+            return end
+        op("p", fn, rd, wr, len(items) * max(n, 64) * PE)
+
+    def dma(q, sem, out, in_, rd, wr, rows, size):
+        add(q, "dma", rd, wr, 0.06, 1.8, rows / 16 * (ROW + size / BW), True, sem=sem, out=out, in_=in_)
+
+    def exchange(sem, src_of, dst_of, rd, lands, lat, wire=0.0):
+        add("g", "send", rd, lands, 0.6, lat, wire, sem=sem, src=src_of, dst=dst_of)
+
+    vv, ss = g.vector, g.scalar
+    PS = T.PS
+
+    def bank(b, a=0, n=512):
+        return PS[:, 512 * b + a:512 * b + a + n]
+
+    def cyc(n):
+        return FIX + max(n, 64) * CY
+
+    def ts(out, in0, s1, s2, o0, o1, rd, wr, n=64):
+        if o1 is None:
+            op("v", lambda: vv.tensor_scalar(out, in0, s1, None, o0), rd, wr, cyc(n))
+        else:
+            op("v", lambda: vv.tensor_scalar(out, in0, s1, s2, o0, o1), rd, wr, cyc(n))
+
+    def tt(out, a, b, o, rd, wr, n):
+        op("v", lambda: vv.tensor_tensor(out, a, b, o), rd, wr, cyc(n))
+
+    def cp(out, a, rd, wr, n=64):
+        op("v", lambda: vv.tensor_copy(out, a), rd, wr, cyc(n))
+
+    def fill(ap, c, wr, n=64):
+        op("v", lambda: vv.memset(ap, c), (), wr, cyc(n))
+
+    def act(out, a, rd, wr, n, func=AF.Identity, bias=0.0, scale=1.0):
+        op("s", lambda: ss.activation(out, a, func, bias=bias, scale=scale), rd, wr, cyc(n))
+
+    def pick(q, buf, a, win, off, b, n, rd, key):
+        cut = [0, n // 64 * 2, n // 16] if len(q) == 2 else [0, n // 16]
+        for k, e in enumerate(q):
+            (cp if e == "v" else act)(buf[:, a + 16 * cut[k]:a + 16 * cut[k + 1]], win.indirect(off[:, b + cut[k]:b + cut[k + 1]]),
+                                      rd, [key + "ab"[k]], GAT * 16 * (cut[k + 1] - cut[k]))
+        return [key + "ab"[k] for k in range(len(q))]
+
+    def digit(q, out, src, rd, wr, n):
+        if q == "v":
+            ts(out, src, 1.0 / 17, 192.0, A.mult, A.add, rd, wr, n / 2)
+        else:
+            act(out, src, rd, wr, n, bias=192.0, scale=1.0 / 17)
+
+    def sel(out, a, pat, cmp, base, mult, rd, wr, n):
+        op("g", lambda: g.affine_select(out, a, pat, cmp, 0.0, base, mult), rd, wr, 0.17 + 2 * n * CY)
+
+    dma("y", "n0", T.NAT[:, 0:256], T.nxt[:], (), ["nat0"], 128, 1024)
+    dma("s", "n0", T.NAT[:, 256:512], T.prv[:], (), ["nat1"], 128, 1024)
+    dma("y", "n1", T.NAT[:, 512:768], T.rw[:], (), ["nat2"], 128, 1024)
+    dma("s", "wl", T.WR[0::2, 1:15], T.w[:], (), ["wr0"], 64, 28)
+    dma("s", "wl", T.WR[1::2, 0:14], T.w[:], (), ["wr1"], 64, 28)
+
+    def load(n):
+        if n == "k":
+            dma("y", "n2", T.NAT[:, 768:1024], T.key[:], (), ["nat3"], 128, 1024)
+        if n == "l":
+            for k, tab in enumerate((T.nxt, T.prv)):
+                for h in range(2):
+                    dma("y", "lt", T.LTI[:, 2 * k + h], tab[h::2, :], (), ["lti%d" % (2 * k + h)], 128, 512)
+        if n == "p":
+            dma("y", "pri", T.PRI[:], T.pri[:], (), ["PRI"], 128, 1024)
+        if n in "xz":
+            c = slice(0, 2048) if n == "x" else slice(2048, 4096)
+            dma("y", n, T.X[:, c], T.x[:, c], (), [n], 128, 4096)
+    for n in PLAN["first"]:
+        load(n)
+
+    op("g", lambda: g.iota(T.PI[:, 0:1], [[0, 1]], 0, 1), (), ["PI"], 0.14)
+    fill(T.ONES[:], 1.0, ["ONES"], 128)
+    for b in ("MA", "SEL", "EQ"):
+        fill(T[b][:], 0.0, [b])
+    for k, m in enumerate((1, 15, 13)):
+        ts(T.CI[:, k:k + 1], T.PI[:, 0:1], m, None, A.bitwise_and, None, ["PI"], ["CI%d" % k])
+    fill(T.WID[:], 0.0, ["WID"], 288)
+    cp(T.CF[:, 0:3], T.CI[:, 0:3], ["CI0", "CI1", "CI2"], ["CF"])
+    fill(T.NEG[:], -192.0, ["NEG"], 256)
+    ts(T.CF[:, 3:4], T.CF[:, 0:1], 16.0, 1.0, A.mult, A.add, ["CF"], ["C17"])
+    ts(T.CF[:, 4:5], T.CF[:, 0:1], -1.0, 1.0, A.mult, A.add, ["CF"], ["EVN"])
+    ts(T.CF[:, 5:6], T.CF[:, 1:2], 16.0, None, A.mult, None, ["CF"], ["P16"])
+    fill(T.PB[:, 0:16], 0.0, ["PB0"])
+    for k in range(2):
+        fill(T.ADD[:, 1024 * k:1024 * k + 1024], 0.0, ["ADDa%d" % k], 512)
+    sel(T.TMQ[:], T.ONES[:, 0:64], [[-2, 64]], A.is_ge, 0, 1, ["ONES"], ["TMQ"], 64)
+    sel(T.PM[:], T.TMQ[:], [[2, 64]], A.is_ge, 1, -1, ["TMQ"], ["PM"], 64)
+    sel(T.SEL[:, 1::2], T.ONES[:, 0:64], [[-1, 8], [-8, 8]], A.is_equal, 0, 1, ["ONES"], ["SEL"], 64)
+    sel(T.ID[:], T.ONES[:, 0:128], [[-1, 128]], A.is_equal, 0, 1, ["ONES"], ["ID"], 128)
+    sel(T.TMP[:], T.ONES[:, 0:128], [[-16, 8], [0, 16]], A.is_ge, 0, 1, ["ONES"], ["TMP"], 128)
+    sel(T.SAME[:], T.TMP[:], [[16, 8], [0, 16]], A.is_ge, 15, -1, ["TMP"], ["SAME"], 128)
+    op("g", lambda: g.iota(T.TJ[:], [[0, N], [256, J // N]], 0, 0, allow_small_or_imprecise_dtypes=True), (), ["TJ"], 0.2)
+    sel(T.INA[:], T.NEG[:], [[-2, N], [0, C]], A.is_ge, 0, 1, ["NEG"], ["INA"], 512)
+    sel(T.IND[:], T.INA[:], [[2, N], [0, C]], A.is_ge, 1, -1, ["INA"], ["IND"], 512)
+    for k in range(8):
+        act(T.ADD[:, 2048 + 256 * k:2304 + 256 * k], T.ONES[:], ["ONES"], ["ADDb%d" % k], 256, scale=0.0)
+    act(T.MA[:, 0::2], T.PM[:], ["PM"], ["MA"], 64)
+    act(T.PK[:], T.MA[:], ["MA", "C17"], ["PK"], 128, scale=T.CF[:, 3:4])
+    act(T.EQ[:, 2 * rank:2 * rank + 1], T.CF[:, 4:5], ["EVN", "EQ"], ["EQ0"], 64)
+    act(T.EQ[:, 2 * rank + 1:2 * rank + 2], T.CF[:, 0:1], ["CF", "EQ"], ["EQ1"], 64)
+    act(T.S256[:], T.SAME[:], ["SAME"], ["S256"], 128, scale=1.0 / 256)
+    for k, (s, cmp) in enumerate(((1, A.is_ge), (-1, A.is_gt), (1, A.is_gt), (-1, A.is_ge))):
+        sel(T.TRI[:, 128 * k:128 * k + 128], T.S256[:], [[s, 128]], cmp, 0, -s, ["S256"], ["tri%d" % k], 128)
+    for k, c in enumerate((BIG, -BIG, 16.0)):
+        act(T.IDS[:, 128 * k:128 * k + 128], T.ID[:], ["ID"], ["ids%d" % k], 128, scale=c)
+    act(T.TBC[:], T.TJ[:], ["TJ", "P16"], ["TBC"], 64, bias=T.CF[:, 5:6])
+    act(T.WID[:, 15:143:16], T.SAME[:, 0::16], ["SAME", "CF", "WID"], ["widt"], 64, scale=T.CF[:, 1:2])
+    act(T.SQ[:], T.SAME[:, 0::16], ["SAME", "CF"], ["SQ"], 64, scale=T.CF[:, 2:3])
+    act(T.TMR[:], T.SAME[:], ["SAME", "CF"], ["TMR"], 128, scale=T.CF[:, 2:3])
+    for k, c in enumerate((13.0, 1.0, 5.0)):
+        ts(T.WID[:, 144 * k + 159:144 * k + 287:16], T.SQ[:], c, None, A.is_equal, None, ["SQ", "WID"], ["wid%d" % k])
+    ts(T.RWS[:], T.TMR[:], 9.0, None, A.is_equal, None, ["TMR"], ["RWS"])
+    cp(T.SAMH[:], T.SAME[:], ["SAME"], ["SAMH"])
+
+    cp(T.HI[:, 0:512], T.NAT[:, 0:512], ["nat0", "nat1"], ["HIa"], 512)
+    ts(T.RY[:], T.NAT[:, 512:768], 6144.0, None, A.add, None, ["nat2"], ["RY"], 256)
+    tt(T.LO[:, 0:512], T.NAT[:, 0:512], T.HI[:, 0:512], A.subtract, ["nat0", "nat1", "HIa"], ["LOa"], 1024)
+    ts(T.HI[:, 512:768], T.RY[:], -6144.0, None, A.add, None, ["RY"], ["HIb"], 128)
+    tt(T.LO[:, 512:768], T.NAT[:, 512:768], T.HI[:, 512:768], A.subtract, ["nat2", "HIb"], ["LOb"], 512)
+    for r in (0, 2, 1, 3, 4, 5):
+        src, key = ((T.HI, "HI"), (T.LO, "LO"))[r % 2]
+        k = r // 2
+        dma("y", "pt", T.PT[8 * r:8 * r + 8, :], src[:, 256 * k:256 * k + 256], [key + "aab"[k]], ["pt%d" % r], 128, 512)
+    for n in PLAN["then"]:
+        load(n)
+    cp(T.HI[:, 768:1024], T.NAT[:, 768:1024], ["nat3"], ["HIc"], 256)
+    tt(T.LO[:, 768:1024], T.NAT[:, 768:1024], T.HI[:, 768:1024], A.subtract, ["nat3", "HIc"], ["LOc"], 512)
+    zero = ["ADDa0", "ADDa1"] + ["ADDb%d" % k for k in range(8)]
+    for r in range(4, 8):
+        src, key = ((T.HI, "HI"), (T.LO, "LO"))[r % 2]
+        k = r // 2
+        dma("y", "add", T.ADD[2 * r + 1::16, :], src[:, 256 * k:256 * k + 256], [key + "aabc"[k]] + zero, ["add%d" % r], 128, 512)
+    VALK = ["val%d" % k for k in range(4)]
+
+    def load_val(k):
+        dma("y", VALK[k], T.VAL[:, 2048 * k:2048 * k + 2048], T.val[:, 2048 * k:2048 * k + 2048], (), [VALK[k]], 128, 4096)
+
+    L0 = rank * LW
+    cp(T.WC[:, 1:14], T.WR[:, 1:14], ["wr0", "wr1"], ["WC"])
+    ts(T.WD[:, 0:2], T.WC[:, 5:13:7], T.CF[:, 4:5], None, A.mult, None, ["WC", "EVN"], ["WD"])
+    cols = [(T.WD[:, 0:1], T.WD[:, 1:2])] + [(T.WC[:, a:a + 1], T.WC[:, a + 7:a + 8]) for a in (3, 6, 1)]
+    for t in range(4):
+        act(T.LALL[:, L0 + 128 * t:L0 + 128 * t + 128], T.MA[:], ["MA", "WD"], ["la%d" % t], 128, scale=cols[t][0])
+    for t in range(4):
+        act(T.LALL[:, L0 + 513 + 128 * t:L0 + 640 + 128 * t:2], T.PM[:], ["PM", "WD"], ["lo%d" % t], 64, scale=cols[t][1])
+    act(T.LALL[:, L0 + 512:L0 + 1024:2], T.LALL[:, L0:L0 + 512:2], ["la%d" % t for t in range(4)], ["le"], 256, scale=-17.0)
+    own = ["la%d" % t for t in range(4)] + ["lo%d" % t for t in range(4)] + ["le", "lb"]
+    mm([(bank(7, 0, 128), T.EQ[:], T.LALL[:, L0 + 512 + 128 * t:L0 + 640 + 128 * t], t == 0, t == 3) for t in range(4)],
+       ["EQ0", "EQ1"] + own[4:9], ["B7"], 128)
+    act(T.LALL[:, L0 + 1024:L0 + LW], bank(7, 0, 128), (), ["B7", "lb"], 128)
+    PTK = ["pt%d" % r for r in range(6)]
+    exchange("la", lambda c: T.LALL[:, L0:L0 + LW], lambda c: T.LALL[:, L0:L0 + LW], own, ["lpeer"], PLAN["llat"], 3.5)
+
+    cp(T.LTF[:], T.LTI[:], ["lti%d" % k for k in range(4)], ["LTF"], 512)
+    for b in range(8):
+        op("v", lambda b=b: vv.transpose(T.WF[:, b::8], T.LTF[:, :, b, :]), ["LTF"], ["wf%d" % b], cyc(64))
+    cp(T.WL[:], T.WF[:], ["wf%d" % b for b in range(8)], ["WL"], 512)
+
+    def lists(h, k, src, out, b, rd, wr, first=()):
+        it = list(first)
+        for i in range(16):
+            it.append((bank(b, 0, J), T.WID[:, 144 * k + 15 - i:144 * k + 143 - i], src[:, S * h + i:S * h + S:16], not it, i == 15))
+        mm(it, rd, ["B%d" % b], J)
+        cp(out, bank(b, 0, J), (), ["B%d" % b, wr])
+
+    def find(h):
+        n, W0, W1 = C * h + C, 4 * h, 4 * h + 1
+        for j, b in enumerate((W0, W1)):
+            mm([(bank(b, 0, n), T.TRI[:, 256 * j:256 * j + 128], T.PB[:, 16:16 + n], True, False),
+                (bank(b, 0, n), T.TRI[:, 256 * j + 128:256 * j + 256], T.PB[:, 15:15 + n], False, True)],
+               ["P%d" % k for k in range(h + 1)] + ["PB0", "tri%d" % (2 * j), "tri%d" % (2 * j + 1)], ["B%d" % b], n)
+            a = 512 * h + 256 * j
+            op("v", lambda a=a, b=b: vv.tensor_tensor_scan(T.CS[:, a:a + n], T.ONES[:, 0:n], bank(b, 0, n), 1032.0 - 127.5 / 256,
+                                                         A.mult, A.add), ["ONES"], ["B%d" % b, "cs%d%d" % (h, j)], cyc(n))
+        c = slice(C * h, n)
+        a = 512 * h + C * h
+        tt(T.SI[:, c], T.CS[:, a:a + C], T.CS[:, a + 256:a + 256 + C], A.add, ["cs%d0" % h, "cs%d1" % h], ["SI%d" % h], 2 * C)
+        ts(T.SA[:, c], T.SI[:, c], 7, None, A.bitwise_and, None, ["SI%d" % h], ["SA%d" % h], C)
+        cp(T.CB[:, c], T.SA[:, c], ["SA%d" % h], ["CB%d" % h], C)
+        for q in range(N):
+            a = S * h + C * q
+            ts(T.O[:, a:a + C], T.CB[:, c], float(2 * q + 1), None, A.is_equal, None, ["CB%d" % h], ["o%d%d" % (h, q)], C / 2)
+        lists(h, 0, T.O, T.LT[:, J * h:J * h + J], W0, ["o%d%d" % (h, q) for q in range(N)] + ["widt", "TBC", "ID"], "LT%d" % h,
+              [(bank(W0, 0, J), T.ID[:], T.TBC[:], True, False)])
+
+    for h in range(H):
+        cp(T.PB[:, 16 + C * h:16 + C * h + C], T.PRI[:, C * h:C * h + C], ["PRI"], ["P%d" % h], C)
+    for h in range(H):
+        find(h)
+
+    for b in range(8):
+        mm([(bank(b), T.PK[:], T.X[:, 512 * b:512 * b + 512], True, False)], ["PK", "xz"[b // 4]], ["B%d" % b], 512)
+    for b in range(8):
+        mm([(bank(b), T.SEL[0:48, :], T.PT[0:48, 512 * b:512 * b + 512], False, True)], ["SEL"] + PTK, ["B%d" % b], 512)
+    for b in range(8):
+        (act if b < PLAN["evac"] else cp)(T.BASE[:, 512 * b:512 * b + 512], bank(b), (), ["B%d" % b, "base%d" % b], 512)
+    BK = ["base%d" % b for b in range(8)]
+
+    for k in range(4):
+        c = slice(1024 * k, 1024 * k + 1024)
+        tt(T.CT[:, c], T.BASE[:, 0:F].indirect(T.WL[:, 64 * k:64 * k + 64]), T.ADD[:, c], A.add,
+           BK + ["WL"] + zero + ["add%d" % r for r in range(4, 8)], ["ce%d" % k, "cp%d" % k], GAT * 1024)
+        act(T.TB[:, c], T.BASE[:, 0:F].indirect(T.WL[:, 256 + 64 * k:320 + 64 * k]), BK + ["WL"], ["tbe%d" % k, "tbo%d" % k], GAT * 1024)
+    for k in range(PLAN["early"]):
+        load_val(k)
+    dma("y", "ta", T.TA[0::2, :], T.BASE[0::2, :], BK, ["ta"], 64, 8192)
+    for k in range(4 + PLAN["lag"]):
+        c = slice(1024 * k, 1024 * k + 1024)
+        if k < 4:
+            for r in (5, 7):
+                dma("y", "pp%d" % k, T.CT[r::16, c], T.TB[r::16, c], ["tbo%d" % k, "cp%d" % k], ["cq%d_%d" % (k, r)], 16, 1024)
+        b = k - PLAN["lag"]
+        if b >= 0:
+            d = slice(1024 * b, 1024 * b + 1024)
+            dma("y", "tb%d" % b, T.TB[1::2, d], T.BASE[0::2, d], BK, ["tbo%d" % b], 64, 2048)
+        if k < 4:
+            dma("y", "ta", T.TA[1::2, c], T.CT[0::2, c], ["ce%d" % k], ["tao%d" % k], 64, 2048)
+        if k == PLAN["late"]:
+            for b in range(PLAN["early"], 4):
+                load_val(b)
+    TBK = [n % k for k in range(4) for n in ("tbe%d", "tbo%d")]
+    TAK = ["ta"] + ["tao%d" % k for k in range(4)]
+    mm([(bank(3, 0, 128), T.ID[:], T.LALL[:, q * LW + 1024:q * LW + LW], q == 0, q == N - 1) for q in range(N)],
+       ["ID", "lb", "lpeer"], ["B3"], 128)
+    act(T.LBX[:], bank(3, 0, 128), (), ["B3", "LBX"], 128)
+
+    def judge(rd_, h):
+        W0, W1, HB, EB = 4 * h, 4 * h + 1, 4 * h + 2, 4 * h + 3
+        s, j, c = slice(S * h, S * h + S), slice(J * h, J * h + J), slice(C * h, C * h + C)
+        k_ = lambda n: "%s%d" % (n, h)
+        B = lambda b: "B%d" % b
+        chunks = range(4 // H * h, 4 // H * (h + 1))
+        win = slice(F // H * h, F // H * (h + 1))
+        OK = ["o%d%d" % (h, q) for q in range(N)]
+
+        def term(t, half, src, rd, stop=False):
+            a = 512 * half + 128 * t
+            mm([(bank(HB, C * q, C), T.LALL[:, q * LW + a:q * LW + a + 128], src[:, S * h + C * q:S * h + C * q + C], False,
+                 stop and q == N - 1) for q in range(N)], rd + own + ["lpeer"], [B(HB)], C)
+
+        GK = {"C": pick(PLAN["gc"], T.GC, S * h, T.CT[:, win], T.LT, J * h, S,
+                        [n % k for k in chunks for n in ("ce%d", "cq%d_5", "cq%d_7")] + [k_("LT")], k_("GC"))}
+        e = rd_ * H + h
+        K0, I0, O0, G0, Jq = J * e, 3 * J // N * e, 3 * C * e, S * e, J // N
+        lists(h, 1, T.GC, T.KL[:, K0:K0 + J], W1, GK["C"] + ["wid0"], "KL%d" % e)
+
+        def slot(d):
+            return [a for a in cores if a != d].index(core)
+        exchange("ka%d_%d" % (rd_, h), lambda d: T.KL[:, K0 + Jq * T.rank_of(d):K0 + Jq * T.rank_of(d) + Jq],
+                 lambda d: T.KIN[:, I0 + Jq * slot(d):I0 + Jq * slot(d) + Jq], ["KL%d" % e], ["KIN%d" % e], HOP - 0.6 + 32 * ROW)
+        vo = pick(PLAN["vo"], T.VO, O0, T.VAL[:, 0:V], T.KIN, I0, 3 * C, VALK + ["KIN%d" % e], "VO%d" % e)
+        exchange("va%d_%d" % (rd_, h), lambda d: T.VO[:, O0 + C * peers.index(d):O0 + C * peers.index(d) + C],
+                 lambda d: T.VG[:, G0 + C * rank:G0 + C * rank + C], vo, ["VG%d" % e], HOP - 0.6 + 32 * (ROW + 2 * C / BW))
+        VK = pick(PLAN["vown"], T.VG, G0 + C * rank, T.VAL[:, 0:V], T.KL, K0 + Jq * rank, C, VALK + ["KL%d" % e], "vown%d" % e) + ["VG%d" % e]
+        lists(h, 2, T.GC, T.LN[:, j], W0, GK["C"] + ["wid1"], k_("LN"))
+        lists(h, 3, T.GC, T.LP[:, j], W1, GK["C"] + ["wid2"], k_("LP"))
+        GK["B"] = pick(PLAN["gb"], T.GB, S * h, T.TB[:, win], T.LT, J * h, S,
+                       [n % k for k in chunks for n in ("tbe%d", "tbo%d")] + [k_("LT")], k_("GB"))
+        GK["A"] = pick(PLAN["ga"], T.GA, S * h, T.TA[:, 0:F], T.LN, J * h, S, TAK + [k_("LN")], k_("GA"))
+        GK["P"] = pick(PLAN["gp"], T.GP, S * h, T.TB[:, 0:F], T.LP, J * h, S, TBK + [k_("LP")], k_("GP"))
+        tt(T.GR[:, s], T.BASE[:, 0:F].indirect(T.LN[:, j]), T.GC[:, s], A.add, BK + GK["C"] + [k_("LN")], [k_("GR")], GAT * S)
+        mm([(bank(HB), T.LBX[:], T.IND[:], True, False)], ["LBX", "IND"], [B(HB)], S)
+        for t, n in enumerate("CBAP"):
+            digit(PLAN["r" + n.lower()], T["R" + n][:, s], T["G" + n][:, s], GK[n], [k_("R" + n)], S)
+            term(t, 0, T["G" + n], GK[n])
+            term(t, 1, T["R" + n], [k_("R" + n)], t == 3)
+        mm([(bank(EB), T.IDS[:, 0:128], T.O[:, s], True, False)], OK + ["ids0"], [B(EB)], S)
+        mm([(bank(EB), T.RWS[:], T.GR[:, s], False, False)], [k_("GR"), "RWS"], [B(EB)], S)
+        P1 = T.PB[:, 16 + C * h:16 + C * h + C]
+        mm([(bank(W0, 0, C), T.IDS[:, 256:384], P1, True, False)]
+           + [(bank(W0, 0, C), T.IDS[:, 128:256], T.O[:, S * h + C * q:S * h + C * q + C], False, q == N - 1) for q in range(N)],
+           OK + [k_("P"), "ids1", "ids2"], [B(W0)], C)
+        act(T.C5[:, c], bank(W0, 0, C), (), [B(W0), k_("C5")], C, bias=BIG)
+        tt(T.PR[:, s], bank(HB), T.VG[:, G0:G0 + S], A.mult, VK, [B(HB), k_("PR")], S)
+        mm([(bank(EB), T.SAMH[:], T.PR[:, s], False, True)], ["SAMH", k_("PR")], [B(EB)], S)
+        for q in range(N):
+            a = S * h + C * q
+            prev, pk = (T.C5[:, c], k_("C5")) if q == 0 else (T.M[:, a - C:a], "m%d%d" % (h, q - 1))
+            tt(T.M[:, a:a + C], bank(EB, C * q, C), prev, A.max, [pk], [B(EB), "m%d%d" % (h, q)], C)
+        act(T.AB[:, c], T.M[:, S * h + S - C:S * h + S], ["m%d3" % h], [k_("AB")], C, func=AF.Abs, bias=-BIG / 16, scale=1.0 / 16)
+        ts(T.YB[:, c], T.AB[:, c], 128.0 - 15.0 / 32, 191.0, A.add, A.min, [k_("AB")], [k_("YB")], C)
+        if rd_ < R - 1:
+            ts(P1, T.YB[:, c], 129.0, 128.0, A.max, A.subtract, [k_("YB")], [k_("P")], C / 2)
+        else:
+            ts(T.Y[:, c], T.YB[:, c], 129.0, 128.0, A.max, A.subtract, [k_("YB")], [k_("Y")], C)
+            dma("y", "y%d" % h, T.y[:, c], T.Y[:, c], [k_("Y")], (), 128, 4 * C)
+
+    for rd_ in range(R):
+        for h in range(H if rd_ else 0):
+            find(h)
+        for h in range(H):
+            judge(rd_, h)
+
+    known = {q: {} for q in Q}
+    count, groups, tok = {}, {}, {}
+    ln = lanes(topo, core, peers)
+    arrive = sum(len(lanes(topo, c, [d for d in cores if d != c])[core]) for c in peers)
+    for i in order(ops):
+        o = ops[i]
+        q = o["q"]
+        for t in sorted([tok[d] for d in o["deps"] if not (q == "p" and ops[d]["q"] == "p")], key=lambda t: -t["n"]):
+            if known[q].get(t["sem"], 0) < t["n"]:
+                Q[q].wait_ge(T.sem[t["sem"]], t["n"])
+                known[q][t["sem"]] = t["n"]
+            for s, n in t["clock"].items():
+                known[q][s] = max(known[q].get(s, 0), n)
+        if o["kind"] == "op":
+            o["fn"]().then_inc(T.sem[q], 1)
+            count[q] = count.get(q, 0) + 1
+            tok[i] = {"sem": q, "n": count[q], "clock": dict(known[q])}
+        elif o["kind"] == "dma":
+            Q[q].dma_start(o["out"], o["in_"]).then_inc(T.sem[o["sem"]], 16)
+            count[o["sem"]] = count.get(o["sem"], 0) + 16
+            t = tok[i] = groups.setdefault(o["sem"], {"sem": o["sem"], "n": 0, "clock": {}})
+            t["n"] = count[o["sem"]]
+            for s, n in known[q].items():
+                t["clock"][s] = max(t["clock"].get(s, 0), n)
+        else:
+            tr = []
+            for c in peers:
+                rid, pid, _ = topo.addr(c)
+                tr.append(RemoteDMATransfer(dst_ids=[DstId(rid=rid, pnc=pid)], dma_engine_mask=sum(1 << k for k in ln[c]),
+                                            remote_sem=T.sem[o["sem"]], src=o["src"](c), dst=o["dst"](c)))
+                count["ls"] = count.get("ls", 0) + len(ln[c])
+            g.remote_dma_fused(tr, local_sem=T.sem["ls"])
+            count[o["sem"]] = arrive
+            tok[i] = {"sem": o["sem"], "n": arrive, "clock": {}}
+    for s, n in sorted(count.items(), key=lambda a: a[0][0] == "y"):
+        g.wait_ge(T.sem[s], n)

@@ -1,44 +1,53 @@
 from concourse.bass import DstId, RemoteDMATransfer
-from concourse.mybir import AluOpType as A, ActivationFunctionType as AF
+from concourse.mybir import AluOpType as A, ActivationFunctionType as AF, AxisListType as AX
 
 F, V, R, N = 4096, 8192, 3, 4
-BIG = 65536.0
-LW = 9 * 128
+BIG = 4096.0
+LW = 8 * 128
 H = 2
 C = 256 // H
 S = N * C
 J = S // 16
+TA, TB, BA, VA = 0, F, 2 * F, 3 * F + 16
+BANKS = ["B%d" % b for b in range(8)]
+VC = 4
+
+CY, PE, GAT, FIX, WAKE, HOP, ROW, BW = 0.95e-3, 0.48e-3, 1.56, 0.04, 0.12, 2.1, 0.02, 28e3
+PLAN = {"mode": "xxl", "gc": "vs", "gb": "s", "g4": "sssv", "g4x": "sssv", "dig": "vvvv", "digx": "vvvv", "vo": "vs", "gk": "",
+        "evac": "svsvsvsv", "first": "klxz", "then": "p", "llat": 6.0, "vlat": 14.0, "valq": "y", "zadd": "vvssssgg", "direct": 0,
+        "flat": 0, "lfirst": 20.0, "find0": 0, "line": "v", "gkafter": "ce3", "split": 1, "passes": 4, "tries": 300, "slack": 1.0, "lead": 0.0,
+        "vat": ["012", "", "3"], "vafter": [[], ["tbe3"], ["tbe3"], ["tbe3"]]}
 
 
 def _sb(cols, dtype):
     return ("sbuf", [128] + (cols if isinstance(cols, list) else [cols]), dtype)
 
 
-SCRATCH = {"PS": ("psum", [128, 4096], "float32"), "VAL": _sb(V, "bfloat16"), "LALL": _sb(N * LW, "bfloat16")}
-SCRATCH.update({n: _sb(F, "bfloat16") for n in ("X", "BASE", "CT", "TB", "TA", "ADD", "PT")})
-SCRATCH.update({n: _sb(1024, "bfloat16") for n in ("HI", "LO", "O", "GC", "GB", "GA", "GP", "GR", "RC", "RB", "RA", "RP")})
-SCRATCH.update({n: _sb(128, "bfloat16") for n in ("TMP", "TMR", "SAME", "S256", "ID", "MA", "PK", "SEL", "RWS", "EQ", "LBX")})
+SCRATCH = {"PS": ("psum", [128, 4096], "float32"), "TAB": _sb(VA + N * V, "bfloat16"), "LALL": _sb(N * LW, "bfloat16")}
+SCRATCH.update({n: _sb(F, "bfloat16") for n in ("X", "CT", "ADD")})
+SCRATCH.update({n: _sb(4 * H * S, "bfloat16") for n in ("G4", "R4")})
+SCRATCH.update({n: _sb(1024, "bfloat16") for n in ("GC", "GB", "GK", "RC", "RB")})
+SCRATCH.update({n: _sb(128, "bfloat16") for n in ("TMP", "SAME", "S1K", "ID", "PK", "RW1", "RW2", "SUP", "DGB", "K4L")})
+MATS = (("MA", 128), ("EQ", 128), ("WK", 144), ("W4X", 144), ("W4L", 144), ("SEL", 128), ("WA1", 144), ("WN", 144), ("WP", 144), ("WA4", 144),
+        ("DG2", 128), ("DG1", 128), ("SAMH", 128))
+AT = {n: sum(w for _, w in MATS[:k]) for k, (n, _) in enumerate(MATS)}
+ZW = sum(w for _, w in MATS)
 SCRATCH.update({
-    "NAT": _sb(1024, "int32"), "RY": _sb(256, "bfloat16"), "LTI": _sb([4, 8, 16], "int32"), "LTF": _sb([4, 8, 16], "float32"),
-    "WF": _sb(512, "float32"), "WL": _sb(512, "uint16"), "PRI": _sb(256, "int32"), "PB": _sb(272, "bfloat16"),
+    "ZB": _sb(ZW, "bfloat16"), "ZH": _sb(ZW, "float16"), "PT": _sb(F, "float16"), "PH": _sb(768, "float16"), "PV": _sb(768, "float16"),
+    "HI": _sb(512, "bfloat16"), "LO": _sb(512, "bfloat16"), "IO": _sb(16, "float32"), "E16": _sb(16, "float32"), "EK": _sb(16, "float32"),
+    "NAT": _sb(1024, "int32"), "LTI": _sb([4, 8, 16], "int32"), "LTF": _sb([4, 8, 16], "float16"),
+    "WF": _sb(512, "float16"), "WL": _sb(512, "uint16"), "PRI": _sb(256, "int32"), "PB": _sb(272, "bfloat16"),
     "Y": _sb(256, "float32"), "WR": _sb(16, "bfloat16"), "WC": _sb(16, "float32"), "WD": _sb(8, "float32"),
-    "PI": _sb(4, "int32"), "CI": _sb(4, "int32"), "CF": _sb(8, "float32"), "ONES": _sb(256, "bfloat16"),
-    "NEG": _sb(512, "bfloat16"), "INA": _sb(512, "bfloat16"), "IND": _sb(512, "bfloat16"),
-    "TMQ": _sb(64, "bfloat16"), "SAMH": _sb(128, "float16"), "TRI": _sb(512, "bfloat16"), "IDS": _sb(384, "bfloat16"),
-    "PM": _sb(64, "bfloat16"), "WID": _sb(4 * 144, "bfloat16"), "SQ": _sb(8, "bfloat16"), "TJ": _sb(J, "float32"),
-    "TBC": _sb(J, "bfloat16"), "CS": _sb(H * 512, "float16"), "SI": _sb(256, "int32"), "SA": _sb(256, "int32"),
-    "CB": _sb(256, "bfloat16"), "LT": _sb(64, "uint16"), "LN": _sb(64, "uint16"), "LP": _sb(64, "uint16"),
-    "KL": _sb(R * 64, "uint16"), "KIN": _sb(R * 48, "uint16"), "VO": _sb(R * 768, "bfloat16"), "VG": _sb(R * 1024, "bfloat16"),
-    "PR": _sb(1024, "float16"), "C5": _sb(256, "float32"), "M": _sb(1024, "float32"), "AB": _sb(256, "float32"),
-    "YB": _sb(256, "bfloat16"),
+    "PI": _sb(4, "int32"), "CI": _sb(4, "int32"), "CF": _sb(24, "float32"), "ONES": _sb(256, "bfloat16"),
+    "TMQ": _sb(64, "bfloat16"), "TRI": _sb(256, "bfloat16"), "PM": _sb(64, "bfloat16"),
+    "TJ": _sb(J, "float32"), "TBC": _sb(J, "bfloat16"), "TJ4": _sb(128, "float32"), "TJL": _sb(128, "float32"), "K4X": _sb(128, "bfloat16"),
+    "AQ": _sb([N, 272], "float16"), "OFF": _sb(S, "float32"), "CAR": _sb(4, "float32"),
+    "LT": _sb(H * J, "uint16"), "L4": _sb(H * 4 * J, "uint16"), "KL": _sb(R * H * 56, "uint16"), "VG": _sb(R * H * 7 * C, "bfloat16"),
+    "PR": _sb(1024, "float16"), "M": _sb(1024, "float32"), "AA": _sb(256, "float32"), "AB": _sb(256, "float32"), "YB": _sb(256, "bfloat16"),
 })
-SEMAPHORES = (["v", "s", "p", "g", "ls", "la", "n0", "n1", "n2", "lt", "wl", "pri", "x", "z", "pt", "add", "ta"]
-              + [n % k for n in ("pp%d", "tb%d", "y%d", "val%d") for k in range(4)]
+SEMAPHORES = (["v", "s", "p", "g", "ls", "la", "vall", "n0", "n1", "n2", "lt", "wl", "pri", "x", "z", "pt", "add", "ta"]
+              + [n % k for n in ("pp%d", "tb%d", "y%d", "val%d", "rv%d") for k in range(4)]
               + [n % (k, h) for n in ("ka%d_%d", "va%d_%d") for k in range(R) for h in range(H)])
-
-CY, PE, GAT, FIX, WAKE, HOP, ROW, BW = 1.04e-3, 0.52e-3, 1.56, 0.06, 0.1, 2.4, 0.03, 20e3
-PLAN = {"gc": "vs", "gb": "s", "ga": "s", "gp": "s", "vo": "vs", "rc": "v", "rb": "v", "ra": "v", "rp": "s", "vown": "v", "evac": 6,
-        "early": 2, "lag": 2, "late": 3, "first": "pkxz", "then": "l", "llat": 11.0}
 
 
 def lanes(topo, src, dsts):
@@ -55,73 +64,164 @@ def lanes(topo, src, dsts):
     return out
 
 
-def order(ops):
-    n = len(ops)
-    succ = [[] for _ in range(n)]
-    for i, o in enumerate(ops):
-        for d in o["deps"] | o["after"]:
-            succ[d].append(i)
-    tail = [0.0] * n
-    for i in range(n - 1, -1, -1):
-        tail[i] = ops[i]["cost"] + ops[i]["lat"] + max([tail[j] + WAKE for j in succ[i]] + [0.0])
-    left = [len(o["deps"] | o["after"]) for o in ops]
-    start, end, free, wire = [0.0] * n, [0.0] * n, {}, [0.0]
+def helpers(topo, cores):
+    out = {}
+    for c in cores:
+        out[c] = [d for d in topo.cores_of(c) if d not in cores and d not in out.values() and topo.die(d) == topo.die(c)][0]
+    return out
+
+
+def dest(topo, c):
+    rid, pid, _ = topo.addr(c)
+    return DstId(rid=rid, pnc=pid)
+
+
+def place(ops, succ, pred, prio, span):
+    n, back = len(ops), span is not None
+    left = [len(p) for p in pred]
+    start, end, free, wire, dep = [0.0] * n, [0.0] * n, {}, 0.0, [0.0] * n
     ready = [i for i in range(n) if not left[i]]
     done = []
-
-    def est(i):
-        o = ops[i]
-        return max([free.get(o["q"], 0.0)] + [end[d] + WAKE for d in o["deps"]] + [start[d] for d in o["after"]])
     while ready:
-        e = {i: est(i) for i in ready}
+        e = {i: max(dep[i], free.get(ops[i]["q"], 0.0)) for i in ready}
         j = min(ready, key=lambda i: (e[i] + ops[i]["cost"], i))
         near = [i for i in ready if ops[i]["q"] == ops[j]["q"] and e[i] < e[j] + ops[j]["cost"]]
-        k = max(near, key=lambda i: (ops[i]["kind"] == "dma", round(tail[i] - e[i], 3), -i))
+        k = max(near, key=lambda i: (ops[i]["kind"] == "dma" and not back, round(prio[i] - PLAN["slack"] * e[i], 3), -i))
         o = ops[k]
         start[k] = e[k]
-        free[o["q"]] = e[k] + o["cost"]
-        end[k] = free[o["q"]] + o["lat"]
-        if o["wire"]:
-            wire[0] = max(wire[0], end[k] - 0.7) + o["wire"]
-            end[k] = wire[0] + 0.7
+        end[k] = free[o["q"]] = e[k] + o["cost"]
+        if not back:
+            end[k] += o["lat"]
+            if o["wire"]:
+                wire = max(wire, end[k] - 0.5) + o["wire"]
+                end[k] = wire + 0.5
         ready.remove(k)
         done.append(k)
-        for i in succ[k]:
+        for i, gap in succ[k]:
+            if back:
+                dep[i] = max(dep[i], end[k] + (0.0 if gap is None else gap + span[i]))
+            else:
+                dep[i] = max(dep[i], start[k] if gap is None else end[k] + gap)
             left[i] -= 1
             if not left[i]:
                 ready.append(i)
-    return done
+    return done, start, end
+
+
+def order(ops):
+    n = len(ops)
+    if n in ORDER:
+        return ORDER[n]
+    succ, pred = [[] for _ in range(n)], [[] for _ in range(n)]
+    for i, o in enumerate(ops):
+        for d in o["deps"] | o["after"]:
+            gap = None if d not in o["deps"] else 0.0 if o["q"] == ops[d]["q"] == "p" else WAKE
+            succ[d].append((i, gap))
+            pred[i].append((d, gap))
+    tail = [0.0] * n
+    for i in range(n - 1, -1, -1):
+        tail[i] = ops[i]["cost"] + ops[i]["lat"] + ops[i]["wire"] + max([tail[j] + WAKE for j, _ in succ[i]] + [0.0])
+    lead = [o["lead"] for o in ops]
+    for i in range(n - 1, -1, -1):
+        lead[i] = max([lead[i]] + [lead[j] for j, gap in succ[i] if gap is not None])
+    best = None
+    for _ in range(PLAN["passes"]):
+        tail = [tail[i] + lead[i] for i in range(n)]
+        done, start, end = place(ops, succ, pred, tail, None)
+        if best is None or max(end) < best[0]:
+            best = (max(end), done, tail)
+        tail = place(ops, pred, succ, end, [end[i] - start[i] - ops[i]["cost"] for i in range(n)])[2]
+    seed = 1
+    for k in range(PLAN["tries"]):
+        prio = list(best[2])
+        for _ in range(n // (10, 40)[k % 2]):
+            seed = (seed * 1103515245 + 12345) % 2 ** 31
+            prio[seed // 64 % n] += (seed // 16384 % 201 - 100) * (0.005, 0.015, 0.04)[k % 3]
+        done, start, end = place(ops, succ, pred, prio, None)
+        if max(end) <= best[0]:
+            best = (max(end), done, prio)
+    EST.append(best[0])
+    ORDER[n] = best[1]
+    return best[1]
+
+
+EST, ORDER = [], {}
+
+
+def val_at(T, b, k):
+    return T.TAB[:, VA + V * b + V // VC * k:VA + V * b + V // VC * (k + 1)]
+
+
+def block(cores, at, q):
+    return 0 if at == q else 1 + [c for c in cores if c != at].index(q)
+
+
+def direct(topo, cores, c):
+    return [d for d in cores if d != c and topo.die(d) == topo.die(c)] if PLAN["direct"] else []
+
+
+def helper_program(g, core, T, topo):
+    cores = list(T.cores)
+    src = [c for c, d in helpers(topo, cores).items() if d == core]
+    if not src or "l" not in PLAN["mode"]:
+        return
+    to = [c for c in cores if c != src[0] and c not in direct(topo, cores, src[0])]
+    n = len(topo.engines(core, to[0]))
+    got = len(topo.engines(src[0], core)) // (2 if PLAN["direct"] else 1)
+    for k in range(VC):
+        g.wait_ge(T.sem["rv%d" % k], got)
+        g.remote_dma_fused([RemoteDMATransfer(dst_ids=[dest(topo, c) for c in to], dma_engine_mask=topo.mask(core, to[0]),
+                                              remote_sem=T.sem["vall"], src=val_at(T, 0, k),
+                                              dsts=[val_at(T, block(cores, c, src[0]), k) for c in to])], local_sem=T.sem["ls"])
+    g.wait_ge(T.sem["ls"], n * VC)
 
 
 def rank_program(g, core, T, topo):
     cores = list(T.cores)
     rank = T.rank_of(core)
     if rank is None:
-        return
+        return helper_program(g, core, T, topo)
     peers = [c for c in cores if c != core]
+    learner = [T.rank_of(c) for c in [core] + peers]
     Q = {"v": g.vector, "s": g.scalar, "p": g.tensor, "g": g, "y": g.sync}
-    ops, wrs, rds, last = [], {}, {}, {}
+    ops, wrs, rds, last, lead = [], {}, {}, {}, [0.0]
 
-    def add(q, kind, rd, wr, cost, lat=0.0, wire=0.0, fixed=False, **k):
+    opened, size, issued = {}, {}, {}
+
+    def add(q, kind, rd, wr, cost, lat=0.0, wire=0.0, fixed=False, group=None, **k):
         deps = set()
         for key in rd:
             deps |= set(wrs.get(key, []))
+        i = len(ops)
+        if group:
+            if group not in opened:
+                opened[group] = set(wrs.get(wr[0], []) + rds.get(wr[0], []))
+                wrs[wr[0]], rds[wr[0]] = [], []
+            deps |= opened[group]
+            wrs[wr[0]].append(i)
+            wr = wr[1:]
+        if q != "p":
+            for key in [key for key in wr if key in BANKS]:
+                deps |= set(wrs.get(key, []) + [d for d in rds.get(key, []) if ops[d]["q"] != q])
+                rds.setdefault(key, []).append(i)
+            wr = [key for key in wr if key not in BANKS]
         for key in wr:
             deps |= set(wrs.get(key, []) + rds.get(key, []))
-        i = len(ops)
         after = set()
         if fixed:
-            if q in last:
-                after.add(last[q])
-            last[q] = i
+            if fixed in last:
+                after.add(last[fixed])
+            last[fixed] = i
         for key in wr:
             wrs[key], rds[key] = [i], []
         for key in rd:
             rds.setdefault(key, []).append(i)
-        ops.append(dict(k, q=q, kind=kind, deps=deps, after=after, cost=cost, lat=lat, wire=wire))
+        ops.append(dict(k, q=q, kind=kind, deps=deps, after=after, cost=cost, lat=lat, wire=wire, lead=lead[0]))
+
+    line = [PLAN["line"]]
 
     def op(q, fn, rd, wr, cost):
-        add(q, "op", rd, wr, cost, fn=fn)
+        add(q, "op", rd, wr, cost, fixed=q in line[0] and wr[-1] not in ("SELH", "WH", "DGB", "DH") and "line" + q, fn=fn)
 
     def mm(items, rd, wr, n):
         def fn():
@@ -130,14 +230,30 @@ def rank_program(g, core, T, topo):
             return end
         op("p", fn, rd, wr, len(items) * max(n, 64) * PE)
 
+    def acc(group, items, rd, b, n, wr=()):
+        size[group] = size.get(group, 0) + len(items)
+
+        def fn():
+            for it in items:
+                issued[group] = issued.get(group, 0) + 1
+                end = g.tensor.matmul(*it, issued[group] == 1, issued[group] == size[group])
+            return end
+        add("p", "op", rd, ["B%d" % b] + list(wr), len(items) * max(n, 64) * PE, group=group, fn=fn)
+
     def dma(q, sem, out, in_, rd, wr, rows, size):
-        add(q, "dma", rd, wr, 0.06, 1.8, rows / 16 * (ROW + size / BW), True, sem=sem, out=out, in_=in_)
+        add(q, "dma", rd, wr, 0.06, 1.55, rows / 16 * (ROW + size / BW), q, sem=sem, out=out, in_=in_)
+
+    ln = lanes(topo, core, peers)
+    arrive = sum(len(lanes(topo, c, [d for d in cores if d != c])[core]) for c in peers)
+
+    def send(tr, sem, n, rd, lands, lat, wire=0.0):
+        add("g", "send", rd, lands, 0.3, lat, wire, sem=sem, n=n, tr=tr)
 
     def exchange(sem, src_of, dst_of, rd, lands, lat, wire=0.0):
-        add("g", "send", rd, lands, 0.6, lat, wire, sem=sem, src=src_of, dst=dst_of)
+        send([(c, ln[c], sem, src_of(c), dst_of(c)) for c in peers], sem, arrive, rd, lands, lat, wire)
 
     vv, ss = g.vector, g.scalar
-    PS = T.PS
+    PS, TAB = T.PS, T.TAB
 
     def bank(b, a=0, n=512):
         return PS[:, 512 * b + a:512 * b + a + n]
@@ -164,17 +280,11 @@ def rank_program(g, core, T, topo):
         op("s", lambda: ss.activation(out, a, func, bias=bias, scale=scale), rd, wr, cyc(n))
 
     def pick(q, buf, a, win, off, b, n, rd, key):
-        cut = [0, n // 64 * 2, n // 16] if len(q) == 2 else [0, n // 16]
+        cut = [n // 32 * k // len(q) * 2 for k in range(len(q) + 1)]
         for k, e in enumerate(q):
             (cp if e == "v" else act)(buf[:, a + 16 * cut[k]:a + 16 * cut[k + 1]], win.indirect(off[:, b + cut[k]:b + cut[k + 1]]),
-                                      rd, [key + "ab"[k]], GAT * 16 * (cut[k + 1] - cut[k]))
-        return [key + "ab"[k] for k in range(len(q))]
-
-    def digit(q, out, src, rd, wr, n):
-        if q == "v":
-            ts(out, src, 1.0 / 17, 192.0, A.mult, A.add, rd, wr, n / 2)
-        else:
-            act(out, src, rd, wr, n, bias=192.0, scale=1.0 / 17)
+                                      rd, ["%s.%d" % (key, k)], GAT * 16 * (cut[k + 1] - cut[k]))
+        return ["%s.%d" % (key, k) for k in range(len(q))]
 
     def sel(out, a, pat, cmp, base, mult, rd, wr, n):
         op("g", lambda: g.affine_select(out, a, pat, cmp, 0.0, base, mult), rd, wr, 0.17 + 2 * n * CY)
@@ -184,6 +294,7 @@ def rank_program(g, core, T, topo):
     dma("y", "n1", T.NAT[:, 512:768], T.rw[:], (), ["nat2"], 128, 1024)
     dma("s", "wl", T.WR[0::2, 1:15], T.w[:], (), ["wr0"], 64, 28)
     dma("s", "wl", T.WR[1::2, 0:14], T.w[:], (), ["wr1"], 64, 28)
+    VALK = ["val%d" % k for k in range(VC)]
 
     def load(n):
         if n == "k":
@@ -197,219 +308,341 @@ def rank_program(g, core, T, topo):
         if n in "xz":
             c = slice(0, 2048) if n == "x" else slice(2048, 4096)
             dma("y", n, T.X[:, c], T.x[:, c], (), [n], 128, 4096)
+        if n in "0123":
+            k = int(n)
+            dma(PLAN["valq"], VALK[k], val_at(T, 0, k), T.val[:, V // VC * k:V // VC * (k + 1)], (), [VALK[k]], 128, 2 * V // VC)
     for n in PLAN["first"]:
         load(n)
 
     op("g", lambda: g.iota(T.PI[:, 0:1], [[0, 1]], 0, 1), (), ["PI"], 0.14)
     fill(T.ONES[:], 1.0, ["ONES"], 128)
-    for b in ("MA", "SEL", "EQ"):
-        fill(T[b][:], 0.0, [b])
-    for k, m in enumerate((1, 15, 13)):
+    fill(T.ZB[:, 0:AT["DG2"]], 0.0, ["ZB"], AT["DG2"] / 2)
+
+    def zb(n, a=0, b=128, step=1):
+        return T.ZB[:, AT[n] + a:AT[n] + b:step]
+
+    def zh(n, a=0, b=128):
+        return T.ZH[:, AT[n] + a:AT[n] + b]
+    for k, m in enumerate((1, 15, 13, 3)):
         ts(T.CI[:, k:k + 1], T.PI[:, 0:1], m, None, A.bitwise_and, None, ["PI"], ["CI%d" % k])
-    fill(T.WID[:], 0.0, ["WID"], 288)
-    cp(T.CF[:, 0:3], T.CI[:, 0:3], ["CI0", "CI1", "CI2"], ["CF"])
-    fill(T.NEG[:], -192.0, ["NEG"], 256)
-    ts(T.CF[:, 3:4], T.CF[:, 0:1], 16.0, 1.0, A.mult, A.add, ["CF"], ["C17"])
-    ts(T.CF[:, 4:5], T.CF[:, 0:1], -1.0, 1.0, A.mult, A.add, ["CF"], ["EVN"])
-    ts(T.CF[:, 5:6], T.CF[:, 1:2], 16.0, None, A.mult, None, ["CF"], ["P16"])
+    cp(T.CF[:, 0:4], T.CI[:, 0:4], ["CI0", "CI1", "CI2", "CI3"], ["CF"])
+    ODD, ROW16, KIND, ROW4, C17, EVN, P16, E17, K4, IS2, NEV, NOD, BI0, BIA, R16, RA1, RA2, KX0, KX1, KL0, KT, KU = [
+        T.CF[:, k:k + 1] for k in range(22)]
+    op("g", lambda: g.iota(T.IO[:], [[1, 16]], 0, 0, allow_small_or_imprecise_dtypes=True), (), ["IO"], 0.2)
+    ts(T.E16[:], T.IO[:], ROW16, None, A.is_equal, None, ["IO", "CF"], ["E16"])
+    ts(T.EK[:], T.IO[:], KIND, None, A.is_equal, None, ["IO", "CF"], ["EK"])
+    ts(IS2, ROW4, 2.0, None, A.is_equal, None, ["CF"], ["IS2"])
+    ts(K4, ROW4, float(F), float(BA), A.mult, A.min, ["CF"], ["K4"])
+    R15 = T.E16[:, 15:16]
+
+    def col(out, a, scale, bias, rd, key):
+        act(out, a, rd, [key], 64, scale=scale, bias=bias)
+    col(C17, ODD, 16.0, 1.0, ["CF"], "C17")
+    col(EVN, ODD, -1.0, 1.0, ["CF"], "EVN")
+    col(E17, ODD, -1.0 / 17, 1.0 / 17, ["CF"], "E17")
+    col(NEV, ODD, 1.0, -1.0, ["CF"], "NEV")
+    col(NOD, ODD, -1.0, 0.0, ["CF"], "NOD")
+    col(P16, ROW16, 16.0, 16.0, ["CF"], "P16")
+    col(R16, R15, 16.0, 0.0, ["E16"], "R16")
+    col(BI0, T.E16[:, 3:4], 2048.0, R15, ["E16"], "BI0")
+    col(BIA, T.E16[:, 7:8], 2048.0, BI0, ["BI0"], "BIA")
+    col(RA1, T.EK[:, 9:10], 1.0 / 16, 0.0, ["EK"], "RA1")
+    col(RA2, R15, -BIG, RA1, ["E16", "RA1"], "RA2")
     fill(T.PB[:, 0:16], 0.0, ["PB0"])
+    fill(T.AQ[:, :, 0:16], 1024.0, ["AQ0"])
+    fill(TAB[:, 3 * F:VA], 0.0, ["gap"])
     for k in range(2):
-        fill(T.ADD[:, 1024 * k:1024 * k + 1024], 0.0, ["ADDa%d" % k], 512)
+        act(T.OFF[:, 256 * k:256 * k + 256], T.ONES[:], ["ONES"], ["OFF"], 256, scale=0.0)
+    for b in range(N):
+        act(T.OFF[:, C * b:C * b + 1], T.ONES[:, 0:1], [], ["OFF"], 64, scale=1024.5 - (learner[b] + 1) / 4 + 1.0 / 2048)
+    zero = []
+    for k, q in enumerate(PLAN["zadd"]):
+        zero.append("ADD%d" % k)
+        if q == "v":
+            fill(T.ADD[:, 512 * k:512 * k + 512], 0.0, [zero[-1]], 256)
+        elif q == "g":
+            op("g", lambda k=k: g.iota(T.ADD[:, 512 * k:512 * k + 512], [[0, 512]], 0, 0, allow_small_or_imprecise_dtypes=True), (), [zero[-1]], 1.2)
+        else:
+            for j in range(2):
+                act(T.ADD[:, 512 * k + 256 * j:512 * k + 256 * j + 256], T.ONES[:], ["ONES"], [zero[-1]], 256, scale=0.0)
     sel(T.TMQ[:], T.ONES[:, 0:64], [[-2, 64]], A.is_ge, 0, 1, ["ONES"], ["TMQ"], 64)
     sel(T.PM[:], T.TMQ[:], [[2, 64]], A.is_ge, 1, -1, ["TMQ"], ["PM"], 64)
-    sel(T.SEL[:, 1::2], T.ONES[:, 0:64], [[-1, 8], [-8, 8]], A.is_equal, 0, 1, ["ONES"], ["SEL"], 64)
+    sel(zb("SEL", 1, 128, 2), T.ONES[:, 0:64], [[-1, 8], [-8, 8]], A.is_equal, 0, 1, ["ONES", "ZB"], ["SEL"], 64)
+    op("g", lambda: g.affine_select(zb("SEL", 3, 128, 4), zb("SEL", 3, 128, 4), [[-1, 8], [-16, 4]], A.not_equal, -1.0, 0, 1), (), ["SEL"], 0.25)
+    cp(zh("SEL"), zb("SEL"), ["SEL"], ["SELH"])
     sel(T.ID[:], T.ONES[:, 0:128], [[-1, 128]], A.is_equal, 0, 1, ["ONES"], ["ID"], 128)
     sel(T.TMP[:], T.ONES[:, 0:128], [[-16, 8], [0, 16]], A.is_ge, 0, 1, ["ONES"], ["TMP"], 128)
     sel(T.SAME[:], T.TMP[:], [[16, 8], [0, 16]], A.is_ge, 15, -1, ["TMP"], ["SAME"], 128)
     op("g", lambda: g.iota(T.TJ[:], [[0, N], [256, J // N]], 0, 0, allow_small_or_imprecise_dtypes=True), (), ["TJ"], 0.2)
-    sel(T.INA[:], T.NEG[:], [[-2, N], [0, C]], A.is_ge, 0, 1, ["NEG"], ["INA"], 512)
-    sel(T.IND[:], T.INA[:], [[2, N], [0, C]], A.is_ge, 1, -1, ["INA"], ["IND"], 512)
-    for k in range(8):
-        act(T.ADD[:, 2048 + 256 * k:2304 + 256 * k], T.ONES[:], ["ONES"], ["ADDb%d" % k], 256, scale=0.0)
-    act(T.MA[:, 0::2], T.PM[:], ["PM"], ["MA"], 64)
-    act(T.PK[:], T.MA[:], ["MA", "C17"], ["PK"], 128, scale=T.CF[:, 3:4])
-    act(T.EQ[:, 2 * rank:2 * rank + 1], T.CF[:, 4:5], ["EVN", "EQ"], ["EQ0"], 64)
-    act(T.EQ[:, 2 * rank + 1:2 * rank + 2], T.CF[:, 0:1], ["CF", "EQ"], ["EQ1"], 64)
-    act(T.S256[:], T.SAME[:], ["SAME"], ["S256"], 128, scale=1.0 / 256)
-    for k, (s, cmp) in enumerate(((1, A.is_ge), (-1, A.is_gt), (1, A.is_gt), (-1, A.is_ge))):
-        sel(T.TRI[:, 128 * k:128 * k + 128], T.S256[:], [[s, 128]], cmp, 0, -s, ["S256"], ["tri%d" % k], 128)
-    for k, c in enumerate((BIG, -BIG, 16.0)):
-        act(T.IDS[:, 128 * k:128 * k + 128], T.ID[:], ["ID"], ["ids%d" % k], 128, scale=c)
-    act(T.TBC[:], T.TJ[:], ["TJ", "P16"], ["TBC"], 64, bias=T.CF[:, 5:6])
-    act(T.WID[:, 15:143:16], T.SAME[:, 0::16], ["SAME", "CF", "WID"], ["widt"], 64, scale=T.CF[:, 1:2])
-    act(T.SQ[:], T.SAME[:, 0::16], ["SAME", "CF"], ["SQ"], 64, scale=T.CF[:, 2:3])
-    act(T.TMR[:], T.SAME[:], ["SAME", "CF"], ["TMR"], 128, scale=T.CF[:, 2:3])
-    for k, c in enumerate((13.0, 1.0, 5.0)):
-        ts(T.WID[:, 144 * k + 159:144 * k + 287:16], T.SQ[:], c, None, A.is_equal, None, ["SQ", "WID"], ["wid%d" % k])
-    ts(T.RWS[:], T.TMR[:], 9.0, None, A.is_equal, None, ["TMR"], ["RWS"])
-    cp(T.SAMH[:], T.SAME[:], ["SAME"], ["SAMH"])
+    act(zb("MA", 0, 128, 2), T.PM[:], ["PM", "ZB"], ["MA"], 64)
+    act(T.PK[:], zb("MA"), ["MA", "C17"], ["PK"], 128, scale=C17)
+    G0 = T.SAME[:, 0::16]
 
-    cp(T.HI[:, 0:512], T.NAT[:, 0:512], ["nat0", "nat1"], ["HIa"], 512)
-    ts(T.RY[:], T.NAT[:, 512:768], 6144.0, None, A.add, None, ["nat2"], ["RY"], 256)
-    tt(T.LO[:, 0:512], T.NAT[:, 0:512], T.HI[:, 0:512], A.subtract, ["nat0", "nat1", "HIa"], ["LOa"], 1024)
-    ts(T.HI[:, 512:768], T.RY[:], -6144.0, None, A.add, None, ["RY"], ["HIb"], 128)
-    tt(T.LO[:, 512:768], T.NAT[:, 512:768], T.HI[:, 512:768], A.subtract, ["nat2", "HIb"], ["LOb"], 512)
+    def mark(n, a, scale, rd, key):
+        act(zb(n, a, min(a + 128, dict(MATS)[n]), 16), G0, ["SAME", "ZB"] + rd, [key], 64, scale=scale)
+    mark("EQ", 1, NEV, ["NEV"], "EQ0")
+    mark("EQ", 3, NOD, ["NOD"], "EQ1")
+    act(T.S1K[:], T.SAME[:], ["SAME"], ["S1K"], 128, scale=1.0 / 1024)
+    for k, (s, cmp) in enumerate(((1, A.is_ge), (-1, A.is_gt))):
+        sel(T.TRI[:, 128 * k:128 * k + 128], T.S1K[:], [[s, 128]], cmp, 0, -s, ["S1K"], ["tri%d" % k], 128)
+    sel(T.SUP[:], T.SAME[:], [[1, 128]], A.is_equal, -1, -1, ["SAME"], ["SUP"], 128)
+    act(T.TBC[:], T.TJ[:], ["TJ", "P16"], ["TBC"], 64, bias=P16)
+    for n, a in (("WN", 15), ("WA1", 14), ("WA4", 11)):
+        mark(n, a, -1.0, [], n + "n")
+    for n in ("WP", "WA1", "WA4"):
+        mark(n, 15, R16, ["R16"], n + "p")
+    cp(zh("WA1", 0, 576), zb("WA1", 0, 576), ["WNn", "WA1n", "WA4n", "WPp", "WA1p", "WA4p"], ["WH"], 288)
+    mark("WK", 15, T.EK[:, 13:14], ["EK"], "WK")
+    for n, kinds in (("W4X", (1, 5, None, 1)), ("W4L", (1, 5, 13, 1))):
+        if n[2].lower() in PLAN["mode"]:
+            for k, c in enumerate(kinds):
+                if c:
+                    mark(n, 12 + k, T.EK[:, c:c + 1], ["EK"], n)
+    tt(T.DGB[:], T.ID[:], T.SUP[:], A.subtract, ["ID", "SUP"], ["DGB"], 256)
+    act(zb("DG1"), T.DGB[:], ["DGB"], ["DG1"], 128, scale=2 * BIG)
+    act(zb("DG2"), zb("WP", 15, 143), ["WPp"], ["DG2"], 128, scale=-BIG / 8)
+    act(zb("SAMH"), T.SAME[:], ["SAME"], ["SAMH"], 128, scale=1.0 / 16)
+    cp(zh("DG2", 0, 384), zb("DG2", 0, 384), ["DG1", "DG2", "SAMH"], ["DH"], 192)
+    act(T.RW1[:], T.SAME[:], ["SAME", "RA1"], ["RW1"], 128, scale=RA1)
+    act(T.RW2[:], T.SAME[:], ["SAME", "RA2"], ["RW2"], 128, scale=RA2)
+    if "x" in PLAN["mode"]:
+        op("g", lambda: g.iota(T.TJ4[:], [[0, N], [64, 32]], 16, 0, allow_small_or_imprecise_dtypes=True), (), ["TJ4"], 0.4)
+        col(KT, ROW16, 4.0, -8.0, ["CF"], "KT")
+        col(KU, KT, IS2, 0.0, ["KT", "IS2"], "KU")
+        act(T.K4X[:], T.TJ4[:], ["TJ4", "KU"], ["K4X"], 128, scale=IS2, bias=KU)
+        for h, a in enumerate((KX0, KX1)):
+            col(a, IS2, float(TB - BA + F // H * h), K4, ["IS2", "K4"], "KX%d" % h)
+    if "l" in PLAN["mode"]:
+        col(KL0, IS2, float(VA - BA - 1), K4, ["IS2", "K4"], "KL0")
+        op("g", lambda: g.iota(T.TJL[:], [[V, N], [0, 32]], 0, 0, allow_small_or_imprecise_dtypes=True), (), ["TJL"], 0.4)
+        act(T.K4L[:], T.TJL[:], ["TJL", "IS2"], ["K4L"], 128, scale=IS2)
+
+    MAGIC = 1.5 * 2 ** 28
+    ts(T.PH[:, 0:512], T.NAT[:, 0:512], MAGIC, -MAGIC, A.add, A.add, ["nat0", "nat1"], ["PHa"], 512)
+    ts(T.PV[:, 0:512], T.NAT[:, 0:512], -2048.0, None, A.add, None, ["nat0", "nat1"], ["PVa"], 512)
+    ts(T.PH[:, 512:768], T.NAT[:, 512:768], MAGIC, -MAGIC, A.add, A.add, ["nat2"], ["PHb"], 256)
+    cp(T.PV[:, 512:768], T.NAT[:, 512:768], ["nat2"], ["PVb"], 256)
     for r in (0, 2, 1, 3, 4, 5):
-        src, key = ((T.HI, "HI"), (T.LO, "LO"))[r % 2]
-        k = r // 2
-        dma("y", "pt", T.PT[8 * r:8 * r + 8, :], src[:, 256 * k:256 * k + 256], [key + "aab"[k]], ["pt%d" % r], 128, 512)
+        n, k = ("PH", "PV")[r % 2], r // 2
+        dma("y", "pt", T.PT[8 * r:8 * r + 8, :], T[n][:, 256 * k:256 * k + 256], [n + "aab"[k]], ["pt%d" % r], 128, 512)
     for n in PLAN["then"]:
         load(n)
-    cp(T.HI[:, 768:1024], T.NAT[:, 768:1024], ["nat3"], ["HIc"], 256)
-    tt(T.LO[:, 768:1024], T.NAT[:, 768:1024], T.HI[:, 768:1024], A.subtract, ["nat3", "HIc"], ["LOc"], 512)
-    zero = ["ADDa0", "ADDa1"] + ["ADDb%d" % k for k in range(8)]
-    for r in range(4, 8):
-        src, key = ((T.HI, "HI"), (T.LO, "LO"))[r % 2]
-        k = r // 2
-        dma("y", "add", T.ADD[2 * r + 1::16, :], src[:, 256 * k:256 * k + 256], [key + "aabc"[k]] + zero, ["add%d" % r], 128, 512)
-    VALK = ["val%d" % k for k in range(4)]
+    ts(T.HI[:], T.NAT[:, 512:1024], MAGIC, -MAGIC, A.add, A.add, ["nat2", "nat3"], ["HI"], 512)
+    tt(T.LO[:], T.NAT[:, 512:1024], T.HI[:], A.subtract, ["nat2", "nat3", "HI"], ["LO"], 1024)
+    for r in range(4):
+        n, k = ("HI", "LO")[r % 2], r // 2
+        dma("y", "add", T.ADD[2 * r + 9::16, :], T[n][:, 256 * k:256 * k + 256], [n] + zero, ["add%d" % r], 128, 512)
+    ADDK = zero + ["add%d" % r for r in range(4)]
+    for n in PLAN["vat"][0]:
+        load(n)
 
-    def load_val(k):
-        dma("y", VALK[k], T.VAL[:, 2048 * k:2048 * k + 2048], T.val[:, 2048 * k:2048 * k + 2048], (), [VALK[k]], 128, 4096)
-
-    L0 = rank * LW
-    cp(T.WC[:, 1:14], T.WR[:, 1:14], ["wr0", "wr1"], ["WC"])
-    ts(T.WD[:, 0:2], T.WC[:, 5:13:7], T.CF[:, 4:5], None, A.mult, None, ["WC", "EVN"], ["WD"])
+    act(T.WC[:, 1:14], T.WR[:, 1:14], ["wr0", "wr1"], ["WC"], 64)
+    act(T.WD[:, 0:2], T.WC[:, 5:13:7], ["WC", "EVN"], ["WD"], 64, scale=EVN)
     cols = [(T.WD[:, 0:1], T.WD[:, 1:2])] + [(T.WC[:, a:a + 1], T.WC[:, a + 7:a + 8]) for a in (3, 6, 1)]
     for t in range(4):
-        act(T.LALL[:, L0 + 128 * t:L0 + 128 * t + 128], T.MA[:], ["MA", "WD"], ["la%d" % t], 128, scale=cols[t][0])
+        act(T.LALL[:, 128 * t:128 * t + 128], zb("MA"), ["MA", "WD"], ["la%d" % t], 128, scale=cols[t][0])
     for t in range(4):
-        act(T.LALL[:, L0 + 513 + 128 * t:L0 + 640 + 128 * t:2], T.PM[:], ["PM", "WD"], ["lo%d" % t], 64, scale=cols[t][1])
-    act(T.LALL[:, L0 + 512:L0 + 1024:2], T.LALL[:, L0:L0 + 512:2], ["la%d" % t for t in range(4)], ["le"], 256, scale=-17.0)
-    own = ["la%d" % t for t in range(4)] + ["lo%d" % t for t in range(4)] + ["le", "lb"]
-    mm([(bank(7, 0, 128), T.EQ[:], T.LALL[:, L0 + 512 + 128 * t:L0 + 640 + 128 * t], t == 0, t == 3) for t in range(4)],
-       ["EQ0", "EQ1"] + own[4:9], ["B7"], 128)
-    act(T.LALL[:, L0 + 1024:L0 + LW], bank(7, 0, 128), (), ["B7", "lb"], 128)
+        act(T.LALL[:, 513 + 128 * t:640 + 128 * t:2], T.PM[:], ["PM", "WD"], ["lo%d" % t], 64, scale=cols[t][1])
+    act(T.LALL[:, 512:1024:2], T.LALL[:, 0:512:2], ["la%d" % t for t in range(4)], ["le"], 256, scale=-17.0)
+    mm([(bank(7, 0, 128), zb("EQ"), T.LALL[:, 512 + 128 * t:640 + 128 * t], t == 0, False) for t in range(4)]
+       + [(bank(7, 0, 128), T.ID[:], T.LALL[:, 512:640], False, True)],
+       ["EQ0", "EQ1", "ID", "le"] + ["lo%d" % t for t in range(4)], ["B7"], 128)
+    act(T.LALL[:, 512:640], bank(7, 0, 128), (), ["B7", "lo0", "le"], 128)
+    own = ["la%d" % t for t in range(4)] + ["lo%d" % t for t in range(4)] + ["le"]
     PTK = ["pt%d" % r for r in range(6)]
-    exchange("la", lambda c: T.LALL[:, L0:L0 + LW], lambda c: T.LALL[:, L0:L0 + LW], own, ["lpeer"], PLAN["llat"], 3.5)
+    exchange("la", lambda c: T.LALL[:, 0:LW], lambda c: T.LALL[:, LW * block(cores, c, core):LW * (block(cores, c, core) + 1)],
+             own, ["lpeer"], PLAN["llat"], 3.0)
+    ops[-1]["lead"] = PLAN["lfirst"]
 
-    cp(T.LTF[:], T.LTI[:], ["lti%d" % k for k in range(4)], ["LTF"], 512)
+    def send_val(k, rd):
+        mine, near = helpers(topo, cores)[core], direct(topo, cores, core)
+        e = topo.engines(core, mine)
+        total = sum(VC * len(e) // (2 if core in direct(topo, cores, c) else 1) for c in peers)
+        tr = [(mine, e[0::2] if near else e, "rv%d" % k, val_at(T, 0, k), val_at(T, 0, k))]
+        tr += [(c, e[1::2], "vall", val_at(T, 0, k), val_at(T, block(cores, c, core), k)) for c in near]
+        send(tr, "vall", total, [VALK[k]] + ["sent%d" % (k - 1)] * (k > 0) + rd, ["sent%d" % k],
+             PLAN["vlat"] * (k == VC - 1), 8 * len(tr) * (ROW + 2 * V / VC / BW))
+        ops[-1]["chain"] = k < VC - 1
+    VALL = VALK + ["sent%d" % (VC - 1)]
+
+    ts(T.LTF[:], T.LTI[:], -2048.0, None, A.add, None, ["lti%d" % k for k in range(4)], ["LTF"], 512)
     for b in range(8):
         op("v", lambda b=b: vv.transpose(T.WF[:, b::8], T.LTF[:, :, b, :]), ["LTF"], ["wf%d" % b], cyc(64))
-    cp(T.WL[:], T.WF[:], ["wf%d" % b for b in range(8)], ["WL"], 512)
+    ts(T.WL[:], T.WF[:], 2048.0, None, A.add, None, ["wf%d" % b for b in range(8)], ["WL"], 256)
 
-    def lists(h, k, src, out, b, rd, wr, first=()):
-        it = list(first)
-        for i in range(16):
-            it.append((bank(b, 0, J), T.WID[:, 144 * k + 15 - i:144 * k + 143 - i], src[:, S * h + i:S * h + S:16], not it, i == 15))
-        mm(it, rd, ["B%d" % b], J)
-        cp(out, bank(b, 0, J), (), ["B%d" % b, wr])
+    def counts(h, a, step, b0=0, b1=N):
+        return T.AQ[:, b0:b1, 16 + C * h + a:16 + C * h + C + min(a, 0):step]
+
+    def AK(h):
+        return ["a%d%d" % (h, b) for b in range(N)] + (["AQ0"] if h == 0 else ["a%d%d" % (h - 1, b) for b in range(N)])
 
     def find(h):
-        n, W0, W1 = C * h + C, 4 * h, 4 * h + 1
-        for j, b in enumerate((W0, W1)):
-            mm([(bank(b, 0, n), T.TRI[:, 256 * j:256 * j + 128], T.PB[:, 16:16 + n], True, False),
-                (bank(b, 0, n), T.TRI[:, 256 * j + 128:256 * j + 256], T.PB[:, 15:15 + n], False, True)],
-               ["P%d" % k for k in range(h + 1)] + ["PB0", "tri%d" % (2 * j), "tri%d" % (2 * j + 1)], ["B%d" % b], n)
-            a = 512 * h + 256 * j
-            op("v", lambda a=a, b=b: vv.tensor_tensor_scan(T.CS[:, a:a + n], T.ONES[:, 0:n], bank(b, 0, n), 1032.0 - 127.5 / 256,
-                                                         A.mult, A.add), ["ONES"], ["B%d" % b, "cs%d%d" % (h, j)], cyc(n))
-        c = slice(C * h, n)
-        a = 512 * h + C * h
-        tt(T.SI[:, c], T.CS[:, a:a + C], T.CS[:, a + 256:a + 256 + C], A.add, ["cs%d0" % h, "cs%d1" % h], ["SI%d" % h], 2 * C)
-        ts(T.SA[:, c], T.SI[:, c], 7, None, A.bitwise_and, None, ["SI%d" % h], ["SA%d" % h], C)
-        cp(T.CB[:, c], T.SA[:, c], ["SA%d" % h], ["CB%d" % h], C)
-        for q in range(N):
-            a = S * h + C * q
-            ts(T.O[:, a:a + C], T.CB[:, c], float(2 * q + 1), None, A.is_equal, None, ["CB%d" % h], ["o%d%d" % (h, q)], C / 2)
-        lists(h, 0, T.O, T.LT[:, J * h:J * h + J], W0, ["o%d%d" % (h, q) for q in range(N)] + ["widt", "TBC", "ID"], "LT%d" % h,
-              [(bank(W0, 0, J), T.ID[:], T.TBC[:], True, False)])
+        W0, W1 = 4 * h, 4 * h + 1
+        a = 16 + C * h
+        mm([(bank(W0, 0, C), T.TRI[:, 0:128], T.PB[:, a:a + C], True, False),
+            (bank(W0, 0, C), T.TRI[:, 128:256], T.PB[:, a - 1:a - 1 + C], False, True)],
+           ["P%d" % h, "P%d" % (h - 1) if h else "PB0", "tri0", "tri1"], ["B%d" % W0], C)
+        for b in range(N):
+            op("v", lambda b=b: vv.tensor_tensor_scan(T.AQ[:, b, a:a + C], T.OFF[:, C * b:C * b + C], bank(W0, 0, C),
+                                                      T.CAR[:, 0:1] if h else 0.0, A.add, A.add),
+               ["OFF"] + ["CAR"] * h, ["B%d" % W0, "a%d%d" % (h, b)], cyc(C))
+        if h == 0:
+            op("v", lambda: vv.tensor_reduce(T.CAR[:, 0:1], bank(W0, 0, C), AX.X, A.add), (), ["B%d" % W0, "CAR"], cyc(C))
+        out = bank(W1, 0, J)
+        mm([(out, T.ID[:], T.TBC[:], True, False)], ["ID", "TBC"], ["B%d" % W1], J)
+        mm([(out, zh("WA1", 14 - i, 142 - i), counts(h, i, 16), False, False) for i in range(15)]
+           + [(out, zh("WN"), counts(h, 15, 16), False, False), (out, zh("WP", 15, 143), counts(h, -1, 16), False, True)],
+           AK(h) + ["WH"], ["B%d" % W1], J)
+        ts(T.LT[:, J * h:J * h + J], out, float(F // H - 1), None, A.min, None, (), ["B%d" % W1, "LT%d" % h])
 
     for h in range(H):
         cp(T.PB[:, 16 + C * h:16 + C * h + C], T.PRI[:, C * h:C * h + C], ["PRI"], ["P%d" % h], C)
-    for h in range(H):
+    for h in range(PLAN["find0"]):
         find(h)
 
-    for b in range(8):
-        mm([(bank(b), T.PK[:], T.X[:, 512 * b:512 * b + 512], True, False)], ["PK", "xz"[b // 4]], ["B%d" % b], 512)
-    for b in range(8):
-        mm([(bank(b), T.SEL[0:48, :], T.PT[0:48, 512 * b:512 * b + 512], False, True)], ["SEL"] + PTK, ["B%d" % b], 512)
-    for b in range(8):
-        (act if b < PLAN["evac"] else cp)(T.BASE[:, 512 * b:512 * b + 512], bank(b), (), ["B%d" % b, "base%d" % b], 512)
+    def ask(rd_, h, src, rd, less):
+        e, W0, Jq = rd_ * H + h, 4 * h, J // N
+        K0, V0 = 7 * Jq * e, 7 * C * e
+        mm([(bank(W0, 0, J), zb("WK", 15 - i, 143 - i), src[:, S * h + i:S * h + S:16], i == 0, i == 15) for i in range(16)],
+           rd + ["WK"], ["B%d" % W0], J)
+        ts(T.KL[:, K0 + 3 * Jq:K0 + 7 * Jq], bank(W0, 0, J), -less, None, A.add, None, (), ["B%d" % W0, "KL%d" % e])
+        exchange("ka%d_%d" % (rd_, h), lambda d: T.KL[:, K0 + Jq * (3 + block(cores, core, d)):K0 + Jq * (4 + block(cores, core, d))],
+                 lambda d: T.KL[:, K0 + Jq * (block(cores, d, core) - 1):K0 + Jq * block(cores, d, core)], ["KL%d" % e], ["KIN%d" % e], HOP)
+        vo = pick(PLAN["vo"], T.VG, V0, TAB[:, VA:VA + V], T.KL, K0, S, VALK + ["KIN%d" % e, "KL%d" % e], "VO%d" % e)
+        exchange("va%d_%d" % (rd_, h), lambda d: T.VG[:, V0 + C * (block(cores, core, d) - 1):V0 + C * block(cores, core, d)],
+                 lambda d: T.VG[:, V0 + C * (3 + block(cores, d, core)):V0 + C * (4 + block(cores, d, core))], vo, ["VG%d" % e], HOP + 0.3)
+        return lambda b0, b1: T.VG[:, V0 + (3 + b0) * C:V0 + (3 + b1) * C], vo + ["VG%d" % e]
+
+    line[0] = "vsp"
+    banks, ahead = ((2, 3, 6, 7, 0, 4, 1, 5), 4) if PLAN["find0"] else (range(8), 8)
+
+    def pack(k):
+        mm([(bank(banks[k]), T.PK[:], T.X[:, 512 * k:512 * k + 512], True, False)], ["PK", "xz"[k // 4]], ["B%d" % banks[k]], 512)
+    for k in range(ahead):
+        pack(k)
+    for k, b in enumerate(banks):
+        mm([(bank(b), T.ZH[0:48, AT["SEL"]:AT["SEL"] + 128], T.PT[0:48, 512 * k:512 * k + 512], False, True)], ["SELH"] + PTK, ["B%d" % b], 512)
+        if k + ahead < 8:
+            pack(k + ahead)
+        out = TAB[:, BA + 512 * k:BA + 512 * k + 512]
+        if PLAN["evac"][k] == "s":
+            act(out, bank(b), ["BIA"], ["B%d" % b, "base%d" % k], 512, bias=BIA)
+        else:
+            ts(out, bank(b), BIA, None, A.add, None, ["BIA"], ["B%d" % b, "base%d" % k], 512)
     BK = ["base%d" % b for b in range(8)]
+    BASE = TAB[:, BA:BA + F]
 
     for k in range(4):
-        c = slice(1024 * k, 1024 * k + 1024)
-        tt(T.CT[:, c], T.BASE[:, 0:F].indirect(T.WL[:, 64 * k:64 * k + 64]), T.ADD[:, c], A.add,
-           BK + ["WL"] + zero + ["add%d" % r for r in range(4, 8)], ["ce%d" % k, "cp%d" % k], GAT * 1024)
-        act(T.TB[:, c], T.BASE[:, 0:F].indirect(T.WL[:, 256 + 64 * k:320 + 64 * k]), BK + ["WL"], ["tbe%d" % k, "tbo%d" % k], GAT * 1024)
-    for k in range(PLAN["early"]):
-        load_val(k)
-    dma("y", "ta", T.TA[0::2, :], T.BASE[0::2, :], BK, ["ta"], 64, 8192)
-    for k in range(4 + PLAN["lag"]):
-        c = slice(1024 * k, 1024 * k + 1024)
-        if k < 4:
-            for r in (5, 7):
-                dma("y", "pp%d" % k, T.CT[r::16, c], T.TB[r::16, c], ["tbo%d" % k, "cp%d" % k], ["cq%d_%d" % (k, r)], 16, 1024)
-        b = k - PLAN["lag"]
-        if b >= 0:
-            d = slice(1024 * b, 1024 * b + 1024)
-            dma("y", "tb%d" % b, T.TB[1::2, d], T.BASE[0::2, d], BK, ["tbo%d" % b], 64, 2048)
-        if k < 4:
-            dma("y", "ta", T.TA[1::2, c], T.CT[0::2, c], ["ce%d" % k], ["tao%d" % k], 64, 2048)
-        if k == PLAN["late"]:
-            for b in range(PLAN["early"], 4):
-                load_val(b)
+        a = 1024 * k
+        tt(T.CT[:, a:a + 1024], BASE.indirect(T.WL[:, 64 * k:64 * k + 64]), T.ADD[:, a:a + 1024], A.add,
+           BK + ["WL"] + ADDK, ["ce%d" % k, "cp%d" % k], GAT * 1024)
+        act(T.X[:, a:a + 1024], BASE.indirect(T.WL[:, 256 + 64 * k:320 + 64 * k]), BK + ["WL"], ["xz"[k // 2], "xb%d" % k], GAT * 1024)
+    for h in range(PLAN["find0"], H):
+        find(h)
+    line[0] = ""
+    dma("y", "ta", TAB[0::2, TA:TA + F], TAB[0::2, BA:BA + F], BK, ["ta"], 64, 8192)
+    dma("y", "ta", TAB[1::2, TB:TB + F], TAB[0::2, BA:BA + F], BK, ["tbo%d" % k for k in range(4)], 64, 8192)
+    for n in PLAN["vat"][1]:
+        load(n)
+    for k in range(4):
+        a = 1024 * k
+        for r in (5, 7):
+            dma("y", "pp%d" % k, T.CT[r::16, a:a + 1024], T.X[r::16, a:a + 1024], ["xb%d" % k, "cp%d" % k], ["cq%d_%d" % (k, r)], 16, 1024)
+        dma("y", "ta", TAB[1::2, TA + a:TA + a + 1024], T.CT[0::2, a:a + 1024], ["ce%d" % k], ["tao%d" % k], 64, 2048)
+        dma("y", "ta", TAB[0::2, TB + a:TB + a + 1024], T.X[0::2, a:a + 1024], ["xb%d" % k], ["tbe%d" % k], 64, 2048)
+    for n in PLAN["vat"][2]:
+        load(n)
+    early = {}
+    if PLAN["mode"][0] == "x" and PLAN["gk"]:
+        for h in range(H):
+            gk = pick(PLAN["gk"], T.GK, S * h, T.ADD[:, F // H * h:F // H * (h + 1)], T.LT, J * h, S,
+                      ADDK + ["LT%d" % h, PLAN["gkafter"]], "GK%d" % h)
+            early[h] = ask(0, h, T.GK, gk, 0.0)
+    for k in range(VC if "l" in PLAN["mode"] else 0):
+        send_val(k, PLAN["vafter"][k])
     TBK = [n % k for k in range(4) for n in ("tbe%d", "tbo%d")]
-    TAK = ["ta"] + ["tao%d" % k for k in range(4)]
-    mm([(bank(3, 0, 128), T.ID[:], T.LALL[:, q * LW + 1024:q * LW + LW], q == 0, q == N - 1) for q in range(N)],
-       ["ID", "lb", "lpeer"], ["B3"], 128)
-    act(T.LBX[:], bank(3, 0, 128), (), ["B3", "LBX"], 128)
+    TABK = BK + TBK + ["ta"] + ["tao%d" % k for k in range(4)]
 
     def judge(rd_, h):
-        W0, W1, HB, EB = 4 * h, 4 * h + 1, 4 * h + 2, 4 * h + 3
-        s, j, c = slice(S * h, S * h + S), slice(J * h, J * h + J), slice(C * h, C * h + C)
+        local = PLAN["mode"][rd_] == "l"
+        W1, HB, EB = 4 * h + 1, 4 * h + 2, 4 * h + 3
+        s, c = slice(S * h, S * h + S), slice(C * h, C * h + C)
         k_ = lambda n: "%s%d" % (n, h)
         B = lambda b: "B%d" % b
         chunks = range(4 // H * h, 4 // H * (h + 1))
-        win = slice(F // H * h, F // H * (h + 1))
-        OK = ["o%d%d" % (h, q) for q in range(N)]
 
-        def term(t, half, src, rd, stop=False):
-            a = 512 * half + 128 * t
-            mm([(bank(HB, C * q, C), T.LALL[:, q * LW + a:q * LW + a + 128], src[:, S * h + C * q:S * h + C * q + C], False,
-                 stop and q == N - 1) for q in range(N)], rd + own + ["lpeer"], [B(HB)], C)
+        def part(buf, b0, b1, k=None):
+            a, b = S * h + C * b0, S * h + C * b1
+            return buf[:, a:b] if k is None else buf[:, 4 * a:4 * b] if k == "all" else buf[:, 4 * a + k:4 * b:4]
 
-        GK = {"C": pick(PLAN["gc"], T.GC, S * h, T.CT[:, win], T.LT, J * h, S,
-                        [n % k for k in chunks for n in ("ce%d", "cq%d_5", "cq%d_7")] + [k_("LT")], k_("GC"))}
-        e = rd_ * H + h
-        K0, I0, O0, G0, Jq = J * e, 3 * J // N * e, 3 * C * e, S * e, J // N
-        lists(h, 1, T.GC, T.KL[:, K0:K0 + J], W1, GK["C"] + ["wid0"], "KL%d" % e)
+        def terms(items, b0, b1, rd):
+            acc(("h", rd_, h), [(bank(HB, C * b, C), T.LALL[:, b * LW + 512 * d + 128 * t:b * LW + 512 * d + 128 * t + 128], part(buf, b, b + 1, k))
+                                for b in range(b0, b1) for t, d, buf, k in items], rd + own + ["lpeer"] * (b1 > 1), HB, C)
 
-        def slot(d):
-            return [a for a in cores if a != d].index(core)
-        exchange("ka%d_%d" % (rd_, h), lambda d: T.KL[:, K0 + Jq * T.rank_of(d):K0 + Jq * T.rank_of(d) + Jq],
-                 lambda d: T.KIN[:, I0 + Jq * slot(d):I0 + Jq * slot(d) + Jq], ["KL%d" % e], ["KIN%d" % e], HOP - 0.6 + 32 * ROW)
-        vo = pick(PLAN["vo"], T.VO, O0, T.VAL[:, 0:V], T.KIN, I0, 3 * C, VALK + ["KIN%d" % e], "VO%d" % e)
-        exchange("va%d_%d" % (rd_, h), lambda d: T.VO[:, O0 + C * peers.index(d):O0 + C * peers.index(d) + C],
-                 lambda d: T.VG[:, G0 + C * rank:G0 + C * rank + C], vo, ["VG%d" % e], HOP - 0.6 + 32 * (ROW + 2 * C / BW))
-        VK = pick(PLAN["vown"], T.VG, G0 + C * rank, T.VAL[:, 0:V], T.KL, K0 + Jq * rank, C, VALK + ["KL%d" % e], "vown%d" % e) + ["VG%d" % e]
-        lists(h, 2, T.GC, T.LN[:, j], W0, GK["C"] + ["wid1"], k_("LN"))
-        lists(h, 3, T.GC, T.LP[:, j], W1, GK["C"] + ["wid2"], k_("LP"))
-        GK["B"] = pick(PLAN["gb"], T.GB, S * h, T.TB[:, win], T.LT, J * h, S,
-                       [n % k for k in chunks for n in ("tbe%d", "tbo%d")] + [k_("LT")], k_("GB"))
-        GK["A"] = pick(PLAN["ga"], T.GA, S * h, T.TA[:, 0:F], T.LN, J * h, S, TAK + [k_("LN")], k_("GA"))
-        GK["P"] = pick(PLAN["gp"], T.GP, S * h, T.TB[:, 0:F], T.LP, J * h, S, TBK + [k_("LP")], k_("GP"))
-        tt(T.GR[:, s], T.BASE[:, 0:F].indirect(T.LN[:, j]), T.GC[:, s], A.add, BK + GK["C"] + [k_("LN")], [k_("GR")], GAT * S)
-        mm([(bank(HB), T.LBX[:], T.IND[:], True, False)], ["LBX", "IND"], [B(HB)], S)
-        for t, n in enumerate("CBAP"):
-            digit(PLAN["r" + n.lower()], T["R" + n][:, s], T["G" + n][:, s], GK[n], [k_("R" + n)], S)
-            term(t, 0, T["G" + n], GK[n])
-            term(t, 1, T["R" + n], [k_("R" + n)], t == 3)
-        mm([(bank(EB), T.IDS[:, 0:128], T.O[:, s], True, False)], OK + ["ids0"], [B(EB)], S)
-        mm([(bank(EB), T.RWS[:], T.GR[:, s], False, False)], [k_("GR"), "RWS"], [B(EB)], S)
+        def digit(q, out, src, mul, rd, key, n):
+            if q == "s":
+                act(out, src, rd, [key], n, scale=mul, bias=192.0)
+            else:
+                ts(out, src, mul, 192.0, A.mult, A.add, rd, [key], n / 2)
+            return [key]
+
+        gc = pick(PLAN["gc"], T.GC, S * h, T.CT[:, F // H * h:F // H * (h + 1)], T.LT, J * h, S,
+                  [n % k for k in chunks for n in ("ce%d", "cq%d_5", "cq%d_7")] + [k_("LT")], k_("GC"))
+        if not local:
+            vg, vk = early[h] if rd_ == 0 and early else ask(rd_, h, T.GC, gc, 1.0)
+        out = bank(W1, 0, C)
+        if local:
+            mm([(out, T.ID[:], T.K4L[:], True, False)], ["ID", "K4L"], [B(W1)], C)
+        else:
+            mm([(out, T.ID[:], T.K4X[:], True, False)], ["ID", "K4X"], [B(W1)], C)
+            mm([(out, zh("WA4", 9 - 4 * i, 137 - 4 * i), counts(h, i, 4), False, False) for i in range(3)]
+               + [(out, zh("WN", 1, 129), counts(h, 3, 4), False, False), (out, zh("WP", 13, 141), counts(h, -1, 4), False, False)],
+               AK(h) + ["WH"], [B(W1)], C)
+        W4 = "W4L" if local else "W4X"
+        mm([(out, zb(W4, 12 - 4 * i, 140 - 4 * i), T.GC[:, S * h + i:S * h + S:4], False, i == 3) for i in range(4)], gc + [W4], [B(W1)], C)
+        ts(T.L4[:, C * h:C * h + C], out, KL0 if local else (KX0, KX1)[h], None, A.add, None, ["KL0" if local else k_("KX")], [B(W1), k_("L4")], C)
+        who, dig = PLAN["g4" if local else "g4x"], PLAN["dig" if local else "digx"]
+        n, g4 = S // len(who), []
+        for k, e in enumerate(who):
+            a = S * h + n * k
+            g4.append("G4%d.%d" % (h, k))
+            (cp if e == "v" else act)(T.G4[:, 4 * a:4 * (a + n)], TAB[:, 0:VA + N * V if local else VA].indirect(T.L4[:, a // 4:(a + n) // 4]),
+                                      TABK + ["gap", k_("L4")] + (VALL if local else []), [g4[k]], GAT * 4 * n)
+        terms([(0, 0, T.GC, None)], 0, N, gc)
+        terms([(0, 1, T.RC, None)], 0, N, digit(dig[0], T.RC[:, s], T.GC[:, s], E17, gc + ["E17"], k_("RC"), S))
+        kinds = [(2, 0), (3, 1)] + ([] if local else [(1, 2)])
+        if local:
+            vg, vk = lambda b0, b1: part(T.G4, b0, b1, 2), g4
+            gb = pick(PLAN["gb"], T.GB, S * h, TAB[:, TB + F // H * h:TB + F // H * (h + 1)], T.LT, J * h, S,
+                      [n % k for k in chunks for n in ("tbe%d", "tbo%d")] + [k_("LT")], k_("GB"))
+            terms([(1, 0, T.GB, None)], 0, N, gb)
+            terms([(1, 1, T.RB, None)], 0, N, digit(dig[1], T.RB[:, s], T.GB[:, s], 1.0 / 17, gb, k_("RB"), S))
+        m = N // len(dig[2:])
+        for k, e in enumerate(dig[2:]):
+            b0, b1 = m * k, m * k + m
+            rd = g4[C * b0 // n:(C * b1 - 1) // n + 1]
+            terms([(t, 0, T.G4, j) for t, j in kinds], b0, b1, rd)
+            if PLAN["flat"]:
+                terms([(t, 1, T.R4, j) for t, j in kinds], b0, b1,
+                      digit(e, part(T.R4, b0, b1, "all"), part(T.G4, b0, b1, "all"), 1.0 / 17, rd, "R4%d.%d" % (h, k), C * m * 4))
+            else:
+                for t, j in kinds:
+                    terms([(t, 1, T.R4, j)], b0, b1,
+                          digit(e, part(T.R4, b0, b1, j), part(T.G4, b0, b1, j), 1.0 / 17, rd, "R4%d.%d.%d" % (h, k, j), C * m))
         P1 = T.PB[:, 16 + C * h:16 + C * h + C]
-        mm([(bank(W0, 0, C), T.IDS[:, 256:384], P1, True, False)]
-           + [(bank(W0, 0, C), T.IDS[:, 128:256], T.O[:, S * h + C * q:S * h + C * q + C], False, q == N - 1) for q in range(N)],
-           OK + [k_("P"), "ids1", "ids2"], [B(W0)], C)
-        act(T.C5[:, c], bank(W0, 0, C), (), [B(W0), k_("C5")], C, bias=BIG)
-        tt(T.PR[:, s], bank(HB), T.VG[:, G0:G0 + S], A.mult, VK, [B(HB), k_("PR")], S)
-        mm([(bank(EB), T.SAMH[:], T.PR[:, s], False, True)], ["SAMH", k_("PR")], [B(EB)], S)
-        for q in range(N):
-            a = S * h + C * q
-            prev, pk = (T.C5[:, c], k_("C5")) if q == 0 else (T.M[:, a - C:a], "m%d%d" % (h, q - 1))
-            tt(T.M[:, a:a + C], bank(EB, C * q, C), prev, A.max, [pk], [B(EB), "m%d%d" % (h, q)], C)
-        act(T.AB[:, c], T.M[:, S * h + S - C:S * h + S], ["m%d3" % h], [k_("AB")], C, func=AF.Abs, bias=-BIG / 16, scale=1.0 / 16)
+        for b0, b1, eb in ((0, 1, 4 * h), (1, N, EB)) if PLAN["split"] else ((0, N, EB),):
+            err, out, n, dg = ("e", rd_, h, b0), bank(eb, C * b0, C * (b1 - b0)), C * (b1 - b0), "DG%d%d" % (h, b0)
+            acc(err, [(out, zh("DG1"), counts(h, 0, 1, b0, b1)), (out, zh("DG2"), counts(h, -1, 1, b0, b1))], AK(h) + ["DH"], eb, n, [dg])
+            acc(err, [(out, T.RW1[:], part(T.GC, b0, b1))], gc + ["RW1", dg], eb, n)
+            acc(err, [(out, T.RW2[:], part(T.G4, b0, b1, 3))], g4 + ["RW2", dg], eb, n)
+            tt(part(T.PR, b0, b1), bank(HB, C * b0, n), vg(b0, b1), A.mult, vk[:-1] if b1 == 1 and not local else vk, [B(HB), "PR%d%d" % (h, b0)], n)
+            acc(err, [(out, zh("SAMH"), part(T.PR, b0, b1))], ["DH", "PR%d%d" % (h, b0), dg], eb, n)
+            for b in range(b0, b1):
+                a = S * h + C * b
+                prev, pk = (P1, k_("P")) if b == 0 else (T.M[:, a - C:a], "m%d%d" % (h, b - 1))
+                tt(T.M[:, a:a + C], bank(eb, C * b, C), prev, A.max, [pk], [B(eb), "m%d%d" % (h, b)], C)
+        act(T.AA[:, c], T.M[:, S * h + S - C:S * h + S], ["m%d3" % h], [k_("AA")], C, func=AF.Abs, bias=-BIG / 2)
+        act(T.AB[:, c], T.AA[:, c], [k_("AA")], [k_("AB")], C, func=AF.Abs, bias=-BIG / 2)
         ts(T.YB[:, c], T.AB[:, c], 128.0 - 15.0 / 32, 191.0, A.add, A.min, [k_("AB")], [k_("YB")], C)
         if rd_ < R - 1:
             ts(P1, T.YB[:, c], 129.0, 128.0, A.max, A.subtract, [k_("YB")], [k_("P")], C / 2)
@@ -419,18 +652,19 @@ def rank_program(g, core, T, topo):
 
     for rd_ in range(R):
         for h in range(H if rd_ else 0):
+            lead[0] = PLAN["lead"] * (H - 1 - h)
             find(h)
         for h in range(H):
+            lead[0] = PLAN["lead"] * (H - 1 - h)
             judge(rd_, h)
 
     known = {q: {} for q in Q}
     count, groups, tok = {}, {}, {}
-    ln = lanes(topo, core, peers)
-    arrive = sum(len(lanes(topo, c, [d for d in cores if d != c])[core]) for c in peers)
     for i in order(ops):
         o = ops[i]
         q = o["q"]
-        for t in sorted([tok[d] for d in o["deps"] if not (q == "p" and ops[d]["q"] == "p")], key=lambda t: -t["n"]):
+        need = [tok[d] for d in o["deps"] if not (q == "p" and ops[d]["q"] == "p") and not ops[d].get("chain")]
+        for t in sorted(need, key=lambda t: -t["n"]):
             if known[q].get(t["sem"], 0) < t["n"]:
                 Q[q].wait_ge(T.sem[t["sem"]], t["n"])
                 known[q][t["sem"]] = t["n"]
@@ -449,13 +683,12 @@ def rank_program(g, core, T, topo):
                 t["clock"][s] = max(t["clock"].get(s, 0), n)
         else:
             tr = []
-            for c in peers:
-                rid, pid, _ = topo.addr(c)
-                tr.append(RemoteDMATransfer(dst_ids=[DstId(rid=rid, pnc=pid)], dma_engine_mask=sum(1 << k for k in ln[c]),
-                                            remote_sem=T.sem[o["sem"]], src=o["src"](c), dst=o["dst"](c)))
-                count["ls"] = count.get("ls", 0) + len(ln[c])
+            for c, eng, sem, src, dst in o["tr"]:
+                tr.append(RemoteDMATransfer(dst_ids=[dest(topo, c)], dma_engine_mask=sum(1 << k for k in eng),
+                                            remote_sem=T.sem[sem], src=src, dst=dst))
+                count["ls"] = count.get("ls", 0) + len(eng)
             g.remote_dma_fused(tr, local_sem=T.sem["ls"])
-            count[o["sem"]] = arrive
-            tok[i] = {"sem": o["sem"], "n": arrive, "clock": {}}
+            count[o["sem"]] = o["n"]
+            tok[i] = {"sem": o["sem"], "n": o["n"], "clock": {}}
     for s, n in sorted(count.items(), key=lambda a: a[0][0] == "y"):
         g.wait_ge(T.sem[s], n)

@@ -10,13 +10,18 @@ S = N * C
 J = S // 16
 TA, TB, BA, VA = 0, F, 2 * F, 3 * F + 16
 BANKS = ["B%d" % b for b in range(8)]
+CUT = [0, 2048, 4096, 6144, 8192]
 VC = 4
 
-CY, PE, GAT, FIX, WAKE, HOP, ROW, BW = 0.95e-3, 0.48e-3, 1.56, 0.04, 0.12, 2.1, 0.02, 28e3
-PLAN = {"mode": "xxl", "gc": "vs", "gb": "s", "g4": "sssv", "g4x": "sssv", "dig": "vvvv", "digx": "vvvv", "vo": "vs", "gk": "",
-        "evac": "svsvsvsv", "first": "klxz", "then": "p", "llat": 6.0, "vlat": 14.0, "valq": "y", "zadd": "vvssssgg", "direct": 0,
-        "flat": 0, "lfirst": 20.0, "find0": 0, "line": "v", "gkafter": "ce3", "split": 1, "passes": 4, "tries": 300, "slack": 1.0, "lead": 0.0,
-        "vat": ["012", "", "3"], "vafter": [[], ["tbe3"], ["tbe3"], ["tbe3"]]}
+CY, PE, GAT, FIX, WAKE, HOP, ROW, BW = 0.95e-3, 0.48e-3, 1.56, 0.02, 0.21, 2.2, 0.012, 26e3
+PLAN = {"mode": "xxl", "gc": "vs", "gb": "s", "g4": [["sssv", "sssv"], ["sssv", "sssv"], ["svss", "svsv"]], "dig": "vvvvvv", "digx": "vvvvvv", "vo": "vs", "gk": "",
+        "evac": "vsvssvss", "first": "kxz", "then": "mp", "llat": 6.0, "vlat": 12.0, "valq": "y", "zadd": "vvvvssss", "direct": 0,
+        "flat": 0, "hsplit": [0, 1], "ways": 0,
+        "cases": [((0.9, 0.9), 0.24, 0.0, 1.0, 0.35), ((1.3, 1.3), 0.1, 0.0, 0.8, 0.2), ((1.15, 1.15), 0.3, 1.0, 1.2, 0.2),
+                  ((1.05, 1.35), 0.1, -0.5, 0.8, 0.2)], "keep": [1, 1], "ons": "", "rnd": "", "half": "ss", "onv": ["W4X", "W4L", "WK", "KT", "KU", "KX0", "KX1", "KL0", "RA1", "RA2"],
+        "free": ["SE", "WH", "DG", "DH", "P0", "P1", "wf", "WL", "LT", "AD"], "wsend": "", "flead": [0.0, 0.0], "lfirst": 20.0,
+        "find0": 0, "line": "v", "gkafter": "ce3", "split": [1, 2], "passes": 4, "tries": 1200, "slack": 1.0, "lead": 0.0,
+        "vat": ["012", "c0 c1 v3 c2 b0 b1 c3 A b2 b3"], "vafter": [[], ["xb3"], ["xb3"], ["xb3"]]}
 
 
 def _sb(cols, dtype):
@@ -24,10 +29,9 @@ def _sb(cols, dtype):
 
 
 SCRATCH = {"PS": ("psum", [128, 4096], "float32"), "TAB": _sb(VA + N * V, "bfloat16"), "LALL": _sb(N * LW, "bfloat16")}
-SCRATCH.update({n: _sb(F, "bfloat16") for n in ("X", "CT", "ADD")})
 SCRATCH.update({n: _sb(4 * H * S, "bfloat16") for n in ("G4", "R4")})
 SCRATCH.update({n: _sb(1024, "bfloat16") for n in ("GC", "GB", "GK", "RC", "RB")})
-SCRATCH.update({n: _sb(128, "bfloat16") for n in ("TMP", "SAME", "S1K", "ID", "PK", "RW1", "RW2", "SUP", "DGB", "K4L")})
+SCRATCH.update({n: _sb(128, "bfloat16") for n in ("TMP", "SAME", "S1K", "ID", "PK", "RW1", "RW2", "SUP", "DGB", "K4L", "NID")})
 MATS = (("MA", 128), ("EQ", 128), ("WK", 144), ("W4X", 144), ("W4L", 144), ("SEL", 128), ("WA1", 144), ("WN", 144), ("WP", 144), ("WA4", 144),
         ("DG2", 128), ("DG1", 128), ("SAMH", 128))
 AT = {n: sum(w for _, w in MATS[:k]) for k, (n, _) in enumerate(MATS)}
@@ -37,11 +41,11 @@ SCRATCH.update({
     "HI": _sb(512, "bfloat16"), "LO": _sb(512, "bfloat16"), "IO": _sb(16, "float32"), "E16": _sb(16, "float32"), "EK": _sb(16, "float32"),
     "NAT": _sb(1024, "int32"), "LTI": _sb([4, 8, 16], "int32"), "LTF": _sb([4, 8, 16], "float16"),
     "WF": _sb(512, "float16"), "WL": _sb(512, "uint16"), "PRI": _sb(256, "int32"), "PB": _sb(272, "bfloat16"),
-    "Y": _sb(256, "float32"), "WR": _sb(16, "bfloat16"), "WC": _sb(16, "float32"), "WD": _sb(8, "float32"),
-    "PI": _sb(4, "int32"), "CI": _sb(4, "int32"), "CF": _sb(24, "float32"), "ONES": _sb(256, "bfloat16"),
+    "Y": _sb(256, "float32"), "WR": _sb(16, "bfloat16"), "WC": _sb(16 * N, "float32"),
+    "PI": _sb(4, "int32"), "CI": _sb(4, "int32"), "CF": _sb(24, "float32"), "ONES": _sb(512, "bfloat16"),
     "TMQ": _sb(64, "bfloat16"), "TRI": _sb(256, "bfloat16"), "PM": _sb(64, "bfloat16"),
     "TJ": _sb(J, "float32"), "TBC": _sb(J, "bfloat16"), "TJ4": _sb(128, "float32"), "TJL": _sb(128, "float32"), "K4X": _sb(128, "bfloat16"),
-    "AQ": _sb([N, 272], "float16"), "OFF": _sb(S, "float32"), "CAR": _sb(4, "float32"),
+    "AQ": _sb([N + 1, 272], "float16"), "RUN": _sb(256, "float32"), "OFF": _sb(4, "float32"), "CAR": _sb(4, "float32"), "CT": _sb(F + 16, "bfloat16"),
     "LT": _sb(H * J, "uint16"), "L4": _sb(H * 4 * J, "uint16"), "KL": _sb(R * H * 56, "uint16"), "VG": _sb(R * H * 7 * C, "bfloat16"),
     "PR": _sb(1024, "float16"), "M": _sb(1024, "float32"), "AA": _sb(256, "float32"), "AB": _sb(256, "float32"), "YB": _sb(256, "bfloat16"),
 })
@@ -79,7 +83,7 @@ def dest(topo, c):
 def place(ops, succ, pred, prio, span):
     n, back = len(ops), span is not None
     left = [len(p) for p in pred]
-    start, end, free, wire, dep = [0.0] * n, [0.0] * n, {}, 0.0, [0.0] * n
+    start, end, free, wire, dep = [0.0] * n, [0.0] * n, {}, [], [0.0] * n
     ready = [i for i in range(n) if not left[i]]
     done = []
     while ready:
@@ -93,8 +97,12 @@ def place(ops, succ, pred, prio, span):
         if not back:
             end[k] += o["lat"]
             if o["wire"]:
-                wire = max(wire, end[k] - 0.5) + o["wire"]
-                end[k] = wire + 0.5
+                t = end[k] - 0.5
+                for a, b in wire:
+                    if t + o["wire"] > a and t < b:
+                        t = b
+                wire = sorted(wire + [(t, t + o["wire"])])
+                end[k] = t + o["wire"] + 0.5 + o.get("more", 0.0)
         ready.remove(k)
         done.append(k)
         for i, gap in succ[k]:
@@ -120,16 +128,38 @@ def order(ops):
             pred[i].append((d, gap))
     tail = [0.0] * n
     for i in range(n - 1, -1, -1):
-        tail[i] = ops[i]["cost"] + ops[i]["lat"] + ops[i]["wire"] + max([tail[j] + WAKE for j, _ in succ[i]] + [0.0])
+        tail[i] = ops[i]["cost"] + ops[i]["lat"] + ops[i]["wire"] + ops[i].get("more", 0.0) + max([tail[j] + WAKE for j, _ in succ[i]] + [0.0])
     lead = [o["lead"] for o in ops]
     for i in range(n - 1, -1, -1):
         lead[i] = max([lead[i]] + [lead[j] for j, gap in succ[i] if gap is not None])
+
+    def worth(done):
+        total = 0.0
+        for speed, wake, hop, move, weight in PLAN["cases"]:
+            start, end, free, wire = [0.0] * n, [0.0] * n, {}, []
+            for k in done:
+                o, t = ops[k], free.get(ops[k]["q"], 0.0)
+                for d, gap in pred[k]:
+                    t = max(t, start[d] if gap is None else end[d] + (wake if gap else 0.0))
+                start[k] = t
+                free[o["q"]] = t = t + o["cost"] * (speed[o["q"] == "p"] if o["kind"] == "op" else 1.0)
+                t += o["lat"] + (hop if o["kind"] == "send" else 0.0)
+                if o["wire"]:
+                    t, w = t - 0.5, o["wire"] * move
+                    for a, b in wire:
+                        if t + w > a and t < b:
+                            t = b
+                    wire = sorted(wire + [(t, t + w)])
+                    t += w + 0.5 + o.get("more", 0.0) * move
+                end[k] = t
+            total += max(end) * weight
+        return total
     best = None
     for _ in range(PLAN["passes"]):
         tail = [tail[i] + lead[i] for i in range(n)]
         done, start, end = place(ops, succ, pred, tail, None)
-        if best is None or max(end) < best[0]:
-            best = (max(end), done, tail)
+        if best is None or worth(done) < best[0]:
+            best = (worth(done), done, tail)
         tail = place(ops, pred, succ, end, [end[i] - start[i] - ops[i]["cost"] for i in range(n)])[2]
     seed = 1
     for k in range(PLAN["tries"]):
@@ -137,9 +167,10 @@ def order(ops):
         for _ in range(n // (10, 40)[k % 2]):
             seed = (seed * 1103515245 + 12345) % 2 ** 31
             prio[seed // 64 % n] += (seed // 16384 % 201 - 100) * (0.005, 0.015, 0.04)[k % 3]
-        done, start, end = place(ops, succ, pred, prio, None)
-        if max(end) <= best[0]:
-            best = (max(end), done, prio)
+        done = place(ops, succ, pred, prio, None)[0]
+        w = worth(done)
+        if w <= best[0]:
+            best = (w, done, prio)
     EST.append(best[0])
     ORDER[n] = best[1]
     return best[1]
@@ -149,7 +180,7 @@ EST, ORDER = [], {}
 
 
 def val_at(T, b, k):
-    return T.TAB[:, VA + V * b + V // VC * k:VA + V * b + V // VC * (k + 1)]
+    return T.TAB[:, VA + V * b + CUT[k]:VA + V * b + CUT[k + 1]]
 
 
 def block(cores, at, q):
@@ -166,14 +197,17 @@ def helper_program(g, core, T, topo):
     if not src or "l" not in PLAN["mode"]:
         return
     to = [c for c in cores if c != src[0] and c not in direct(topo, cores, src[0])]
-    n = len(topo.engines(core, to[0]))
+    e = topo.engines(core, to[0])
     got = len(topo.engines(src[0], core)) // (2 if PLAN["direct"] else 1)
+    far = [c for c in to if topo.die(c) != topo.die(core)]
+    ways = [(far, e[0::2]), ([c for c in to if c not in far], e[1::2])] if PLAN["ways"] else [(to, e)]
     for k in range(VC):
         g.wait_ge(T.sem["rv%d" % k], got)
-        g.remote_dma_fused([RemoteDMATransfer(dst_ids=[dest(topo, c) for c in to], dma_engine_mask=topo.mask(core, to[0]),
+        g.remote_dma_fused([RemoteDMATransfer(dst_ids=[dest(topo, c) for c in part], dma_engine_mask=sum(1 << j for j in eng),
                                               remote_sem=T.sem["vall"], src=val_at(T, 0, k),
-                                              dsts=[val_at(T, block(cores, c, src[0]), k) for c in to])], local_sem=T.sem["ls"])
-    g.wait_ge(T.sem["ls"], n * VC)
+                                              dsts=[val_at(T, block(cores, c, src[0]), k) for c in part]) for part, eng in ways],
+                           local_sem=T.sem["ls"])
+    g.wait_ge(T.sem["ls"], len(e) * VC)
 
 
 def rank_program(g, core, T, topo):
@@ -192,7 +226,7 @@ def rank_program(g, core, T, topo):
         deps = set()
         for key in rd:
             deps |= set(wrs.get(key, []))
-        i = len(ops)
+        i, k["name"] = len(ops), (list(wr) + [""])[-2 if wr else -1]
         if group:
             if group not in opened:
                 opened[group] = set(wrs.get(wr[0], []) + rds.get(wr[0], []))
@@ -221,7 +255,7 @@ def rank_program(g, core, T, topo):
     line = [PLAN["line"]]
 
     def op(q, fn, rd, wr, cost):
-        add(q, "op", rd, wr, cost, fixed=q in line[0] and wr[-1] not in ("SELH", "WH", "DGB", "DH") and "line" + q, fn=fn)
+        add(q, "op", rd, wr, cost, fixed=q in line[0] and wr[-1][:2] not in PLAN["free"] and "line" + q, fn=fn)
 
     def mm(items, rd, wr, n):
         def fn():
@@ -303,19 +337,25 @@ def rank_program(g, core, T, topo):
             for k, tab in enumerate((T.nxt, T.prv)):
                 for h in range(2):
                     dma("y", "lt", T.LTI[:, 2 * k + h], tab[h::2, :], (), ["lti%d" % (2 * k + h)], 128, 512)
+        if n == "m":
+            for k in range(16):
+                a, e = 32 * (k % 4), 32 * (k % 4) + 16 * (k // 4 % 2)
+                dma("y", "lt", T.LTF[a:a + 32, k // 4], T.PV[e:e + 16, 256 * (k // 8):256 * (k // 8) + 256], ["PVa"], ["ltf%d" % k], 32, 256)
         if n == "p":
             dma("y", "pri", T.PRI[:], T.pri[:], (), ["PRI"], 128, 1024)
         if n in "xz":
             c = slice(0, 2048) if n == "x" else slice(2048, 4096)
-            dma("y", n, T.X[:, c], T.x[:, c], (), [n], 128, 4096)
+            dma("y", n, TAB[:, TB + c.start:TB + c.stop], T.x[:, c], (), [n], 128, 4096)
         if n in "0123":
             k = int(n)
-            dma(PLAN["valq"], VALK[k], val_at(T, 0, k), T.val[:, V // VC * k:V // VC * (k + 1)], (), [VALK[k]], 128, 2 * V // VC)
+            dma(PLAN["valq"], VALK[k], val_at(T, 0, k), T.val[:, CUT[k]:CUT[k + 1]], (), [VALK[k]], 128, 2 * (CUT[k + 1] - CUT[k]))
     for n in PLAN["first"]:
         load(n)
 
     op("g", lambda: g.iota(T.PI[:, 0:1], [[0, 1]], 0, 1), (), ["PI"], 0.14)
-    fill(T.ONES[:], 1.0, ["ONES"], 128)
+    op("g", lambda: g.iota(T.IO[:], [[1, 16]], 0, 0, allow_small_or_imprecise_dtypes=True), (), ["IO"], 0.2)
+    ops[-1]["lead"] = 100.0
+    fill(T.ONES[:], 1.0, ["ONES"], 256)
     fill(T.ZB[:, 0:AT["DG2"]], 0.0, ["ZB"], AT["DG2"] / 2)
 
     def zb(n, a=0, b=128, step=1):
@@ -326,9 +366,8 @@ def rank_program(g, core, T, topo):
     for k, m in enumerate((1, 15, 13, 3)):
         ts(T.CI[:, k:k + 1], T.PI[:, 0:1], m, None, A.bitwise_and, None, ["PI"], ["CI%d" % k])
     cp(T.CF[:, 0:4], T.CI[:, 0:4], ["CI0", "CI1", "CI2", "CI3"], ["CF"])
-    ODD, ROW16, KIND, ROW4, C17, EVN, P16, E17, K4, IS2, NEV, NOD, BI0, BIA, R16, RA1, RA2, KX0, KX1, KL0, KT, KU = [
-        T.CF[:, k:k + 1] for k in range(22)]
-    op("g", lambda: g.iota(T.IO[:], [[1, 16]], 0, 0, allow_small_or_imprecise_dtypes=True), (), ["IO"], 0.2)
+    ODD, ROW16, KIND, ROW4, C17, EVN, P16, E17, K4, IS2, NEV, NOD, BI0, BIA, R16, RA1, RA2, KX0, KX1, KL0, KT, KU, N17 = [
+        T.CF[:, k:k + 1] for k in range(23)]
     ts(T.E16[:], T.IO[:], ROW16, None, A.is_equal, None, ["IO", "CF"], ["E16"])
     ts(T.EK[:], T.IO[:], KIND, None, A.is_equal, None, ["IO", "CF"], ["EK"])
     ts(IS2, ROW4, 2.0, None, A.is_equal, None, ["CF"], ["IS2"])
@@ -336,7 +375,12 @@ def rank_program(g, core, T, topo):
     R15 = T.E16[:, 15:16]
 
     def col(out, a, scale, bias, rd, key):
-        act(out, a, rd, [key], 64, scale=scale, bias=bias)
+        if key in PLAN["onv"]:
+            keep, line[0] = line[0], ""
+            ts(out, a, scale, bias, A.mult, A.add, rd, [key])
+            line[0] = keep
+        else:
+            act(out, a, rd, [key], 64, scale=scale, bias=bias)
     col(C17, ODD, 16.0, 1.0, ["CF"], "C17")
     col(EVN, ODD, -1.0, 1.0, ["CF"], "EVN")
     col(E17, ODD, -1.0 / 17, 1.0 / 17, ["CF"], "E17")
@@ -344,27 +388,23 @@ def rank_program(g, core, T, topo):
     col(NOD, ODD, -1.0, 0.0, ["CF"], "NOD")
     col(P16, ROW16, 16.0, 16.0, ["CF"], "P16")
     col(R16, R15, 16.0, 0.0, ["E16"], "R16")
-    col(BI0, T.E16[:, 3:4], 2048.0, R15, ["E16"], "BI0")
+    col(BI0, T.E16[:, 3:4], 2048.0, 0.0, ["E16"], "BI0")
     col(BIA, T.E16[:, 7:8], 2048.0, BI0, ["BI0"], "BIA")
     col(RA1, T.EK[:, 9:10], 1.0 / 16, 0.0, ["EK"], "RA1")
-    col(RA2, R15, -BIG, RA1, ["E16", "RA1"], "RA2")
+    col(RA2, T.E16[:, 5:6], -BIG, RA1, ["E16", "RA1"], "RA2")
     fill(T.PB[:, 0:16], 0.0, ["PB0"])
-    fill(T.AQ[:, :, 0:16], 1024.0, ["AQ0"])
+    fill(T.AQ[:, :, 0:16], 1026.0, ["AQ0"])
     fill(TAB[:, 3 * F:VA], 0.0, ["gap"])
-    for k in range(2):
-        act(T.OFF[:, 256 * k:256 * k + 256], T.ONES[:], ["ONES"], ["OFF"], 256, scale=0.0)
-    for b in range(N):
-        act(T.OFF[:, C * b:C * b + 1], T.ONES[:, 0:1], [], ["OFF"], 64, scale=1024.5 - (learner[b] + 1) / 4 + 1.0 / 2048)
+    fill(T.CT[:, F:F + 16], 0.0, ["pad"])
+    for b in range(0 if PLAN["rnd"] else N):
+        act(T.OFF[:, b:b + 1], T.ONES[:, 0:1], ["ONES"], ["OFF"], 64, scale=1026.5 - (learner[b] + 1) / 4 + 1.0 / 2048)
     zero = []
     for k, q in enumerate(PLAN["zadd"]):
         zero.append("ADD%d" % k)
         if q == "v":
-            fill(T.ADD[:, 512 * k:512 * k + 512], 0.0, [zero[-1]], 256)
-        elif q == "g":
-            op("g", lambda k=k: g.iota(T.ADD[:, 512 * k:512 * k + 512], [[0, 512]], 0, 0, allow_small_or_imprecise_dtypes=True), (), [zero[-1]], 1.2)
+            ts(TAB[:, BA + 512 * k:BA + 512 * k + 512], T.ONES[:], T.E16[:, 5:6], None, A.mult, None, ["ONES", "E16"], [zero[-1]], 256)
         else:
-            for j in range(2):
-                act(T.ADD[:, 512 * k + 256 * j:512 * k + 256 * j + 256], T.ONES[:], ["ONES"], [zero[-1]], 256, scale=0.0)
+            act(TAB[:, BA + 512 * k:BA + 512 * k + 512], T.ONES[:], ["ONES", "E16"], [zero[-1]], 512, scale=T.E16[:, 5:6])
     sel(T.TMQ[:], T.ONES[:, 0:64], [[-2, 64]], A.is_ge, 0, 1, ["ONES"], ["TMQ"], 64)
     sel(T.PM[:], T.TMQ[:], [[2, 64]], A.is_ge, 1, -1, ["TMQ"], ["PM"], 64)
     sel(zb("SEL", 1, 128, 2), T.ONES[:, 0:64], [[-1, 8], [-8, 8]], A.is_equal, 0, 1, ["ONES", "ZB"], ["SEL"], 64)
@@ -379,7 +419,7 @@ def rank_program(g, core, T, topo):
     G0 = T.SAME[:, 0::16]
 
     def mark(n, a, scale, rd, key):
-        act(zb(n, a, min(a + 128, dict(MATS)[n]), 16), G0, ["SAME", "ZB"] + rd, [key], 64, scale=scale)
+        col(zb(n, a, min(a + 128, dict(MATS)[n]), 16), G0, scale, 0.0, ["SAME", "ZB"] + rd, key)
     mark("EQ", 1, NEV, ["NEV"], "EQ0")
     mark("EQ", 3, NOD, ["NOD"], "EQ1")
     act(T.S1K[:], T.SAME[:], ["SAME"], ["S1K"], 128, scale=1.0 / 1024)
@@ -403,6 +443,8 @@ def rank_program(g, core, T, topo):
     act(zb("DG2"), zb("WP", 15, 143), ["WPp"], ["DG2"], 128, scale=-BIG / 8)
     act(zb("SAMH"), T.SAME[:], ["SAME"], ["SAMH"], 128, scale=1.0 / 16)
     cp(zh("DG2", 0, 384), zb("DG2", 0, 384), ["DG1", "DG2", "SAMH"], ["DH"], 192)
+    if any(PLAN["keep"]):
+        act(T.NID[:], T.ID[:], ["ID"], ["NID"], 128, scale=-1.0)
     act(T.RW1[:], T.SAME[:], ["SAME", "RA1"], ["RW1"], 128, scale=RA1)
     act(T.RW2[:], T.SAME[:], ["SAME", "RA2"], ["RW2"], 128, scale=RA2)
     if "x" in PLAN["mode"]:
@@ -413,7 +455,7 @@ def rank_program(g, core, T, topo):
         for h, a in enumerate((KX0, KX1)):
             col(a, IS2, float(TB - BA + F // H * h), K4, ["IS2", "K4"], "KX%d" % h)
     if "l" in PLAN["mode"]:
-        col(KL0, IS2, float(VA - BA - 1), K4, ["IS2", "K4"], "KL0")
+        col(KL0, IS2, float(VA - BA), K4, ["IS2", "K4"], "KL0")
         op("g", lambda: g.iota(T.TJL[:], [[V, N], [0, 32]], 0, 0, allow_small_or_imprecise_dtypes=True), (), ["TJL"], 0.4)
         act(T.K4L[:], T.TJL[:], ["TJL", "IS2"], ["K4L"], 128, scale=IS2)
 
@@ -431,43 +473,71 @@ def rank_program(g, core, T, topo):
     tt(T.LO[:], T.NAT[:, 512:1024], T.HI[:], A.subtract, ["nat2", "nat3", "HI"], ["LO"], 1024)
     for r in range(4):
         n, k = ("HI", "LO")[r % 2], r // 2
-        dma("y", "add", T.ADD[2 * r + 9::16, :], T[n][:, 256 * k:256 * k + 256], [n] + zero, ["add%d" % r], 128, 512)
+        dma("y", "add", TAB[2 * r + 9::16, BA:BA + F], T[n][:, 256 * k:256 * k + 256], [n] + zero, ["add%d" % r], 128, 512)
     ADDK = zero + ["add%d" % r for r in range(4)]
     for n in PLAN["vat"][0]:
         load(n)
 
     act(T.WC[:, 1:14], T.WR[:, 1:14], ["wr0", "wr1"], ["WC"], 64)
-    act(T.WD[:, 0:2], T.WC[:, 5:13:7], ["WC", "EVN"], ["WD"], 64, scale=EVN)
-    cols = [(T.WD[:, 0:1], T.WD[:, 1:2])] + [(T.WC[:, a:a + 1], T.WC[:, a + 7:a + 8]) for a in (3, 6, 1)]
-    for t in range(4):
-        act(T.LALL[:, 128 * t:128 * t + 128], zb("MA"), ["MA", "WD"], ["la%d" % t], 128, scale=cols[t][0])
-    for t in range(4):
-        act(T.LALL[:, 513 + 128 * t:640 + 128 * t:2], T.PM[:], ["PM", "WD"], ["lo%d" % t], 64, scale=cols[t][1])
-    act(T.LALL[:, 512:1024:2], T.LALL[:, 0:512:2], ["la%d" % t for t in range(4)], ["le"], 256, scale=-17.0)
-    mm([(bank(7, 0, 128), zb("EQ"), T.LALL[:, 512 + 128 * t:640 + 128 * t], t == 0, False) for t in range(4)]
-       + [(bank(7, 0, 128), T.ID[:], T.LALL[:, 512:640], False, True)],
-       ["EQ0", "EQ1", "ID", "le"] + ["lo%d" % t for t in range(4)], ["B7"], 128)
-    act(T.LALL[:, 512:640], bank(7, 0, 128), (), ["B7", "lo0", "le"], 128)
-    own = ["la%d" % t for t in range(4)] + ["lo%d" % t for t in range(4)] + ["le"]
+    act(T.WC[:, 14:16], T.WC[:, 5:13:7], ["WC", "EVN"], ["W0"], 64, scale=EVN)
+    mats = {}
+
+    def scaled(q, out, a, by, rd, key, n):
+        rd = rd + [{"s": "xg3", "v": "ce3"}[q]]
+        if q == "s":
+            act(out, a, rd, [key], n, scale=by)
+        else:
+            ts(out, a, by, None, A.mult, None, rd, [key], n / 2)
+
+    def matrices(b, src, who, at):
+        L, W = LW * b, 16 * b
+        la, lo, le = ["la%d%d" % (b, t) for t in range(4)], ["lo%d%d" % (b, t) for t in range(4)], "le%d" % b
+        for t, a in enumerate((14, 3, 6, 1)):
+            scaled(who[0], T.LALL[:, L + 128 * t:L + 128 * t + 128], zb("MA"), T.WC[:, W + a:W + a + 1], ["MA", src], la[t], 128)
+        for t, a in enumerate((15, 10, 13, 8)):
+            scaled(who[1], T.LALL[:, L + 513 + 128 * t:L + 640 + 128 * t:2], T.PM[:], T.WC[:, W + a:W + a + 1], ["PM", src], lo[t], 64)
+        scaled(who[2], T.LALL[:, L + 512:L + 1024:2], T.LALL[:, L:L + 512:2], -17.0, la, le, 256)
+        mm([(bank(at, 0, 128), zb("EQ"), T.LALL[:, L + 512 + 128 * t:L + 640 + 128 * t], t == 0, False) for t in range(4)]
+           + [(bank(at, 0, 128), T.ID[:], T.LALL[:, L + 512:L + 640], False, True)], ["EQ0", "EQ1", "ID", le] + lo, ["B%d" % at], 128)
+        (act if who[3] == "s" else cp)(T.LALL[:, L + 512:L + 640], bank(at, 0, 128), (), ["B%d" % at, lo[0], le], 128)
+        mats[b] = la + lo + [le]
     PTK = ["pt%d" % r for r in range(6)]
-    exchange("la", lambda c: T.LALL[:, 0:LW], lambda c: T.LALL[:, LW * block(cores, c, core):LW * (block(cores, c, core) + 1)],
-             own, ["lpeer"], PLAN["llat"], 3.0)
-    ops[-1]["lead"] = PLAN["lfirst"]
+    if PLAN["wsend"]:
+        exchange("la", lambda c: T.WC[:, 1:16], lambda c: T.WC[:, 16 * block(cores, c, core) + 1:16 * block(cores, c, core) + 16],
+                 ["W0"], ["lpeer"], PLAN["llat"])
+        ops[-1]["lead"] = PLAN["lfirst"]
+        matrices(0, "W0", "ssss", 7)
+    elif PLAN["half"]:
+        matrices(0, "W0", "ssss", 7)
+        exchange("la", lambda c: T.LALL[:, 512:LW], lambda c: T.LALL[:, LW * block(cores, c, core) + 512:LW * (block(cores, c, core) + 1)],
+                 mats[0], ["lpeer"], PLAN["llat"], 1.0)
+        ops[-1]["lead"] = PLAN["lfirst"]
+        col(N17, ODD, 1.0 / 17, -1.0 / 17, ["CF"], "N17")
+        for b in range(1, N):
+            op("g", lambda b=b: g.iota(T.LALL[:, LW * b:LW * b + 512], [[0, 512]], 0, 0, allow_small_or_imprecise_dtypes=True), (), ["lz%d" % b], 1.2)
+    else:
+        matrices(0, "W0", "ssss", 7)
+        exchange("la", lambda c: T.LALL[:, 0:LW], lambda c: T.LALL[:, LW * block(cores, c, core):LW * (block(cores, c, core) + 1)],
+                 mats[0], ["lpeer"], PLAN["llat"], 2.0)
+        ops[-1]["lead"] = PLAN["lfirst"]
+        mats.update({b: ["lpeer"] for b in range(1, N)})
 
     def send_val(k, rd):
         mine, near = helpers(topo, cores)[core], direct(topo, cores, core)
         e = topo.engines(core, mine)
-        total = sum(VC * len(e) // (2 if core in direct(topo, cores, c) else 1) for c in peers)
+        total = sum(VC * len(e) // (2 if PLAN["ways"] or core in direct(topo, cores, c) else 1) for c in peers)
         tr = [(mine, e[0::2] if near else e, "rv%d" % k, val_at(T, 0, k), val_at(T, 0, k))]
         tr += [(c, e[1::2], "vall", val_at(T, 0, k), val_at(T, block(cores, c, core), k)) for c in near]
         send(tr, "vall", total, [VALK[k]] + ["sent%d" % (k - 1)] * (k > 0) + rd, ["sent%d" % k],
-             PLAN["vlat"] * (k == VC - 1), 8 * len(tr) * (ROW + 2 * V / VC / BW))
+             2.0, 8 * len(tr) * (ROW + 2 * (CUT[k + 1] - CUT[k]) / BW))
         ops[-1]["chain"] = k < VC - 1
+        ops[-1]["more"] = PLAN["vlat"] * (k == VC - 1)
     VALL = VALK + ["sent%d" % (VC - 1)]
 
-    ts(T.LTF[:], T.LTI[:], -2048.0, None, A.add, None, ["lti%d" % k for k in range(4)], ["LTF"], 512)
+    if "l" in PLAN["first"] + PLAN["then"]:
+        ts(T.LTF[:], T.LTI[:], -2048.0, None, A.add, None, ["lti%d" % k for k in range(4)], ["LTF"], 512)
     for b in range(8):
-        op("v", lambda b=b: vv.transpose(T.WF[:, b::8], T.LTF[:, :, b, :]), ["LTF"], ["wf%d" % b], cyc(64))
+        op("v", lambda b=b: vv.transpose(T.WF[:, b::8], T.LTF[:, :, b, :]), ["LTF"] + ["ltf%d" % k for k in range(16)], ["wf%d" % b], cyc(64))
     ts(T.WL[:], T.WF[:], 2048.0, None, A.add, None, ["wf%d" % b for b in range(8)], ["WL"], 256)
 
     def counts(h, a, step, b0=0, b1=N):
@@ -476,36 +546,54 @@ def rank_program(g, core, T, topo):
     def AK(h):
         return ["a%d%d" % (h, b) for b in range(N)] + (["AQ0"] if h == 0 else ["a%d%d" % (h - 1, b) for b in range(N)])
 
-    def find(h):
+    def find(h, first=False, keep=PLAN["keep"][PLAN["mode"][0] == "l"]):
         W0, W1 = 4 * h, 4 * h + 1
         a = 16 + C * h
         mm([(bank(W0, 0, C), T.TRI[:, 0:128], T.PB[:, a:a + C], True, False),
             (bank(W0, 0, C), T.TRI[:, 128:256], T.PB[:, a - 1:a - 1 + C], False, True)],
            ["P%d" % h, "P%d" % (h - 1) if h else "PB0", "tri0", "tri1"], ["B%d" % W0], C)
+        run = T.RUN[:, C * h:C * h + C]
+        if PLAN["rnd"] or h == 0 or keep:
+            op("v", lambda: vv.tensor_tensor_scan(run, T.ONES[:, 0:C], bank(W0, 0, C), T.RUN[:, C * h - 1:C * h] if h else 0.0, A.mult, A.add),
+               ["ONES"] + ["RUN0"] * h, ["B%d" % W0, "RUN%d" % h], cyc(C))
+        if keep:
+            act(T.AQ[:, N, a:a + C], run, ["RUN%d" % h], ["all%d" % h], C, scale=4.0, bias=1025.5 + 1.0 / 512)
+        if not PLAN["rnd"] and h == 0:
+            act(T.CAR[:, 0:4], T.OFF[:, 0:4], ["RUN0", "OFF"], ["CAR"], 64, bias=T.RUN[:, C - 1:C])
         for b in range(N):
-            op("v", lambda b=b: vv.tensor_tensor_scan(T.AQ[:, b, a:a + C], T.OFF[:, C * b:C * b + C], bank(W0, 0, C),
-                                                      T.CAR[:, 0:1] if h else 0.0, A.add, A.add),
-               ["OFF"] + ["CAR"] * h, ["B%d" % W0, "a%d%d" % (h, b)], cyc(C))
-        if h == 0:
-            op("v", lambda: vv.tensor_reduce(T.CAR[:, 0:1], bank(W0, 0, C), AX.X, A.add), (), ["B%d" % W0, "CAR"], cyc(C))
+            off = 1026.5 - (learner[b] + 1) / 4 + 1.0 / 2048
+            if not PLAN["rnd"]:
+                op("v", lambda b=b, off=off: vv.tensor_tensor_scan(T.AQ[:, b, a:a + C], T.ONES[:, 0:C], bank(W0, 0, C),
+                                                                   T.CAR[:, b:b + 1] if h else off, A.mult, A.add),
+                   ["ONES"] + ["CAR"] * h, ["B%d" % W0, "a%d%d" % (h, b)], cyc(C))
+            elif PLAN["rnd"][b] == "s":
+                act(T.AQ[:, b, a:a + C], run, ["RUN%d" % h], ["a%d%d" % (h, b)], C, bias=off)
+            else:
+                ts(T.AQ[:, b, a:a + C], run, off, None, A.add, None, ["RUN%d" % h], ["a%d%d" % (h, b)], C)
         out = bank(W1, 0, J)
         mm([(out, T.ID[:], T.TBC[:], True, False)], ["ID", "TBC"], ["B%d" % W1], J)
         mm([(out, zh("WA1", 14 - i, 142 - i), counts(h, i, 16), False, False) for i in range(15)]
            + [(out, zh("WN"), counts(h, 15, 16), False, False), (out, zh("WP", 15, 143), counts(h, -1, 16), False, True)],
            AK(h) + ["WH"], ["B%d" % W1], J)
-        ts(T.LT[:, J * h:J * h + J], out, float(F // H - 1), None, A.min, None, (), ["B%d" % W1, "LT%d" % h])
+        if first or "t" not in PLAN["ons"]:
+            ts(T.LT[:, J * h:J * h + J], out, float(F // H - 1), None, A.min, None, (), ["B%d" % W1, "LT%d" % h])
+        else:
+            act(T.LT[:, J * h:J * h + J], out, (), ["B%d" % W1, "LT%d" % h], 64)
 
     for h in range(H):
         cp(T.PB[:, 16 + C * h:16 + C * h + C], T.PRI[:, C * h:C * h + C], ["PRI"], ["P%d" % h], C)
     for h in range(PLAN["find0"]):
-        find(h)
+        find(h, True)
 
     def ask(rd_, h, src, rd, less):
         e, W0, Jq = rd_ * H + h, 4 * h, J // N
         K0, V0 = 7 * Jq * e, 7 * C * e
         mm([(bank(W0, 0, J), zb("WK", 15 - i, 143 - i), src[:, S * h + i:S * h + S:16], i == 0, i == 15) for i in range(16)],
            rd + ["WK"], ["B%d" % W0], J)
-        ts(T.KL[:, K0 + 3 * Jq:K0 + 7 * Jq], bank(W0, 0, J), -less, None, A.add, None, (), ["B%d" % W0, "KL%d" % e])
+        if "k" in PLAN["ons"]:
+            act(T.KL[:, K0 + 3 * Jq:K0 + 7 * Jq], bank(W0, 0, J), (), ["B%d" % W0, "KL%d" % e], 64, bias=-less)
+        else:
+            ts(T.KL[:, K0 + 3 * Jq:K0 + 7 * Jq], bank(W0, 0, J), -less, None, A.add, None, (), ["B%d" % W0, "KL%d" % e])
         exchange("ka%d_%d" % (rd_, h), lambda d: T.KL[:, K0 + Jq * (3 + block(cores, core, d)):K0 + Jq * (4 + block(cores, core, d))],
                  lambda d: T.KL[:, K0 + Jq * (block(cores, d, core) - 1):K0 + Jq * block(cores, d, core)], ["KL%d" % e], ["KIN%d" % e], HOP)
         vo = pick(PLAN["vo"], T.VG, V0, TAB[:, VA:VA + V], T.KL, K0, S, VALK + ["KIN%d" % e, "KL%d" % e], "VO%d" % e)
@@ -514,54 +602,62 @@ def rank_program(g, core, T, topo):
         return lambda b0, b1: T.VG[:, V0 + (3 + b0) * C:V0 + (3 + b1) * C], vo + ["VG%d" % e]
 
     line[0] = "vsp"
-    banks, ahead = ((2, 3, 6, 7, 0, 4, 1, 5), 4) if PLAN["find0"] else (range(8), 8)
+    banks, ahead = ((range(8), 8), ((2, 3, 4, 5, 6, 7, 0, 1), 6), ((2, 3, 6, 7, 0, 4, 1, 5), 4))[PLAN["find0"]]
 
     def pack(k):
-        mm([(bank(banks[k]), T.PK[:], T.X[:, 512 * k:512 * k + 512], True, False)], ["PK", "xz"[k // 4]], ["B%d" % banks[k]], 512)
+        mm([(bank(banks[k]), T.PK[:], TAB[:, TB + 512 * k:TB + 512 * k + 512], True, False)], ["PK", "xz"[k // 4]], ["B%d" % banks[k]], 512)
     for k in range(ahead):
         pack(k)
     for k, b in enumerate(banks):
         mm([(bank(b), T.ZH[0:48, AT["SEL"]:AT["SEL"] + 128], T.PT[0:48, 512 * k:512 * k + 512], False, True)], ["SELH"] + PTK, ["B%d" % b], 512)
         if k + ahead < 8:
             pack(k + ahead)
-        out = TAB[:, BA + 512 * k:BA + 512 * k + 512]
+        out = TAB[:, TA + 512 * k:TA + 512 * k + 512]
         if PLAN["evac"][k] == "s":
-            act(out, bank(b), ["BIA"], ["B%d" % b, "base%d" % k], 512, bias=BIA)
+            act(out, bank(b), ["BIA"], ["B%d" % b, "even%d" % k, "base%d" % k], 512, bias=BIA)
         else:
-            ts(out, bank(b), BIA, None, A.add, None, ["BIA"], ["B%d" % b, "base%d" % k], 512)
+            ts(out, bank(b), BIA, None, A.add, None, ["BIA"], ["B%d" % b, "even%d" % k, "base%d" % k], 512)
     BK = ["base%d" % b for b in range(8)]
-    BASE = TAB[:, BA:BA + F]
+    BASE = TAB[:, TA:TA + F]
 
     for k in range(4):
         a = 1024 * k
-        tt(T.CT[:, a:a + 1024], BASE.indirect(T.WL[:, 64 * k:64 * k + 64]), T.ADD[:, a:a + 1024], A.add,
+        tt(T.CT[:, a:a + 1024], BASE.indirect(T.WL[:, 64 * k:64 * k + 64]), TAB[:, BA + a:BA + a + 1024], A.add,
            BK + ["WL"] + ADDK, ["ce%d" % k, "cp%d" % k], GAT * 1024)
-        act(T.X[:, a:a + 1024], BASE.indirect(T.WL[:, 256 + 64 * k:320 + 64 * k]), BK + ["WL"], ["xz"[k // 2], "xb%d" % k], GAT * 1024)
-    for h in range(PLAN["find0"], H):
-        find(h)
+        act(TAB[:, TB + a:TB + a + 1024], BASE.indirect(T.WL[:, 256 + 64 * k:320 + 64 * k]), BK + ["WL"], ["xz"[k // 2], "xb%d" % k, "xg%d" % k], GAT * 1024)
     line[0] = ""
-    dma("y", "ta", TAB[0::2, TA:TA + F], TAB[0::2, BA:BA + F], BK, ["ta"], 64, 8192)
-    dma("y", "ta", TAB[1::2, TB:TB + F], TAB[0::2, BA:BA + F], BK, ["tbo%d" % k for k in range(4)], 64, 8192)
-    for n in PLAN["vat"][1]:
-        load(n)
-    for k in range(4):
+    for h in range(PLAN["find0"], H):
+        lead[0] = PLAN["flead"][h]
+        find(h, True)
+    lead[0] = 0.0
+    for b in range(1, N if PLAN["wsend"] else 0):
+        matrices(b, "lpeer", PLAN["wsend"], (3, 7)[b % 2])
+    for b in range(1, N if PLAN["half"] and not PLAN["wsend"] else 0):
+        L, mats[b] = LW * b, ["lpeer", "la%d" % b, "lb%d" % b]
+        scaled(PLAN["half"][0], T.LALL[:, L:L + 128:2], T.LALL[:, L + 512:L + 640:2], N17, ["lpeer", "lz%d" % b, "N17"], "la%d" % b, 64)
+        scaled(PLAN["half"][1], T.LALL[:, L + 128:L + 512:2], T.LALL[:, L + 640:L + 1024:2], -1.0 / 17, ["lpeer", "lz%d" % b], "lb%d" % b, 192)
+    for n in PLAN["vat"][1].split():
+        k = int(n[1:] or 0)
         a = 1024 * k
-        for r in (5, 7):
-            dma("y", "pp%d" % k, T.CT[r::16, a:a + 1024], T.X[r::16, a:a + 1024], ["xb%d" % k, "cp%d" % k], ["cq%d_%d" % (k, r)], 16, 1024)
-        dma("y", "ta", TAB[1::2, TA + a:TA + a + 1024], T.CT[0::2, a:a + 1024], ["ce%d" % k], ["tao%d" % k], 64, 2048)
-        dma("y", "ta", TAB[0::2, TB + a:TB + a + 1024], T.X[0::2, a:a + 1024], ["xb%d" % k], ["tbe%d" % k], 64, 2048)
-    for n in PLAN["vat"][2]:
-        load(n)
+        if n == "A":
+            dma("y", "ta", TAB[1::2, TA:TA + F], T.CT[0::2, 0:F], ["ce%d" % k for k in range(4)], BK, 64, 8192)
+        elif n[0] == "c":
+            for r in (5, 7):
+                dma("y", "pp%d" % k, T.CT[r::16, a:a + 1024], TAB[r::16, TB + a:TB + a + 1024], ["xb%d" % k, "cp%d" % k], ["cq%d_%d" % (k, r)], 16, 1024)
+        elif n[0] == "b":
+            dma("y", "tb%d" % k, TAB[1::2, TB + a:TB + a + 1024], TAB[0::2, TA + a:TA + a + 1024], ["even%d" % (2 * k), "even%d" % (2 * k + 1)],
+                ["xb%d" % k], 64, 2048)
+        else:
+            load(n[1])
     early = {}
     if PLAN["mode"][0] == "x" and PLAN["gk"]:
         for h in range(H):
-            gk = pick(PLAN["gk"], T.GK, S * h, T.ADD[:, F // H * h:F // H * (h + 1)], T.LT, J * h, S,
+            gk = pick(PLAN["gk"], T.GK, S * h, TAB[:, BA + F // H * h:BA + F // H * (h + 1)], T.LT, J * h, S,
                       ADDK + ["LT%d" % h, PLAN["gkafter"]], "GK%d" % h)
             early[h] = ask(0, h, T.GK, gk, 0.0)
     for k in range(VC if "l" in PLAN["mode"] else 0):
         send_val(k, PLAN["vafter"][k])
-    TBK = [n % k for k in range(4) for n in ("tbe%d", "tbo%d")]
-    TABK = BK + TBK + ["ta"] + ["tao%d" % k for k in range(4)]
+    TABK = BK + ADDK + ["xb%d" % k for k in range(4)]
 
     def judge(rd_, h):
         local = PLAN["mode"][rd_] == "l"
@@ -569,15 +665,20 @@ def rank_program(g, core, T, topo):
         s, c = slice(S * h, S * h + S), slice(C * h, C * h + C)
         k_ = lambda n: "%s%d" % (n, h)
         B = lambda b: "B%d" % b
-        chunks = range(4 // H * h, 4 // H * (h + 1))
+        chunks = range(4 // H * h, 4 // H * (h + 1)) if rd_ == 0 else range(4)
+        w0, w1 = F // H * h, F // H * (h + 1) + (16 if rd_ else 0)
 
         def part(buf, b0, b1, k=None):
             a, b = S * h + C * b0, S * h + C * b1
             return buf[:, a:b] if k is None else buf[:, 4 * a:4 * b] if k == "all" else buf[:, 4 * a + k:4 * b:4]
 
         def terms(items, b0, b1, rd):
-            acc(("h", rd_, h), [(bank(HB, C * b, C), T.LALL[:, b * LW + 512 * d + 128 * t:b * LW + 512 * d + 128 * t + 128], part(buf, b, b + 1, k))
-                                for b in range(b0, b1) for t, d, buf, k in items], rd + own + ["lpeer"] * (b1 > 1), HB, C)
+            for hb in sorted(set(hbank[b0:b1])):
+                bs = [b for b in range(b0, b1) if hbank[b] == hb]
+                acc(("h", rd_, hb), [(bank(hb, C * b, C), T.LALL[:, b * LW + 512 * d + 128 * t:b * LW + 512 * d + 128 * t + 128], part(buf, b, b + 1, k))
+                                     for b in bs for t, d, buf, k in items], rd + [m for b in bs for m in mats[b]], hb, C)
+        cut = PLAN["split"][local]
+        hbank = [W1 if cut and b >= cut and PLAN["hsplit"][local] else HB for b in range(N)]
 
         def digit(q, out, src, mul, rd, key, n):
             if q == "s":
@@ -586,10 +687,10 @@ def rank_program(g, core, T, topo):
                 ts(out, src, mul, 192.0, A.mult, A.add, rd, [key], n / 2)
             return [key]
 
-        gc = pick(PLAN["gc"], T.GC, S * h, T.CT[:, F // H * h:F // H * (h + 1)], T.LT, J * h, S,
-                  [n % k for k in chunks for n in ("ce%d", "cq%d_5", "cq%d_7")] + [k_("LT")], k_("GC"))
+        gc = pick(PLAN["gc"], T.GC, S * h, T.CT[:, w0:w1], T.LT, J * h, S,
+                  [n % k for k in chunks for n in ("ce%d", "cq%d_5", "cq%d_7")] + [k_("LT"), "pad"], k_("GC"))
         if not local:
-            vg, vk = early[h] if rd_ == 0 and early else ask(rd_, h, T.GC, gc, 1.0)
+            vg, vk = early[h] if rd_ == 0 and early else ask(rd_, h, T.GC, gc, 0.0)
         out = bank(W1, 0, C)
         if local:
             mm([(out, T.ID[:], T.K4L[:], True, False)], ["ID", "K4L"], [B(W1)], C)
@@ -600,8 +701,11 @@ def rank_program(g, core, T, topo):
                AK(h) + ["WH"], [B(W1)], C)
         W4 = "W4L" if local else "W4X"
         mm([(out, zb(W4, 12 - 4 * i, 140 - 4 * i), T.GC[:, S * h + i:S * h + S:4], False, i == 3) for i in range(4)], gc + [W4], [B(W1)], C)
-        ts(T.L4[:, C * h:C * h + C], out, KL0 if local else (KX0, KX1)[h], None, A.add, None, ["KL0" if local else k_("KX")], [B(W1), k_("L4")], C)
-        who, dig = PLAN["g4" if local else "g4x"], PLAN["dig" if local else "digx"]
+        if "f" in PLAN["ons"]:
+            act(T.L4[:, C * h:C * h + C], out, ["KL0" if local else k_("KX")], [B(W1), k_("L4")], C, bias=KL0 if local else (KX0, KX1)[h])
+        else:
+            ts(T.L4[:, C * h:C * h + C], out, KL0 if local else (KX0, KX1)[h], None, A.add, None, ["KL0" if local else k_("KX")], [B(W1), k_("L4")], C)
+        who, dig = PLAN["g4"][rd_][h], PLAN["dig" if local else "digx"]
         n, g4 = S // len(who), []
         for k, e in enumerate(who):
             a = S * h + n * k
@@ -613,8 +717,7 @@ def rank_program(g, core, T, topo):
         kinds = [(2, 0), (3, 1)] + ([] if local else [(1, 2)])
         if local:
             vg, vk = lambda b0, b1: part(T.G4, b0, b1, 2), g4
-            gb = pick(PLAN["gb"], T.GB, S * h, TAB[:, TB + F // H * h:TB + F // H * (h + 1)], T.LT, J * h, S,
-                      [n % k for k in chunks for n in ("tbe%d", "tbo%d")] + [k_("LT")], k_("GB"))
+            gb = pick(PLAN["gb"], T.GB, S * h, TAB[:, TB + w0:TB + w1], T.LT, J * h, S, ADDK + ["xb%d" % k for k in chunks] + [k_("LT")], k_("GB"))
             terms([(1, 0, T.GB, None)], 0, N, gb)
             terms([(1, 1, T.RB, None)], 0, N, digit(dig[1], T.RB[:, s], T.GB[:, s], 1.0 / 17, gb, k_("RB"), S))
         m = N // len(dig[2:])
@@ -630,19 +733,31 @@ def rank_program(g, core, T, topo):
                     terms([(t, 1, T.R4, j)], b0, b1,
                           digit(e, part(T.R4, b0, b1, j), part(T.G4, b0, b1, j), 1.0 / 17, rd, "R4%d.%d.%d" % (h, k, j), C * m))
         P1 = T.PB[:, 16 + C * h:16 + C * h + C]
-        for b0, b1, eb in ((0, 1, 4 * h), (1, N, EB)) if PLAN["split"] else ((0, N, EB),):
+        kept, per = (P1, k_("P")), n
+        if PLAN["keep"][local]:
+            out = bank(4 * h, 3 * C, C)
+            mm([(out, zh("DG1"), counts(h, 0, 1, N, N + 1), True, False), (out, zh("DG2"), counts(h, -1, 1, N, N + 1), False, False),
+                (out, T.NID[:], P1, False, True)], ["all0", k_("all"), "AQ0", "DH", "NID", k_("P")], [B(4 * h)], C)
+            act(T.AA[:, c], out, (), [B(4 * h), k_("AA")], C, scale=-1.0, bias=BIG)
+            kept = (T.AA[:, c], k_("AA"))
+        for b0, b1, eb in ((0, cut, 4 * h), (cut, N, EB)) if cut else ((0, N, EB),):
+            gk = g4[C * b0 // per:(C * b1 - 1) // per + 1]
             err, out, n, dg = ("e", rd_, h, b0), bank(eb, C * b0, C * (b1 - b0)), C * (b1 - b0), "DG%d%d" % (h, b0)
             acc(err, [(out, zh("DG1"), counts(h, 0, 1, b0, b1)), (out, zh("DG2"), counts(h, -1, 1, b0, b1))], AK(h) + ["DH"], eb, n, [dg])
             acc(err, [(out, T.RW1[:], part(T.GC, b0, b1))], gc + ["RW1", dg], eb, n)
-            acc(err, [(out, T.RW2[:], part(T.G4, b0, b1, 3))], g4 + ["RW2", dg], eb, n)
-            tt(part(T.PR, b0, b1), bank(HB, C * b0, n), vg(b0, b1), A.mult, vk[:-1] if b1 == 1 and not local else vk, [B(HB), "PR%d%d" % (h, b0)], n)
+            acc(err, [(out, T.RW2[:], part(T.G4, b0, b1, 3))], gk + ["RW2", dg], eb, n)
+            tt(part(T.PR, b0, b1), bank(hbank[b0], C * b0, n), vg(b0, b1), A.mult, gk if local else vk[:-1] if b1 == 1 else vk,
+               [B(hbank[b0]), "PR%d%d" % (h, b0)], n)
             acc(err, [(out, zh("SAMH"), part(T.PR, b0, b1))], ["DH", "PR%d%d" % (h, b0), dg], eb, n)
             for b in range(b0, b1):
                 a = S * h + C * b
-                prev, pk = (P1, k_("P")) if b == 0 else (T.M[:, a - C:a], "m%d%d" % (h, b - 1))
+                prev, pk = kept if b == 0 else (T.M[:, a - C:a], "m%d%d" % (h, b - 1))
                 tt(T.M[:, a:a + C], bank(eb, C * b, C), prev, A.max, [pk], [B(eb), "m%d%d" % (h, b)], C)
-        act(T.AA[:, c], T.M[:, S * h + S - C:S * h + S], ["m%d3" % h], [k_("AA")], C, func=AF.Abs, bias=-BIG / 2)
-        act(T.AB[:, c], T.AA[:, c], [k_("AA")], [k_("AB")], C, func=AF.Abs, bias=-BIG / 2)
+        if PLAN["keep"][local]:
+            act(T.AB[:, c], T.M[:, S * h + S - C:S * h + S], ["m%d3" % h], [k_("AB")], C, func=AF.Abs, bias=-BIG)
+        else:
+            act(T.AA[:, c], T.M[:, S * h + S - C:S * h + S], ["m%d3" % h], [k_("AA")], C, func=AF.Abs, bias=-BIG / 2)
+            act(T.AB[:, c], T.AA[:, c], [k_("AA")], [k_("AB")], C, func=AF.Abs, bias=-BIG / 2)
         ts(T.YB[:, c], T.AB[:, c], 128.0 - 15.0 / 32, 191.0, A.add, A.min, [k_("AB")], [k_("YB")], C)
         if rd_ < R - 1:
             ts(P1, T.YB[:, c], 129.0, 128.0, A.max, A.subtract, [k_("YB")], [k_("P")], C / 2)
@@ -652,8 +767,7 @@ def rank_program(g, core, T, topo):
 
     for rd_ in range(R):
         for h in range(H if rd_ else 0):
-            lead[0] = PLAN["lead"] * (H - 1 - h)
-            find(h)
+            find(h, False, PLAN["keep"][PLAN["mode"][rd_] == "l"])
         for h in range(H):
             lead[0] = PLAN["lead"] * (H - 1 - h)
             judge(rd_, h)

from concourse.bass import DstId, RemoteDMATransfer
from concourse.mybir import AluOpType as A, ActivationFunctionType as AF, AxisListType as AX

F, V, R, N = 4096, 8192, 3, 4
BIG = 4096.0
LW = 8 * 128
H = 2
C = 256 // H
S = N * C
J = S // 16
TA, TB, BA, VA = 0, F, 2 * F, 3 * F + 16
BANKS = ["B%d" % b for b in range(8)]
CUT = [0, 2048, 4096, 6144, 8192]
VC = 4

CY, PE, GAT, FIX, WAKE, HOP, ROW, BW = 0.95e-3, 0.48e-3, 1.56, 0.02, 0.21, 2.2, 0.012, 26e3
PLAN = {"mode": "xxl", "gc": "vs", "gb": "s", "g4": [["sssv", "sssv"], ["sssv", "sssv"], ["svss", "svsv"]], "dig": "vvvvvv", "digx": "vvvvvv", "vo": "vs", "gk": "",
        "evac": "vsvssvss", "first": "kxz", "then": "mp", "llat": 6.0, "vlat": 12.0, "valq": "y", "zadd": "vvvvssss", "direct": 0,
        "flat": 0, "hsplit": [0, 1], "ways": 0,
        "cases": [((0.9, 0.9), 0.24, 0.0, 1.0, 0.35), ((1.3, 1.3), 0.1, 0.0, 0.8, 0.2), ((1.15, 1.15), 0.3, 1.0, 1.2, 0.2),
                  ((1.05, 1.35), 0.1, -0.5, 0.8, 0.2)], "keep": [1, 1], "ons": "", "rnd": "", "half": "ss", "onv": ["W4X", "W4L", "WK", "KT", "KU", "KX0", "KX1", "KL0", "RA1", "RA2"],
        "free": ["SE", "WH", "DG", "DH", "P0", "P1", "wf", "WL", "LT", "AD"], "wsend": "", "flead": [0.0, 0.0], "lfirst": 20.0,
        "find0": 0, "line": "v", "gkafter": "ce3", "split": [1, 2], "passes": 4, "tries": 1200, "slack": 1.0, "lead": 0.0,
        "vat": ["012", "c0 c1 v3 c2 b0 b1 c3 A b2 b3"], "vafter": [[], ["xb3"], ["xb3"], ["xb3"]]}


def _sb(cols, dtype):
    return ("sbuf", [128] + (cols if isinstance(cols, list) else [cols]), dtype)


SCRATCH = {"PS": ("psum", [128, 4096], "float32"), "TAB": _sb(VA + N * V, "bfloat16"), "LALL": _sb(N * LW, "bfloat16")}
SCRATCH.update({n: _sb(4 * H * S, "bfloat16") for n in ("G4", "R4")})
SCRATCH.update({n: _sb(1024, "bfloat16") for n in ("GC", "GB", "GK", "RC", "RB")})
SCRATCH.update({n: _sb(128, "bfloat16") for n in ("TMP", "SAME", "S1K", "ID", "PK", "RW1", "RW2", "SUP", "DGB", "K4L", "NID")})
MATS = (("MA", 128), ("EQ", 128), ("WK", 144), ("W4X", 144), ("W4L", 144), ("SEL", 128), ("WA1", 144), ("WN", 144), ("WP", 144), ("WA4", 144),
        ("DG2", 128), ("DG1", 128), ("SAMH", 128))
AT = {n: sum(w for _, w in MATS[:k]) for k, (n, _) in enumerate(MATS)}
ZW = sum(w for _, w in MATS)
SCRATCH.update({
    "ZB": _sb(ZW, "bfloat16"), "ZH": _sb(ZW, "float16"), "PT": _sb(F, "float16"), "PH": _sb(768, "float16"), "PV": _sb(768, "float16"),
    "HI": _sb(512, "bfloat16"), "LO": _sb(512, "bfloat16"), "IO": _sb(16, "float32"), "E16": _sb(16, "float32"), "EK": _sb(16, "float32"),
    "NAT": _sb(1024, "int32"), "LTI": _sb([4, 8, 16], "int32"), "LTF": _sb([4, 8, 16], "float16"),
    "WF": _sb(512, "float16"), "WL": _sb(512, "uint16"), "PRI": _sb(256, "int32"), "PB": _sb(272, "bfloat16"),
    "Y": _sb(256, "float32"), "WR": _sb(16, "bfloat16"), "WC": _sb(16 * N, "float32"),
    "PI": _sb(4, "int32"), "CI": _sb(4, "int32"), "CF": _sb(24, "float32"), "ONES": _sb(512, "bfloat16"),
    "TMQ": _sb(64, "bfloat16"), "TRI": _sb(256, "bfloat16"), "PM": _sb(64, "bfloat16"),
    "TJ": _sb(J, "float32"), "TBC": _sb(J, "bfloat16"), "TJ4": _sb(128, "float32"), "TJL": _sb(128, "float32"), "K4X": _sb(128, "bfloat16"),
    "AQ": _sb([N + 1, 272], "float16"), "RUN": _sb(256, "float32"), "OFF": _sb(4, "float32"), "CAR": _sb(4, "float32"), "CT": _sb(F + 16, "bfloat16"),
    "LT": _sb(H * J, "uint16"), "L4": _sb(H * 4 * J, "uint16"), "KL": _sb(R * H * 56, "uint16"), "VG": _sb(R * H * 7 * C, "bfloat16"),
    "PR": _sb(1024, "float16"), "M": _sb(1024, "float32"), "AA": _sb(256, "float32"), "AB": _sb(256, "float32"), "YB": _sb(256, "bfloat16"),
})
SEMAPHORES = (["v", "s", "p", "g", "ls", "la", "vall", "n0", "n1", "n2", "lt", "wl", "pri", "x", "z", "pt", "add", "ta"]
              + [n % k for n in ("pp%d", "tb%d", "y%d", "val%d", "rv%d") for k in range(4)]
              + [n % (k, h) for n in ("ka%d_%d", "va%d_%d") for k in range(R) for h in range(H)])


def lanes(topo, src, dsts):
    far = [c for c in dsts if topo.die(c) != topo.die(src)]
    near = [c for c in dsts if c not in far]
    out = {}
    for part, start in ((far, 0), (near, 1)):
        for k, c in enumerate(part):
            e = topo.engines(src, c)[start::2]
            n = 1
            while 2 * n * len(part) <= len(e):
                n *= 2
            out[c] = e[k * n:(k + 1) * n]
    return out


def helpers(topo, cores):
    out = {}
    for c in cores:
        out[c] = [d for d in topo.cores_of(c) if d not in cores and d not in out.values() and topo.die(d) == topo.die(c)][0]
    return out


def dest(topo, c):
    rid, pid, _ = topo.addr(c)
    return DstId(rid=rid, pnc=pid)


def place(ops, succ, pred, prio, span):
    n, back = len(ops), span is not None
    left = [len(p) for p in pred]
    start, end, free, wire, dep = [0.0] * n, [0.0] * n, {}, [], [0.0] * n
    ready = [i for i in range(n) if not left[i]]
    done = []
    while ready:
        e = {i: max(dep[i], free.get(ops[i]["q"], 0.0)) for i in ready}
        j = min(ready, key=lambda i: (e[i] + ops[i]["cost"], i))
        near = [i for i in ready if ops[i]["q"] == ops[j]["q"] and e[i] < e[j] + ops[j]["cost"]]
        k = max(near, key=lambda i: (ops[i]["kind"] == "dma" and not back, round(prio[i] - PLAN["slack"] * e[i], 3), -i))
        o = ops[k]
        start[k] = e[k]
        end[k] = free[o["q"]] = e[k] + o["cost"]
        if not back:
            end[k] += o["lat"]
            if o["wire"]:
                t = end[k] - 0.5
                for a, b in wire:
                    if t + o["wire"] > a and t < b:
                        t = b
                wire = sorted(wire + [(t, t + o["wire"])])
                end[k] = t + o["wire"] + 0.5 + o.get("more", 0.0)
        ready.remove(k)
        done.append(k)
        for i, gap in succ[k]:
            if back:
                dep[i] = max(dep[i], end[k] + (0.0 if gap is None else gap + span[i]))
            else:
                dep[i] = max(dep[i], start[k] if gap is None else end[k] + gap)
            left[i] -= 1
            if not left[i]:
                ready.append(i)
    return done, start, end


def order(ops):
    n = len(ops)
    if n in ORDER:
        return ORDER[n]
    succ, pred = [[] for _ in range(n)], [[] for _ in range(n)]
    for i, o in enumerate(ops):
        for d in o["deps"] | o["after"]:
            gap = None if d not in o["deps"] else 0.0 if o["q"] == ops[d]["q"] == "p" else WAKE
            succ[d].append((i, gap))
            pred[i].append((d, gap))
    tail = [0.0] * n
    for i in range(n - 1, -1, -1):
        tail[i] = ops[i]["cost"] + ops[i]["lat"] + ops[i]["wire"] + ops[i].get("more", 0.0) + max([tail[j] + WAKE for j, _ in succ[i]] + [0.0])
    lead = [o["lead"] for o in ops]
    for i in range(n - 1, -1, -1):
        lead[i] = max([lead[i]] + [lead[j] for j, gap in succ[i] if gap is not None])

    def worth(done):
        total = 0.0
        for speed, wake, hop, move, weight in PLAN["cases"]:
            start, end, free, wire = [0.0] * n, [0.0] * n, {}, []
            for k in done:
                o, t = ops[k], free.get(ops[k]["q"], 0.0)
                for d, gap in pred[k]:
                    t = max(t, start[d] if gap is None else end[d] + (wake if gap else 0.0))
                start[k] = t
                free[o["q"]] = t = t + o["cost"] * (speed[o["q"] == "p"] if o["kind"] == "op" else 1.0)
                t += o["lat"] + (hop if o["kind"] == "send" else 0.0)
                if o["wire"]:
                    t, w = t - 0.5, o["wire"] * move
                    for a, b in wire:
                        if t + w > a and t < b:
                            t = b
                    wire = sorted(wire + [(t, t + w)])
                    t += w + 0.5 + o.get("more", 0.0) * move
                end[k] = t
            total += max(end) * weight
        return total
    best = None
    for _ in range(PLAN["passes"]):
        tail = [tail[i] + lead[i] for i in range(n)]
        done, start, end = place(ops, succ, pred, tail, None)
        if best is None or worth(done) < best[0]:
            best = (worth(done), done, tail)
        tail = place(ops, pred, succ, end, [end[i] - start[i] - ops[i]["cost"] for i in range(n)])[2]
    seed = 1
    for k in range(PLAN["tries"]):
        prio = list(best[2])
        for _ in range(n // (10, 40)[k % 2]):
            seed = (seed * 1103515245 + 12345) % 2 ** 31
            prio[seed // 64 % n] += (seed // 16384 % 201 - 100) * (0.005, 0.015, 0.04)[k % 3]
        done = place(ops, succ, pred, prio, None)[0]
        w = worth(done)
        if w <= best[0]:
            best = (w, done, prio)
    EST.append(best[0])
    ORDER[n] = best[1]
    return best[1]


EST, ORDER = [], {}


def val_at(T, b, k):
    return T.TAB[:, VA + V * b + CUT[k]:VA + V * b + CUT[k + 1]]


def block(cores, at, q):
    return 0 if at == q else 1 + [c for c in cores if c != at].index(q)


def direct(topo, cores, c):
    return [d for d in cores if d != c and topo.die(d) == topo.die(c)] if PLAN["direct"] else []


def helper_program(g, core, T, topo):
    cores = list(T.cores)
    src = [c for c, d in helpers(topo, cores).items() if d == core]
    if not src or "l" not in PLAN["mode"]:
        return
    to = [c for c in cores if c != src[0] and c not in direct(topo, cores, src[0])]
    e = topo.engines(core, to[0])
    got = len(topo.engines(src[0], core)) // (2 if PLAN["direct"] else 1)
    far = [c for c in to if topo.die(c) != topo.die(core)]
    ways = [(far, e[0::2]), ([c for c in to if c not in far], e[1::2])] if PLAN["ways"] else [(to, e)]
    for k in range(VC):
        g.wait_ge(T.sem["rv%d" % k], got)
        g.remote_dma_fused([RemoteDMATransfer(dst_ids=[dest(topo, c) for c in part], dma_engine_mask=sum(1 << j for j in eng),
                                              remote_sem=T.sem["vall"], src=val_at(T, 0, k),
                                              dsts=[val_at(T, block(cores, c, src[0]), k) for c in part]) for part, eng in ways],
                           local_sem=T.sem["ls"])
    g.wait_ge(T.sem["ls"], len(e) * VC)


def rank_program(g, core, T, topo):
    cores = list(T.cores)
    rank = T.rank_of(core)
    if rank is None:
        return helper_program(g, core, T, topo)
    peers = [c for c in cores if c != core]
    learner = [T.rank_of(c) for c in [core] + peers]
    Q = {"v": g.vector, "s": g.scalar, "p": g.tensor, "g": g, "y": g.sync}
    ops, wrs, rds, last, lead = [], {}, {}, {}, [0.0]

    opened, size, issued = {}, {}, {}

    def add(q, kind, rd, wr, cost, lat=0.0, wire=0.0, fixed=False, group=None, **k):
        deps = set()
        for key in rd:
            deps |= set(wrs.get(key, []))
        i, k["name"] = len(ops), (list(wr) + [""])[-2 if wr else -1]
        if group:
            if group not in opened:
                opened[group] = set(wrs.get(wr[0], []) + rds.get(wr[0], []))
                wrs[wr[0]], rds[wr[0]] = [], []
            deps |= opened[group]
            wrs[wr[0]].append(i)
            wr = wr[1:]
        if q != "p":
            for key in [key for key in wr if key in BANKS]:
                deps |= set(wrs.get(key, []) + [d for d in rds.get(key, []) if ops[d]["q"] != q])
                rds.setdefault(key, []).append(i)
            wr = [key for key in wr if key not in BANKS]
        for key in wr:
            deps |= set(wrs.get(key, []) + rds.get(key, []))
        after = set()
        if fixed:
            if fixed in last:
                after.add(last[fixed])
            last[fixed] = i
        for key in wr:
            wrs[key], rds[key] = [i], []
        for key in rd:
            rds.setdefault(key, []).append(i)
        ops.append(dict(k, q=q, kind=kind, deps=deps, after=after, cost=cost, lat=lat, wire=wire, lead=lead[0]))

    line = [PLAN["line"]]

    def op(q, fn, rd, wr, cost):
        add(q, "op", rd, wr, cost, fixed=q in line[0] and wr[-1][:2] not in PLAN["free"] and "line" + q, fn=fn)

    def mm(items, rd, wr, n):
        def fn():
            for it in items:
                end = g.tensor.matmul(*it)
            return end
        op("p", fn, rd, wr, len(items) * max(n, 64) * PE)

    def acc(group, items, rd, b, n, wr=()):
        size[group] = size.get(group, 0) + len(items)

        def fn():
            for it in items:
                issued[group] = issued.get(group, 0) + 1
                end = g.tensor.matmul(*it, issued[group] == 1, issued[group] == size[group])
            return end
        add("p", "op", rd, ["B%d" % b] + list(wr), len(items) * max(n, 64) * PE, group=group, fn=fn)

    def dma(q, sem, out, in_, rd, wr, rows, size):
        add(q, "dma", rd, wr, 0.06, 1.55, rows / 16 * (ROW + size / BW), q, sem=sem, out=out, in_=in_)

    ln = lanes(topo, core, peers)
    arrive = sum(len(lanes(topo, c, [d for d in cores if d != c])[core]) for c in peers)

    def send(tr, sem, n, rd, lands, lat, wire=0.0):
        add("g", "send", rd, lands, 0.3, lat, wire, sem=sem, n=n, tr=tr)

    def exchange(sem, src_of, dst_of, rd, lands, lat, wire=0.0):
        send([(c, ln[c], sem, src_of(c), dst_of(c)) for c in peers], sem, arrive, rd, lands, lat, wire)

    vv, ss = g.vector, g.scalar
    PS, TAB = T.PS, T.TAB

    def bank(b, a=0, n=512):
        return PS[:, 512 * b + a:512 * b + a + n]

    def cyc(n):
        return FIX + max(n, 64) * CY

    def ts(out, in0, s1, s2, o0, o1, rd, wr, n=64):
        if o1 is None:
            op("v", lambda: vv.tensor_scalar(out, in0, s1, None, o0), rd, wr, cyc(n))
        else:
            op("v", lambda: vv.tensor_scalar(out, in0, s1, s2, o0, o1), rd, wr, cyc(n))

    def tt(out, a, b, o, rd, wr, n):
        op("v", lambda: vv.tensor_tensor(out, a, b, o), rd, wr, cyc(n))

    def cp(out, a, rd, wr, n=64):
        op("v", lambda: vv.tensor_copy(out, a), rd, wr, cyc(n))

    def fill(ap, c, wr, n=64):
        op("v", lambda: vv.memset(ap, c), (), wr, cyc(n))

    def act(out, a, rd, wr, n, func=AF.Identity, bias=0.0, scale=1.0):
        op("s", lambda: ss.activation(out, a, func, bias=bias, scale=scale), rd, wr, cyc(n))

    def pick(q, buf, a, win, off, b, n, rd, key):
        cut = [n // 32 * k // len(q) * 2 for k in range(len(q) + 1)]
        for k, e in enumerate(q):
            (cp if e == "v" else act)(buf[:, a + 16 * cut[k]:a + 16 * cut[k + 1]], win.indirect(off[:, b + cut[k]:b + cut[k + 1]]),
                                      rd, ["%s.%d" % (key, k)], GAT * 16 * (cut[k + 1] - cut[k]))
        return ["%s.%d" % (key, k) for k in range(len(q))]

    def sel(out, a, pat, cmp, base, mult, rd, wr, n):
        op("g", lambda: g.affine_select(out, a, pat, cmp, 0.0, base, mult), rd, wr, 0.17 + 2 * n * CY)

    dma("y", "n0", T.NAT[:, 0:256], T.nxt[:], (), ["nat0"], 128, 1024)
    dma("s", "n0", T.NAT[:, 256:512], T.prv[:], (), ["nat1"], 128, 1024)
    dma("y", "n1", T.NAT[:, 512:768], T.rw[:], (), ["nat2"], 128, 1024)
    dma("s", "wl", T.WR[0::2, 1:15], T.w[:], (), ["wr0"], 64, 28)
    dma("s", "wl", T.WR[1::2, 0:14], T.w[:], (), ["wr1"], 64, 28)
    VALK = ["val%d" % k for k in range(VC)]

    def load(n):
        if n == "k":
            dma("y", "n2", T.NAT[:, 768:1024], T.key[:], (), ["nat3"], 128, 1024)
        if n == "l":
            for k, tab in enumerate((T.nxt, T.prv)):
                for h in range(2):
                    dma("y", "lt", T.LTI[:, 2 * k + h], tab[h::2, :], (), ["lti%d" % (2 * k + h)], 128, 512)
        if n == "m":
            for k in range(16):
                a, e = 32 * (k % 4), 32 * (k % 4) + 16 * (k // 4 % 2)
                dma("y", "lt", T.LTF[a:a + 32, k // 4], T.PV[e:e + 16, 256 * (k // 8):256 * (k // 8) + 256], ["PVa"], ["ltf%d" % k], 32, 256)
        if n == "p":
            dma("y", "pri", T.PRI[:], T.pri[:], (), ["PRI"], 128, 1024)
        if n in "xz":
            c = slice(0, 2048) if n == "x" else slice(2048, 4096)
            dma("y", n, TAB[:, TB + c.start:TB + c.stop], T.x[:, c], (), [n], 128, 4096)
        if n in "0123":
            k = int(n)
            dma(PLAN["valq"], VALK[k], val_at(T, 0, k), T.val[:, CUT[k]:CUT[k + 1]], (), [VALK[k]], 128, 2 * (CUT[k + 1] - CUT[k]))
    for n in PLAN["first"]:
        load(n)

    op("g", lambda: g.iota(T.PI[:, 0:1], [[0, 1]], 0, 1), (), ["PI"], 0.14)
    op("g", lambda: g.iota(T.IO[:], [[1, 16]], 0, 0, allow_small_or_imprecise_dtypes=True), (), ["IO"], 0.2)
    ops[-1]["lead"] = 100.0
    fill(T.ONES[:], 1.0, ["ONES"], 256)
    fill(T.ZB[:, 0:AT["DG2"]], 0.0, ["ZB"], AT["DG2"] / 2)

    def zb(n, a=0, b=128, step=1):
        return T.ZB[:, AT[n] + a:AT[n] + b:step]

    def zh(n, a=0, b=128):
        return T.ZH[:, AT[n] + a:AT[n] + b]
    for k, m in enumerate((1, 15, 13, 3)):
        ts(T.CI[:, k:k + 1], T.PI[:, 0:1], m, None, A.bitwise_and, None, ["PI"], ["CI%d" % k])
    cp(T.CF[:, 0:4], T.CI[:, 0:4], ["CI0", "CI1", "CI2", "CI3"], ["CF"])
    ODD, ROW16, KIND, ROW4, C17, EVN, P16, E17, K4, IS2, NEV, NOD, BI0, BIA, R16, RA1, RA2, KX0, KX1, KL0, KT, KU, N17 = [
        T.CF[:, k:k + 1] for k in range(23)]
    ts(T.E16[:], T.IO[:], ROW16, None, A.is_equal, None, ["IO", "CF"], ["E16"])
    ts(T.EK[:], T.IO[:], KIND, None, A.is_equal, None, ["IO", "CF"], ["EK"])
    ts(IS2, ROW4, 2.0, None, A.is_equal, None, ["CF"], ["IS2"])
    ts(K4, ROW4, float(F), float(BA), A.mult, A.min, ["CF"], ["K4"])
    R15 = T.E16[:, 15:16]

    def col(out, a, scale, bias, rd, key):
        if key in PLAN["onv"]:
            keep, line[0] = line[0], ""
            ts(out, a, scale, bias, A.mult, A.add, rd, [key])
            line[0] = keep
        else:
            act(out, a, rd, [key], 64, scale=scale, bias=bias)
    col(C17, ODD, 16.0, 1.0, ["CF"], "C17")
    col(EVN, ODD, -1.0, 1.0, ["CF"], "EVN")
    col(E17, ODD, -1.0 / 17, 1.0 / 17, ["CF"], "E17")
    col(NEV, ODD, 1.0, -1.0, ["CF"], "NEV")
    col(NOD, ODD, -1.0, 0.0, ["CF"], "NOD")
    col(P16, ROW16, 16.0, 16.0, ["CF"], "P16")
    col(R16, R15, 16.0, 0.0, ["E16"], "R16")
    col(BI0, T.E16[:, 3:4], 2048.0, 0.0, ["E16"], "BI0")
    col(BIA, T.E16[:, 7:8], 2048.0, BI0, ["BI0"], "BIA")
    col(RA1, T.EK[:, 9:10], 1.0 / 16, 0.0, ["EK"], "RA1")
    col(RA2, T.E16[:, 5:6], -BIG, RA1, ["E16", "RA1"], "RA2")
    fill(T.PB[:, 0:16], 0.0, ["PB0"])
    fill(T.AQ[:, :, 0:16], 1026.0, ["AQ0"])
    fill(TAB[:, 3 * F:VA], 0.0, ["gap"])
    fill(T.CT[:, F:F + 16], 0.0, ["pad"])
    for b in range(0 if PLAN["rnd"] else N):
        act(T.OFF[:, b:b + 1], T.ONES[:, 0:1], ["ONES"], ["OFF"], 64, scale=1026.5 - (learner[b] + 1) / 4 + 1.0 / 2048)
    zero = []
    for k, q in enumerate(PLAN["zadd"]):
        zero.append("ADD%d" % k)
        if q == "v":
            ts(TAB[:, BA + 512 * k:BA + 512 * k + 512], T.ONES[:], T.E16[:, 5:6], None, A.mult, None, ["ONES", "E16"], [zero[-1]], 256)
        else:
            act(TAB[:, BA + 512 * k:BA + 512 * k + 512], T.ONES[:], ["ONES", "E16"], [zero[-1]], 512, scale=T.E16[:, 5:6])
    sel(T.TMQ[:], T.ONES[:, 0:64], [[-2, 64]], A.is_ge, 0, 1, ["ONES"], ["TMQ"], 64)
    sel(T.PM[:], T.TMQ[:], [[2, 64]], A.is_ge, 1, -1, ["TMQ"], ["PM"], 64)
    sel(zb("SEL", 1, 128, 2), T.ONES[:, 0:64], [[-1, 8], [-8, 8]], A.is_equal, 0, 1, ["ONES", "ZB"], ["SEL"], 64)
    op("g", lambda: g.affine_select(zb("SEL", 3, 128, 4), zb("SEL", 3, 128, 4), [[-1, 8], [-16, 4]], A.not_equal, -1.0, 0, 1), (), ["SEL"], 0.25)
    cp(zh("SEL"), zb("SEL"), ["SEL"], ["SELH"])
    sel(T.ID[:], T.ONES[:, 0:128], [[-1, 128]], A.is_equal, 0, 1, ["ONES"], ["ID"], 128)
    sel(T.TMP[:], T.ONES[:, 0:128], [[-16, 8], [0, 16]], A.is_ge, 0, 1, ["ONES"], ["TMP"], 128)
    sel(T.SAME[:], T.TMP[:], [[16, 8], [0, 16]], A.is_ge, 15, -1, ["TMP"], ["SAME"], 128)
    op("g", lambda: g.iota(T.TJ[:], [[0, N], [256, J // N]], 0, 0, allow_small_or_imprecise_dtypes=True), (), ["TJ"], 0.2)
    act(zb("MA", 0, 128, 2), T.PM[:], ["PM", "ZB"], ["MA"], 64)
    act(T.PK[:], zb("MA"), ["MA", "C17"], ["PK"], 128, scale=C17)
    G0 = T.SAME[:, 0::16]

    def mark(n, a, scale, rd, key):
        col(zb(n, a, min(a + 128, dict(MATS)[n]), 16), G0, scale, 0.0, ["SAME", "ZB"] + rd, key)
    mark("EQ", 1, NEV, ["NEV"], "EQ0")
    mark("EQ", 3, NOD, ["NOD"], "EQ1")
    act(T.S1K[:], T.SAME[:], ["SAME"], ["S1K"], 128, scale=1.0 / 1024)
    for k, (s, cmp) in enumerate(((1, A.is_ge), (-1, A.is_gt))):
        sel(T.TRI[:, 128 * k:128 * k + 128], T.S1K[:], [[s, 128]], cmp, 0, -s, ["S1K"], ["tri%d" % k], 128)
    sel(T.SUP[:], T.SAME[:], [[1, 128]], A.is_equal, -1, -1, ["SAME"], ["SUP"], 128)
    act(T.TBC[:], T.TJ[:], ["TJ", "P16"], ["TBC"], 64, bias=P16)
    for n, a in (("WN", 15), ("WA1", 14), ("WA4", 11)):
        mark(n, a, -1.0, [], n + "n")
    for n in ("WP", "WA1", "WA4"):
        mark(n, 15, R16, ["R16"], n + "p")
    cp(zh("WA1", 0, 576), zb("WA1", 0, 576), ["WNn", "WA1n", "WA4n", "WPp", "WA1p", "WA4p"], ["WH"], 288)
    mark("WK", 15, T.EK[:, 13:14], ["EK"], "WK")
    for n, kinds in (("W4X", (1, 5, None, 1)), ("W4L", (1, 5, 13, 1))):
        if n[2].lower() in PLAN["mode"]:
            for k, c in enumerate(kinds):
                if c:
                    mark(n, 12 + k, T.EK[:, c:c + 1], ["EK"], n)
    tt(T.DGB[:], T.ID[:], T.SUP[:], A.subtract, ["ID", "SUP"], ["DGB"], 256)
    act(zb("DG1"), T.DGB[:], ["DGB"], ["DG1"], 128, scale=2 * BIG)
    act(zb("DG2"), zb("WP", 15, 143), ["WPp"], ["DG2"], 128, scale=-BIG / 8)
    act(zb("SAMH"), T.SAME[:], ["SAME"], ["SAMH"], 128, scale=1.0 / 16)
    cp(zh("DG2", 0, 384), zb("DG2", 0, 384), ["DG1", "DG2", "SAMH"], ["DH"], 192)
    if any(PLAN["keep"]):
        act(T.NID[:], T.ID[:], ["ID"], ["NID"], 128, scale=-1.0)
    act(T.RW1[:], T.SAME[:], ["SAME", "RA1"], ["RW1"], 128, scale=RA1)
    act(T.RW2[:], T.SAME[:], ["SAME", "RA2"], ["RW2"], 128, scale=RA2)
    if "x" in PLAN["mode"]:
        op("g", lambda: g.iota(T.TJ4[:], [[0, N], [64, 32]], 16, 0, allow_small_or_imprecise_dtypes=True), (), ["TJ4"], 0.4)
        col(KT, ROW16, 4.0, -8.0, ["CF"], "KT")
        col(KU, KT, IS2, 0.0, ["KT", "IS2"], "KU")
        act(T.K4X[:], T.TJ4[:], ["TJ4", "KU"], ["K4X"], 128, scale=IS2, bias=KU)
        for h, a in enumerate((KX0, KX1)):
            col(a, IS2, float(TB - BA + F // H * h), K4, ["IS2", "K4"], "KX%d" % h)
    if "l" in PLAN["mode"]:
        col(KL0, IS2, float(VA - BA), K4, ["IS2", "K4"], "KL0")
        op("g", lambda: g.iota(T.TJL[:], [[V, N], [0, 32]], 0, 0, allow_small_or_imprecise_dtypes=True), (), ["TJL"], 0.4)
        act(T.K4L[:], T.TJL[:], ["TJL", "IS2"], ["K4L"], 128, scale=IS2)

    MAGIC = 1.5 * 2 ** 28
    ts(T.PH[:, 0:512], T.NAT[:, 0:512], MAGIC, -MAGIC, A.add, A.add, ["nat0", "nat1"], ["PHa"], 512)
    ts(T.PV[:, 0:512], T.NAT[:, 0:512], -2048.0, None, A.add, None, ["nat0", "nat1"], ["PVa"], 512)
    ts(T.PH[:, 512:768], T.NAT[:, 512:768], MAGIC, -MAGIC, A.add, A.add, ["nat2"], ["PHb"], 256)
    cp(T.PV[:, 512:768], T.NAT[:, 512:768], ["nat2"], ["PVb"], 256)
    for r in (0, 2, 1, 3, 4, 5):
        n, k = ("PH", "PV")[r % 2], r // 2
        dma("y", "pt", T.PT[8 * r:8 * r + 8, :], T[n][:, 256 * k:256 * k + 256], [n + "aab"[k]], ["pt%d" % r], 128, 512)
    for n in PLAN["then"]:
        load(n)
    ts(T.HI[:], T.NAT[:, 512:1024], MAGIC, -MAGIC, A.add, A.add, ["nat2", "nat3"], ["HI"], 512)
    tt(T.LO[:], T.NAT[:, 512:1024], T.HI[:], A.subtract, ["nat2", "nat3", "HI"], ["LO"], 1024)
    for r in range(4):
        n, k = ("HI", "LO")[r % 2], r // 2
        dma("y", "add", TAB[2 * r + 9::16, BA:BA + F], T[n][:, 256 * k:256 * k + 256], [n] + zero, ["add%d" % r], 128, 512)
    ADDK = zero + ["add%d" % r for r in range(4)]
    for n in PLAN["vat"][0]:
        load(n)

    act(T.WC[:, 1:14], T.WR[:, 1:14], ["wr0", "wr1"], ["WC"], 64)
    act(T.WC[:, 14:16], T.WC[:, 5:13:7], ["WC", "EVN"], ["W0"], 64, scale=EVN)
    mats = {}

    def scaled(q, out, a, by, rd, key, n):
        rd = rd + [{"s": "xg3", "v": "ce3"}[q]]
        if q == "s":
            act(out, a, rd, [key], n, scale=by)
        else:
            ts(out, a, by, None, A.mult, None, rd, [key], n / 2)

    def matrices(b, src, who, at):
        L, W = LW * b, 16 * b
        la, lo, le = ["la%d%d" % (b, t) for t in range(4)], ["lo%d%d" % (b, t) for t in range(4)], "le%d" % b
        for t, a in enumerate((14, 3, 6, 1)):
            scaled(who[0], T.LALL[:, L + 128 * t:L + 128 * t + 128], zb("MA"), T.WC[:, W + a:W + a + 1], ["MA", src], la[t], 128)
        for t, a in enumerate((15, 10, 13, 8)):
            scaled(who[1], T.LALL[:, L + 513 + 128 * t:L + 640 + 128 * t:2], T.PM[:], T.WC[:, W + a:W + a + 1], ["PM", src], lo[t], 64)
        scaled(who[2], T.LALL[:, L + 512:L + 1024:2], T.LALL[:, L:L + 512:2], -17.0, la, le, 256)
        mm([(bank(at, 0, 128), zb("EQ"), T.LALL[:, L + 512 + 128 * t:L + 640 + 128 * t], t == 0, False) for t in range(4)]
           + [(bank(at, 0, 128), T.ID[:], T.LALL[:, L + 512:L + 640], False, True)], ["EQ0", "EQ1", "ID", le] + lo, ["B%d" % at], 128)
        (act if who[3] == "s" else cp)(T.LALL[:, L + 512:L + 640], bank(at, 0, 128), (), ["B%d" % at, lo[0], le], 128)
        mats[b] = la + lo + [le]
    PTK = ["pt%d" % r for r in range(6)]
    if PLAN["wsend"]:
        exchange("la", lambda c: T.WC[:, 1:16], lambda c: T.WC[:, 16 * block(cores, c, core) + 1:16 * block(cores, c, core) + 16],
                 ["W0"], ["lpeer"], PLAN["llat"])
        ops[-1]["lead"] = PLAN["lfirst"]
        matrices(0, "W0", "ssss", 7)
    elif PLAN["half"]:
        matrices(0, "W0", "ssss", 7)
        exchange("la", lambda c: T.LALL[:, 512:LW], lambda c: T.LALL[:, LW * block(cores, c, core) + 512:LW * (block(cores, c, core) + 1)],
                 mats[0], ["lpeer"], PLAN["llat"], 1.0)
        ops[-1]["lead"] = PLAN["lfirst"]
        col(N17, ODD, 1.0 / 17, -1.0 / 17, ["CF"], "N17")
        for b in range(1, N):
            op("g", lambda b=b: g.iota(T.LALL[:, LW * b:LW * b + 512], [[0, 512]], 0, 0, allow_small_or_imprecise_dtypes=True), (), ["lz%d" % b], 1.2)
    else:
        matrices(0, "W0", "ssss", 7)
        exchange("la", lambda c: T.LALL[:, 0:LW], lambda c: T.LALL[:, LW * block(cores, c, core):LW * (block(cores, c, core) + 1)],
                 mats[0], ["lpeer"], PLAN["llat"], 2.0)
        ops[-1]["lead"] = PLAN["lfirst"]
        mats.update({b: ["lpeer"] for b in range(1, N)})

    def send_val(k, rd):
        mine, near = helpers(topo, cores)[core], direct(topo, cores, core)
        e = topo.engines(core, mine)
        total = sum(VC * len(e) // (2 if PLAN["ways"] or core in direct(topo, cores, c) else 1) for c in peers)
        tr = [(mine, e[0::2] if near else e, "rv%d" % k, val_at(T, 0, k), val_at(T, 0, k))]
        tr += [(c, e[1::2], "vall", val_at(T, 0, k), val_at(T, block(cores, c, core), k)) for c in near]
        send(tr, "vall", total, [VALK[k]] + ["sent%d" % (k - 1)] * (k > 0) + rd, ["sent%d" % k],
             2.0, 8 * len(tr) * (ROW + 2 * (CUT[k + 1] - CUT[k]) / BW))
        ops[-1]["chain"] = k < VC - 1
        ops[-1]["more"] = PLAN["vlat"] * (k == VC - 1)
    VALL = VALK + ["sent%d" % (VC - 1)]

    if "l" in PLAN["first"] + PLAN["then"]:
        ts(T.LTF[:], T.LTI[:], -2048.0, None, A.add, None, ["lti%d" % k for k in range(4)], ["LTF"], 512)
    for b in range(8):
        op("v", lambda b=b: vv.transpose(T.WF[:, b::8], T.LTF[:, :, b, :]), ["LTF"] + ["ltf%d" % k for k in range(16)], ["wf%d" % b], cyc(64))
    ts(T.WL[:], T.WF[:], 2048.0, None, A.add, None, ["wf%d" % b for b in range(8)], ["WL"], 256)

    def counts(h, a, step, b0=0, b1=N):
        return T.AQ[:, b0:b1, 16 + C * h + a:16 + C * h + C + min(a, 0):step]

    def AK(h):
        return ["a%d%d" % (h, b) for b in range(N)] + (["AQ0"] if h == 0 else ["a%d%d" % (h - 1, b) for b in range(N)])

    def find(h, first=False, keep=PLAN["keep"][PLAN["mode"][0] == "l"]):
        W0, W1 = 4 * h, 4 * h + 1
        a = 16 + C * h
        mm([(bank(W0, 0, C), T.TRI[:, 0:128], T.PB[:, a:a + C], True, False),
            (bank(W0, 0, C), T.TRI[:, 128:256], T.PB[:, a - 1:a - 1 + C], False, True)],
           ["P%d" % h, "P%d" % (h - 1) if h else "PB0", "tri0", "tri1"], ["B%d" % W0], C)
        run = T.RUN[:, C * h:C * h + C]
        if PLAN["rnd"] or h == 0 or keep:
            op("v", lambda: vv.tensor_tensor_scan(run, T.ONES[:, 0:C], bank(W0, 0, C), T.RUN[:, C * h - 1:C * h] if h else 0.0, A.mult, A.add),
               ["ONES"] + ["RUN0"] * h, ["B%d" % W0, "RUN%d" % h], cyc(C))
        if keep:
            act(T.AQ[:, N, a:a + C], run, ["RUN%d" % h], ["all%d" % h], C, scale=4.0, bias=1025.5 + 1.0 / 512)
        if not PLAN["rnd"] and h == 0:
            act(T.CAR[:, 0:4], T.OFF[:, 0:4], ["RUN0", "OFF"], ["CAR"], 64, bias=T.RUN[:, C - 1:C])
        for b in range(N):
            off = 1026.5 - (learner[b] + 1) / 4 + 1.0 / 2048
            if not PLAN["rnd"]:
                op("v", lambda b=b, off=off: vv.tensor_tensor_scan(T.AQ[:, b, a:a + C], T.ONES[:, 0:C], bank(W0, 0, C),
                                                                   T.CAR[:, b:b + 1] if h else off, A.mult, A.add),
                   ["ONES"] + ["CAR"] * h, ["B%d" % W0, "a%d%d" % (h, b)], cyc(C))
            elif PLAN["rnd"][b] == "s":
                act(T.AQ[:, b, a:a + C], run, ["RUN%d" % h], ["a%d%d" % (h, b)], C, bias=off)
            else:
                ts(T.AQ[:, b, a:a + C], run, off, None, A.add, None, ["RUN%d" % h], ["a%d%d" % (h, b)], C)
        out = bank(W1, 0, J)
        mm([(out, T.ID[:], T.TBC[:], True, False)], ["ID", "TBC"], ["B%d" % W1], J)
        mm([(out, zh("WA1", 14 - i, 142 - i), counts(h, i, 16), False, False) for i in range(15)]
           + [(out, zh("WN"), counts(h, 15, 16), False, False), (out, zh("WP", 15, 143), counts(h, -1, 16), False, True)],
           AK(h) + ["WH"], ["B%d" % W1], J)
        if first or "t" not in PLAN["ons"]:
            ts(T.LT[:, J * h:J * h + J], out, float(F // H - 1), None, A.min, None, (), ["B%d" % W1, "LT%d" % h])
        else:
            act(T.LT[:, J * h:J * h + J], out, (), ["B%d" % W1, "LT%d" % h], 64)

    for h in range(H):
        cp(T.PB[:, 16 + C * h:16 + C * h + C], T.PRI[:, C * h:C * h + C], ["PRI"], ["P%d" % h], C)
    for h in range(PLAN["find0"]):
        find(h, True)

    def ask(rd_, h, src, rd, less):
        e, W0, Jq = rd_ * H + h, 4 * h, J // N
        K0, V0 = 7 * Jq * e, 7 * C * e
        mm([(bank(W0, 0, J), zb("WK", 15 - i, 143 - i), src[:, S * h + i:S * h + S:16], i == 0, i == 15) for i in range(16)],
           rd + ["WK"], ["B%d" % W0], J)
        if "k" in PLAN["ons"]:
            act(T.KL[:, K0 + 3 * Jq:K0 + 7 * Jq], bank(W0, 0, J), (), ["B%d" % W0, "KL%d" % e], 64, bias=-less)
        else:
            ts(T.KL[:, K0 + 3 * Jq:K0 + 7 * Jq], bank(W0, 0, J), -less, None, A.add, None, (), ["B%d" % W0, "KL%d" % e])
        exchange("ka%d_%d" % (rd_, h), lambda d: T.KL[:, K0 + Jq * (3 + block(cores, core, d)):K0 + Jq * (4 + block(cores, core, d))],
                 lambda d: T.KL[:, K0 + Jq * (block(cores, d, core) - 1):K0 + Jq * block(cores, d, core)], ["KL%d" % e], ["KIN%d" % e], HOP)
        vo = pick(PLAN["vo"], T.VG, V0, TAB[:, VA:VA + V], T.KL, K0, S, VALK + ["KIN%d" % e, "KL%d" % e], "VO%d" % e)
        exchange("va%d_%d" % (rd_, h), lambda d: T.VG[:, V0 + C * (block(cores, core, d) - 1):V0 + C * block(cores, core, d)],
                 lambda d: T.VG[:, V0 + C * (3 + block(cores, d, core)):V0 + C * (4 + block(cores, d, core))], vo, ["VG%d" % e], HOP + 0.3)
        return lambda b0, b1: T.VG[:, V0 + (3 + b0) * C:V0 + (3 + b1) * C], vo + ["VG%d" % e]

    line[0] = "vsp"
    banks, ahead = ((range(8), 8), ((2, 3, 4, 5, 6, 7, 0, 1), 6), ((2, 3, 6, 7, 0, 4, 1, 5), 4))[PLAN["find0"]]

    def pack(k):
        mm([(bank(banks[k]), T.PK[:], TAB[:, TB + 512 * k:TB + 512 * k + 512], True, False)], ["PK", "xz"[k // 4]], ["B%d" % banks[k]], 512)
    for k in range(ahead):
        pack(k)
    for k, b in enumerate(banks):
        mm([(bank(b), T.ZH[0:48, AT["SEL"]:AT["SEL"] + 128], T.PT[0:48, 512 * k:512 * k + 512], False, True)], ["SELH"] + PTK, ["B%d" % b], 512)
        if k + ahead < 8:
            pack(k + ahead)
        out = TAB[:, TA + 512 * k:TA + 512 * k + 512]
        if PLAN["evac"][k] == "s":
            act(out, bank(b), ["BIA"], ["B%d" % b, "even%d" % k, "base%d" % k], 512, bias=BIA)
        else:
            ts(out, bank(b), BIA, None, A.add, None, ["BIA"], ["B%d" % b, "even%d" % k, "base%d" % k], 512)
    BK = ["base%d" % b for b in range(8)]
    BASE = TAB[:, TA:TA + F]

    for k in range(4):
        a = 1024 * k
        tt(T.CT[:, a:a + 1024], BASE.indirect(T.WL[:, 64 * k:64 * k + 64]), TAB[:, BA + a:BA + a + 1024], A.add,
           BK + ["WL"] + ADDK, ["ce%d" % k, "cp%d" % k], GAT * 1024)
        act(TAB[:, TB + a:TB + a + 1024], BASE.indirect(T.WL[:, 256 + 64 * k:320 + 64 * k]), BK + ["WL"], ["xz"[k // 2], "xb%d" % k, "xg%d" % k], GAT * 1024)
    line[0] = ""
    for h in range(PLAN["find0"], H):
        lead[0] = PLAN["flead"][h]
        find(h, True)
    lead[0] = 0.0
    for b in range(1, N if PLAN["wsend"] else 0):
        matrices(b, "lpeer", PLAN["wsend"], (3, 7)[b % 2])
    for b in range(1, N if PLAN["half"] and not PLAN["wsend"] else 0):
        L, mats[b] = LW * b, ["lpeer", "la%d" % b, "lb%d" % b]
        scaled(PLAN["half"][0], T.LALL[:, L:L + 128:2], T.LALL[:, L + 512:L + 640:2], N17, ["lpeer", "lz%d" % b, "N17"], "la%d" % b, 64)
        scaled(PLAN["half"][1], T.LALL[:, L + 128:L + 512:2], T.LALL[:, L + 640:L + 1024:2], -1.0 / 17, ["lpeer", "lz%d" % b], "lb%d" % b, 192)
    for n in PLAN["vat"][1].split():
        k = int(n[1:] or 0)
        a = 1024 * k
        if n == "A":
            dma("y", "ta", TAB[1::2, TA:TA + F], T.CT[0::2, 0:F], ["ce%d" % k for k in range(4)], BK, 64, 8192)
        elif n[0] == "c":
            for r in (5, 7):
                dma("y", "pp%d" % k, T.CT[r::16, a:a + 1024], TAB[r::16, TB + a:TB + a + 1024], ["xb%d" % k, "cp%d" % k], ["cq%d_%d" % (k, r)], 16, 1024)
        elif n[0] == "b":
            dma("y", "tb%d" % k, TAB[1::2, TB + a:TB + a + 1024], TAB[0::2, TA + a:TA + a + 1024], ["even%d" % (2 * k), "even%d" % (2 * k + 1)],
                ["xb%d" % k], 64, 2048)
        else:
            load(n[1])
    early = {}
    if PLAN["mode"][0] == "x" and PLAN["gk"]:
        for h in range(H):
            gk = pick(PLAN["gk"], T.GK, S * h, TAB[:, BA + F // H * h:BA + F // H * (h + 1)], T.LT, J * h, S,
                      ADDK + ["LT%d" % h, PLAN["gkafter"]], "GK%d" % h)
            early[h] = ask(0, h, T.GK, gk, 0.0)
    for k in range(VC if "l" in PLAN["mode"] else 0):
        send_val(k, PLAN["vafter"][k])
    TABK = BK + ADDK + ["xb%d" % k for k in range(4)]

    def judge(rd_, h):
        local = PLAN["mode"][rd_] == "l"
        W1, HB, EB = 4 * h + 1, 4 * h + 2, 4 * h + 3
        s, c = slice(S * h, S * h + S), slice(C * h, C * h + C)
        k_ = lambda n: "%s%d" % (n, h)
        B = lambda b: "B%d" % b
        chunks = range(4 // H * h, 4 // H * (h + 1)) if rd_ == 0 else range(4)
        w0, w1 = F // H * h, F // H * (h + 1) + (16 if rd_ else 0)

        def part(buf, b0, b1, k=None):
            a, b = S * h + C * b0, S * h + C * b1
            return buf[:, a:b] if k is None else buf[:, 4 * a:4 * b] if k == "all" else buf[:, 4 * a + k:4 * b:4]

        def terms(items, b0, b1, rd):
            for hb in sorted(set(hbank[b0:b1])):
                bs = [b for b in range(b0, b1) if hbank[b] == hb]
                acc(("h", rd_, hb), [(bank(hb, C * b, C), T.LALL[:, b * LW + 512 * d + 128 * t:b * LW + 512 * d + 128 * t + 128], part(buf, b, b + 1, k))
                                     for b in bs for t, d, buf, k in items], rd + [m for b in bs for m in mats[b]], hb, C)
        cut = PLAN["split"][local]
        hbank = [W1 if cut and b >= cut and PLAN["hsplit"][local] else HB for b in range(N)]

        def digit(q, out, src, mul, rd, key, n):
            if q == "s":
                act(out, src, rd, [key], n, scale=mul, bias=192.0)
            else:
                ts(out, src, mul, 192.0, A.mult, A.add, rd, [key], n / 2)
            return [key]

        gc = pick(PLAN["gc"], T.GC, S * h, T.CT[:, w0:w1], T.LT, J * h, S,
                  [n % k for k in chunks for n in ("ce%d", "cq%d_5", "cq%d_7")] + [k_("LT"), "pad"], k_("GC"))
        if not local:
            vg, vk = early[h] if rd_ == 0 and early else ask(rd_, h, T.GC, gc, 0.0)
        out = bank(W1, 0, C)
        if local:
            mm([(out, T.ID[:], T.K4L[:], True, False)], ["ID", "K4L"], [B(W1)], C)
        else:
            mm([(out, T.ID[:], T.K4X[:], True, False)], ["ID", "K4X"], [B(W1)], C)
            mm([(out, zh("WA4", 9 - 4 * i, 137 - 4 * i), counts(h, i, 4), False, False) for i in range(3)]
               + [(out, zh("WN", 1, 129), counts(h, 3, 4), False, False), (out, zh("WP", 13, 141), counts(h, -1, 4), False, False)],
               AK(h) + ["WH"], [B(W1)], C)
        W4 = "W4L" if local else "W4X"
        mm([(out, zb(W4, 12 - 4 * i, 140 - 4 * i), T.GC[:, S * h + i:S * h + S:4], False, i == 3) for i in range(4)], gc + [W4], [B(W1)], C)
        if "f" in PLAN["ons"]:
            act(T.L4[:, C * h:C * h + C], out, ["KL0" if local else k_("KX")], [B(W1), k_("L4")], C, bias=KL0 if local else (KX0, KX1)[h])
        else:
            ts(T.L4[:, C * h:C * h + C], out, KL0 if local else (KX0, KX1)[h], None, A.add, None, ["KL0" if local else k_("KX")], [B(W1), k_("L4")], C)
        who, dig = PLAN["g4"][rd_][h], PLAN["dig" if local else "digx"]
        n, g4 = S // len(who), []
        for k, e in enumerate(who):
            a = S * h + n * k
            g4.append("G4%d.%d" % (h, k))
            (cp if e == "v" else act)(T.G4[:, 4 * a:4 * (a + n)], TAB[:, 0:VA + N * V if local else VA].indirect(T.L4[:, a // 4:(a + n) // 4]),
                                      TABK + ["gap", k_("L4")] + (VALL if local else []), [g4[k]], GAT * 4 * n)
        terms([(0, 0, T.GC, None)], 0, N, gc)
        terms([(0, 1, T.RC, None)], 0, N, digit(dig[0], T.RC[:, s], T.GC[:, s], E17, gc + ["E17"], k_("RC"), S))
        kinds = [(2, 0), (3, 1)] + ([] if local else [(1, 2)])
        if local:
            vg, vk = lambda b0, b1: part(T.G4, b0, b1, 2), g4
            gb = pick(PLAN["gb"], T.GB, S * h, TAB[:, TB + w0:TB + w1], T.LT, J * h, S, ADDK + ["xb%d" % k for k in chunks] + [k_("LT")], k_("GB"))
            terms([(1, 0, T.GB, None)], 0, N, gb)
            terms([(1, 1, T.RB, None)], 0, N, digit(dig[1], T.RB[:, s], T.GB[:, s], 1.0 / 17, gb, k_("RB"), S))
        m = N // len(dig[2:])
        for k, e in enumerate(dig[2:]):
            b0, b1 = m * k, m * k + m
            rd = g4[C * b0 // n:(C * b1 - 1) // n + 1]
            terms([(t, 0, T.G4, j) for t, j in kinds], b0, b1, rd)
            if PLAN["flat"]:
                terms([(t, 1, T.R4, j) for t, j in kinds], b0, b1,
                      digit(e, part(T.R4, b0, b1, "all"), part(T.G4, b0, b1, "all"), 1.0 / 17, rd, "R4%d.%d" % (h, k), C * m * 4))
            else:
                for t, j in kinds:
                    terms([(t, 1, T.R4, j)], b0, b1,
                          digit(e, part(T.R4, b0, b1, j), part(T.G4, b0, b1, j), 1.0 / 17, rd, "R4%d.%d.%d" % (h, k, j), C * m))
        P1 = T.PB[:, 16 + C * h:16 + C * h + C]
        kept, per = (P1, k_("P")), n
        if PLAN["keep"][local]:
            out = bank(4 * h, 3 * C, C)
            mm([(out, zh("DG1"), counts(h, 0, 1, N, N + 1), True, False), (out, zh("DG2"), counts(h, -1, 1, N, N + 1), False, False),
                (out, T.NID[:], P1, False, True)], ["all0", k_("all"), "AQ0", "DH", "NID", k_("P")], [B(4 * h)], C)
            act(T.AA[:, c], out, (), [B(4 * h), k_("AA")], C, scale=-1.0, bias=BIG)
            kept = (T.AA[:, c], k_("AA"))
        for b0, b1, eb in ((0, cut, 4 * h), (cut, N, EB)) if cut else ((0, N, EB),):
            gk = g4[C * b0 // per:(C * b1 - 1) // per + 1]
            err, out, n, dg = ("e", rd_, h, b0), bank(eb, C * b0, C * (b1 - b0)), C * (b1 - b0), "DG%d%d" % (h, b0)
            acc(err, [(out, zh("DG1"), counts(h, 0, 1, b0, b1)), (out, zh("DG2"), counts(h, -1, 1, b0, b1))], AK(h) + ["DH"], eb, n, [dg])
            acc(err, [(out, T.RW1[:], part(T.GC, b0, b1))], gc + ["RW1", dg], eb, n)
            acc(err, [(out, T.RW2[:], part(T.G4, b0, b1, 3))], gk + ["RW2", dg], eb, n)
            tt(part(T.PR, b0, b1), bank(hbank[b0], C * b0, n), vg(b0, b1), A.mult, gk if local else vk[:-1] if b1 == 1 else vk,
               [B(hbank[b0]), "PR%d%d" % (h, b0)], n)
            acc(err, [(out, zh("SAMH"), part(T.PR, b0, b1))], ["DH", "PR%d%d" % (h, b0), dg], eb, n)
            for b in range(b0, b1):
                a = S * h + C * b
                prev, pk = kept if b == 0 else (T.M[:, a - C:a], "m%d%d" % (h, b - 1))
                tt(T.M[:, a:a + C], bank(eb, C * b, C), prev, A.max, [pk], [B(eb), "m%d%d" % (h, b)], C)
        if PLAN["keep"][local]:
            act(T.AB[:, c], T.M[:, S * h + S - C:S * h + S], ["m%d3" % h], [k_("AB")], C, func=AF.Abs, bias=-BIG)
        else:
            act(T.AA[:, c], T.M[:, S * h + S - C:S * h + S], ["m%d3" % h], [k_("AA")], C, func=AF.Abs, bias=-BIG / 2)
            act(T.AB[:, c], T.AA[:, c], [k_("AA")], [k_("AB")], C, func=AF.Abs, bias=-BIG / 2)
        ts(T.YB[:, c], T.AB[:, c], 128.0 - 15.0 / 32, 191.0, A.add, A.min, [k_("AB")], [k_("YB")], C)
        if rd_ < R - 1:
            ts(P1, T.YB[:, c], 129.0, 128.0, A.max, A.subtract, [k_("YB")], [k_("P")], C / 2)
        else:
            ts(T.Y[:, c], T.YB[:, c], 129.0, 128.0, A.max, A.subtract, [k_("YB")], [k_("Y")], C)
            dma("y", "y%d" % h, T.y[:, c], T.Y[:, c], [k_("Y")], (), 128, 4 * C)

    for rd_ in range(R):
        for h in range(H if rd_ else 0):
            find(h, False, PLAN["keep"][PLAN["mode"][rd_] == "l"])
        for h in range(H):
            lead[0] = PLAN["lead"] * (H - 1 - h)
            judge(rd_, h)

    known = {q: {} for q in Q}
    count, groups, tok = {}, {}, {}
    for i in order(ops):
        o = ops[i]
        q = o["q"]
        need = [tok[d] for d in o["deps"] if not (q == "p" and ops[d]["q"] == "p") and not ops[d].get("chain")]
        for t in sorted(need, key=lambda t: -t["n"]):
            if known[q].get(t["sem"], 0) < t["n"]:
                Q[q].wait_ge(T.sem[t["sem"]], t["n"])
                known[q][t["sem"]] = t["n"]
            for s, n in t["clock"].items():
                known[q][s] = max(known[q].get(s, 0), n)
        if o["kind"] == "op":
            o["fn"]().then_inc(T.sem[q], 1)
            count[q] = count.get(q, 0) + 1
            tok[i] = {"sem": q, "n": count[q], "clock": dict(known[q])}
        elif o["kind"] == "dma":
            Q[q].dma_start(o["out"], o["in_"]).then_inc(T.sem[o["sem"]], 16)
            count[o["sem"]] = count.get(o["sem"], 0) + 16
            t = tok[i] = groups.setdefault(o["sem"], {"sem": o["sem"], "n": 0, "clock": {}})
            t["n"] = count[o["sem"]]
            for s, n in known[q].items():
                t["clock"][s] = max(t["clock"].get(s, 0), n)
        else:
            tr = []
            for c, eng, sem, src, dst in o["tr"]:
                tr.append(RemoteDMATransfer(dst_ids=[dest(topo, c)], dma_engine_mask=sum(1 << k for k in eng),
                                            remote_sem=T.sem[sem], src=src, dst=dst))
                count["ls"] = count.get("ls", 0) + len(eng)
            g.remote_dma_fused(tr, local_sem=T.sem["ls"])
            count[o["sem"]] = o["n"]
            tok[i] = {"sem": o["sem"], "n": o["n"], "clock": {}}
    for s, n in sorted(count.items(), key=lambda a: a[0][0] == "y"):
        g.wait_ge(T.sem[s], n)
